import numpy as np, ml_dtypes
CORES = [3,7,11,15,131,135,139,143]
N = 8
BF = ml_dtypes.bfloat16
P, T, WR, H, VIS, MT, LP = 2048, 1024, 128, 768, 2, 3, 11
lev = np.arange(16)[:, None]
def parts(rng, step=2):
    p = np.arange(P); bit = 1 << np.maximum(LP - 1 - lev, 0); base = rng.integers(1, 3, (1, 8, 16, 1)); s = []
    for n in (P, T):
        flip = rng.random((N, 8, 16, n), dtype=np.float32) < rng.choice(np.array([0.02, 0.1, 0.3]), (N, 8, 1, n))
        s.append(np.where(flip, 3 - base, base))
    b, a = s; tree = 1 + ((p[None, :] & bit) > 0).astype(np.int64)
    start = rng.integers(0, P, (N, len(range(0, 8, step)), T))
    b[:, ::step] = np.where(lev < LP, tree, b[:, ::step])
    a[:, ::step] = np.where(lev < LP, np.moveaxis(tree[:, start], 0, 2), a[:, ::step])
    u = rng.random((N, 8, 16, P)); R = np.where(rng.random((N, 8, 16, P), dtype=np.float32) < 0.5, rng.integers(0, P, (N, 8, 16, P)), (P * u * u * u).astype(np.int64))
    near = ((p[None, :] ^ bit) & -bit) | (R[:, ::step] & (bit - 1))
    R[:, ::step] = np.where(lev < LP, near, R[:, ::step])
    E = rng.integers(0, 16, (N, 8, 16, P)); D = rng.integers(0, 16, (N, 8, 16, T))
    return b, E, R, a, D, rng.integers(0, 256, (N, 8, 16, 1)), rng.integers(60, 111, (N, 8, 16, 1))
def cut(s, n, h):
    return np.where((lev < n) & (lev != h), s, 0)
def cuts(rng, b, a):
    nb = np.maximum(rng.integers(0, 17, (N, 8, 1, P)), rng.integers(0, 17, (N, 8, 1, P))); na = rng.integers(0, 17, (N, 8, 1, T))
    nb[:, 1::2] = 4 * rng.integers(0, 5, (N, 4, 1, P)); na[:, 1::2] = 4 * rng.integers(0, 5, (N, 4, 1, T))
    return cut(b, nb, rng.integers(0, 32, (N, 8, 1, P))), cut(a, na, rng.integers(0, 24, (N, 8, 1, T)))
def pack(b, E, R, a, D, w, t):
    return {"peers": np.ascontiguousarray((b + 4 * E + 64 * R).reshape(N, 128, P)).astype(np.int32), "trav": np.ascontiguousarray((a + 4 * D).reshape(N, 128, T)).astype(np.float32).astype(BF),
            "wts": np.ascontiguousarray(w.reshape(N, 128, 1)).astype(np.int32), "th": np.ascontiguousarray(t.reshape(N, 128, 1)).astype(np.int32)}
def setup_inputs(rng):
    b, E, R, a, D, w, t = parts(rng); b, a = cuts(rng, b, a)
    return pack(b, E, R, a, D, w, t)
def setup_inputs_alone(rng):
    b, E, R, a, D, w, t = parts(rng)
    full = b[:, 1::4, :, 0].copy(); b, a = cuts(rng, b, a); b[:, 1::4, :, 0] = full
    w[:, ::2] = 0; w[:, ::2, 0] = 1; w[:, ::2, 1] = 16; t[:, ::2] = 241
    for q in range(N):
        for g in range(0, 8, 2):
            x = np.concatenate([rng.permutation(256) for i in range(T // 256)])
            D[q, g, 0] = x & 15; D[q, g, 1] = x >> 4; R[q, g] = rng.permutation(P)[None, :]
    three = rng.integers(0, 16, (N, 4, 16, 3)); D[:, 1::2] = np.take_along_axis(three, rng.integers(0, 3, (N, 4, 1, T)), 3)
    w[:, 1::4] = 0; R[:, 3::4] = rng.choice(np.array([0, P - 1, 5, P // 2]), (N, 2, 16, P))
    return pack(b, E, R, a, D, w, t)
def setup_inputs_ties(rng):
    b, E, R, a, D, w, t = parts(rng)
    b = cut(b, rng.integers(0, 3, (N, 8, 1, P)), 99); a = cut(a, rng.integers(0, 3, (N, 8, 1, T)), 99)
    v = rng.integers(1, 15, (8, 16)); o = np.argsort(rng.random((N, 8, 16, T)), axis=2)
    D = np.take_along_axis(v[None, :, :, None], o, 2)
    D = D + (lev == rng.integers(0, 16, (N, 8, 1, T))) * rng.integers(-1, 2, (N, 8, 1, T))
    E[:, ::2] = 0; E[:, 1::2] = 15; s = np.add.reduce(v, axis=1)
    t[:] = np.where(np.arange(8) % 2 == 0, s, 240 - s)[None, :, None, None]
    return pack(b, E, R, a, D, w, t)
def setup_inputs_ends(rng):
    b, E, R, a, D, w, t = parts(rng); b, a = cuts(rng, b, a); o = rng.permutation(8); base = rng.integers(1, 3, (16, 1))
    for i in (0, 1, 4, 5): a[:, o[i]] = base
    for i in (0, 1, 4, 5, 6): b[:, o[i]] = base
    a[:, o[1]] = np.where(lev == 15, rng.integers(0, 3, (N, 1, T)), base); b[:, o[1]] = np.where(lev == 15, rng.integers(0, 3, (N, 1, P)), base)
    a[:, o[2:4]] = 0; b[:, o[2:4]] = 0
    b[:, o[4]] = np.where(lev == 0, 3 - base, base); b[:, o[5]] = np.where(lev == 15, 0, base)
    a[:, o[6]] = np.where(lev == 0, 0, base); b[:, o[6]] = np.where(lev == 0, rng.integers(1, 3, (N, 1, P)), base)
    R[:, o[:4]] = np.where(rng.random((N, 4, 16, P)) < 0.5, R[:, o[:4]], rng.choice(np.array([0, P - 1]), (N, 4, 16, P)))
    x = np.stack([np.concatenate([rng.permutation(256) for i in range(T // 256)]) for q in range(2 * N)]).reshape(2, N, 1, T); z = np.arange(256)[None, :]
    h, k, n = int(o[2]), int(o[3]), int(o[7]); v = rng.integers(0, 16, (16, 1)); sh = np.minimum(lev, 7)
    t[:, h] = 0; w[:, h] = np.where(lev == 0, 1, np.where(lev == 1, 16, 0))
    D[:, h] = np.where(lev == 0, x[0] & 15, np.where(lev == 1, x[0] >> 4, v)); E[:, h, :, :256] = np.where(lev == 0, z & 15, np.where(lev == 1, z >> 4, v))
    t[::2, k] = 241; t[1::2, k] = 240; w[:, k] = np.where(lev < 8, 1 << sh, 0)
    D[:, k] = 15 * np.where(lev < 8, (x[1] >> sh) & 1, 1)
    there = E[:, k]; there[:, :, (15 * z[0]) & (P - 1)] = 15 - 15 * np.where(lev < 8, (z >> sh) & 1, 1)
    w[:, n] = rng.integers(240, 256, (N, 16, 1)); D[:, n] = rng.integers(13, 16, (N, 16, T))
    return pack(b, E, R, a, D, w, t)
def setup_inputs_grid(rng):
    b, E, R, a, D, w, t = parts(rng, 1); p = np.arange(P)[None, :]
    b = cut(b, 16, rng.integers(0, 64, (N, 8, 1, P))); a = cut(a, rng.integers(6, 17, (N, 8, 1, T)), rng.integers(0, 5, (N, 8, 1, T)))
    late = (lev >= 12) & (lev < 15); bit = 1 << np.clip(lev - 12, 0, 2); low = (p & (bit - 1)) | ((p ^ bit) & bit)
    for i in rng.permutation(8)[:2]:
        g = int(i); base = rng.integers(1, 3, (16, 1))
        b[:, g] = np.where(lev == 15, rng.integers(1, 3, (N, 1, P)), np.where(late & ((p & bit) > 0), 3 - base, base))
        hole = (lev == rng.integers(12, 15, (N, 1, T))) | (lev == rng.choice(np.array([12, 13, 14, 99, 99, 99]), (N, 1, T)))
        a[:, g] = np.where(hole, 0, np.where(lev == 15, rng.integers(1, 3, (N, 1, T)), base))
        R[:, g] = np.where(late, (R[:, g] & -8) | low, R[:, g])
    return pack(b, E, R, a, D, w, t)
def setup_inputs_spread(rng):
    b, E, R, a, D, w, t = parts(rng)
    u = rng.random((N, 8, 1, P)); b = np.where(rng.random((N, 8, 16, P)) < u * u, 0, b)
    u = rng.random((N, 8, 1, T)); a = np.where(rng.random((N, 8, 16, T)) < u * u, 0, a)
    u = rng.random((N, 8, 1, P)); E = (16 * rng.random((N, 8, 16, P)) * u * u).astype(np.int64)
    u = rng.random((N, 8, 1, T)); D = (16 * rng.random((N, 8, 16, T)) * u * u).astype(np.int64)
    R = np.minimum(np.exp2(LP * rng.random((N, 8, 16, P))).astype(np.int64), P) - 1; R[:, 1::2] = P - 1 - R[:, 1::2]
    w = np.minimum(np.exp2(8 * rng.random((N, 8, 16, 1))).astype(np.int64), 255) * (rng.random((N, 8, 16, 1)) > 0.125)
    return pack(b, E, R, a, D, w, rng.integers(0, 242, (N, 8, 16, 1)))
def check_inputs(d):
    bad = []
    for k, hi in (("peers", 64 * P - 1), ("wts", 255), ("th", 241)):
        if np.min(d[k]) < 0 or np.max(d[k]) > hi: bad.append("range of " + k)
    if np.any((np.asarray(d["peers"]).astype(np.int64) & 3) == 3): bad.append("symbols of peers")
    t = np.asarray(d["trav"]).astype(np.float64)
    if not np.all((t >= 0) & (t <= 62) & (t == np.floor(t))): bad.append("range of trav")
    if np.any(t - 4 * np.floor(t * 0.25) == 3): bad.append("symbols of trav")
    return bad
def reference(peers, trav, wts, th):
    c = peers.astype(np.int32).reshape(N, 8, 16, P); B = c & 3; E = (c >> 2) & 15; R = c >> 6
    t = trav.astype(np.float32).astype(np.int32).reshape(N, 8, 16, T); a = t & 3; D = t >> 2
    w = wts.astype(np.int32).reshape(N, 8, 16, 1); lim = th.astype(np.int32).reshape(N, 8, 16, 1)
    below = np.arange(WR)[None, :] < np.arange(WR)[:, None]
    for visit in range(VIS):
        if visit: a = np.roll(a, 1, axis=0); D = np.roll(D, 1, axis=0)
        G = np.full(a.shape, -1, np.int32)
        m = (np.add.reduce(w * D, axis=2) & (P - 1)).astype(np.int64)
        for meeting in range(MT):
            ix = m[:, :, None, :]
            b = np.take_along_axis(B, ix, 3); e = np.take_along_axis(E, ix, 3); r = np.take_along_axis(R, ix, 3)
            part = (a != b) | (a == 0) | (b == 0)
            l = np.where(np.any(part, axis=2), np.argmax(part, axis=2), 15)[:, :, None, :]
            at = lev == l
            al = np.take_along_axis(a, l, 2); bl = np.take_along_axis(b, l, 2); rl = np.take_along_axis(r, l, 2); tl = np.take_along_axis(lim, l, 2)
            far = np.add.reduce(np.abs(D - e), axis=2)[:, :, None, :]
            s = m[:, :, :WR]; twin = np.any((s[..., :, None] == s[..., None, :]) & below, axis=3)
            wr = np.zeros((N, 8, T), bool); wr[:, :, :WR] = ~twin; wl = wr[:, :, None, :]
            c1 = wl & (al == 0) & (bl == 0) & (far >= tl); c2 = (al == 0) & (bl != 0)
            c3 = wl & (al != 0) & (bl == 0); c4 = wl & (al != 0) & (bl != 0) & (al != bl)
            swap = c4 & (lev < l) & (G >= 0)
            na = np.where(at & c1, 1, np.where(at & c2, 3 - b, a)).astype(np.int32)
            nb = np.where(at & c1, 2, np.where(at & c3, 3 - a, b)).astype(np.int32)
            nd = np.where(c1, np.maximum(D, e), D); ne = np.where(c1, np.minimum(D, e), e)
            nr = np.where((at & c3 & (G >= 0)) | swap, G, r)
            ng = np.where(at & (c1 | c2), ix, np.where(swap, r, G)).astype(np.int32)
            for q in range(N):
                for g in range(8):
                    j = np.flatnonzero(wr[q, g]); p = m[q, g, j]
                    B[q, g][:, p] = nb[q, g][:, j]; E[q, g][:, p] = ne[q, g][:, j]; R[q, g][:, p] = nr[q, g][:, j]
            a, D, G = na, nd, ng; m = rl[:, :, 0, :].astype(np.int64)
    yp = (B + 4 * E + 64 * R)[..., :H]
    return {"yp": np.ascontiguousarray(yp.reshape(N, 128, H)).astype(np.float32), "yt": np.ascontiguousarray((a + 4 * D).reshape(N, 128, T)).astype(np.float32).astype(BF)}

@@ -1,0 +1,645 @@
+from concourse.mybir import AluOpType, ActivationFunctionType
+
+ALU = AluOpType
+ACT = ActivationFunctionType
+P, NT, WR, HO = 2048, 1024, 128, 768
+TW = P + 2 * WR
+CH = [(128, 576), (576, 1024)]
+LD = [(0, 512), (512, 1024), (1024, 1536), (1536, 1792), (1792, 2048)]
+ZB = NT + WR
+BIGC = 12582912.0
+OPT = dict(eqv=(1, 1), sint=(1, 1, 1, 1, 1, 1), sxq=5, rv=5, dps=0, hs=0, dpv=0, chgv=0, dlv=1, bg=1, one=1,
+           cs=("i2", "i4", "i64r", "n16r", "bo32", "nbo"), tries=30, steps=5000)
+
+BF, F32, F16, I32, U16 = "bfloat16", "float32", "float16", "int32", "uint16"
+WB = ["mis", "s", "tt", "lo", "df", "ad", "c1", "x", "db", "hw", "dw", "chg", "nd", "c4", "sw", "sl", "bg"]
+WF = ["rg", "bn", "xn", "u", "dl", "gv", "xg"]
+WH = ["y", "z"]
+MB = ["i1", "n1", "i2", "n2", "n3", "i4", "n4", "i64", "i64r", "n16r", "bo", "bo32", "bo4", "nbo", "nbo4",
+      "mt", "ml", "mf", "n4t", "tu", "tu3", "g2", "g3", "g4", "wm"]
+SCRATCH = {
+    "xi": ("sbuf", [128, P], I32), "bt": ("sbuf", [128, TW], I32), "rt": ("sbuf", [128, TW], F32),
+    "xq": ("sbuf", [128, TW], F32), "yo": ("sbuf", [128, TW], F32),
+    "tv": ("sbuf", [128, NT], BF), "da": ("sbuf", [128, NT], BF), "dbb": ("sbuf", [128, NT], BF),
+    "sb": ("sbuf", [128, NT + WR], BF), "lb": ("sbuf", [128, NT + WR], BF),
+    "ns": ("sbuf", [128, NT], BF), "nm": ("sbuf", [128, NT], BF), "nt": ("sbuf", [128, NT], BF),
+    "nz": ("sbuf", [128, 7 * ZB], F16), "nq": ("sbuf", [128, NT], BF), "ot": ("sbuf", [128, NT], BF),
+    "ea": ("sbuf", [128, 768], BF), "eq": ("sbuf", [128, 768], BF),
+    "off": ("sbuf", [128, 7 * 72], U16),
+    "ci": ("sbuf", [128, 128], I32), "cj": ("sbuf", [128, 128], I32),
+    "wi": ("sbuf", [128, 256], I32), "wj": ("sbuf", [128, 256], I32),
+    "wt": ("sbuf", [128, 4], I32), "tht": ("sbuf", [128, 4], I32), "pi": ("sbuf", [128, 8], I32),
+    "col": ("sbuf", [128, 24], F32),
+    "c144": ("sbuf", [128, 144], BF), "cg": ("sbuf", [128, 240], BF), "cs": ("sbuf", [128, NT], BF),
+    "sel": ("sbuf", [128, NT], BF), "nsel": ("sbuf", [128, NT], BF), "cmp": ("sbuf", [128, 768], BF),
+    "cv": ("sbuf", [128, 512], BF),
+    "dgb": ("sbuf", [128, 144], BF), "dgw": ("sbuf", [128, 144], BF),
+    "cw": ("sbuf", [128, 240], BF), "cw2": ("sbuf", [128, 240], BF), "n192": ("sbuf", [128, 128], BF),
+    "dum": ("sbuf", [128, 128], F32),
+}
+for _n in WB:
+    SCRATCH["w_" + _n] = ("sbuf", [128, 6 * WR], BF)
+for _n in WF:
+    SCRATCH["w_" + _n] = ("sbuf", [128, 6 * WR], F32)
+for _n in WH:
+    SCRATCH["w_" + _n] = ("sbuf", [128, 6 * WR], F16)
+for _n in MB:
+    SCRATCH["m_" + _n] = ("sbuf", [128, 128], BF)
+for _n in range(8):
+    SCRATCH["ps%d" % _n] = ("psum", [128, 512], F32)
+NDMA = 16
+SEMAPHORES = ["V", "S", "PE", "G", "sent"] + ["d%d" % i for i in range(NDMA)] + ["r%d" % i for i in range(4)]
+
+COSTS = [(1.04, 0.52, 1.56, 3.8, 90.0, 180.0, 50.0), (0.9, 0.45, 1.1, 1.8, 60.0, 150.0, 30.0),
+         (1.2, 0.6, 2.0, 5.5, 180.0, 250.0, 80.0)]
+
+
+def R(name, a, b, step=1):
+    return (name, a, b, step)
+
+
+def build(costs):
+    ops = []
+    CYC, PECYC, GA, SC, _, DMA, RDMA = costs
+
+    def width(r):
+        return len(range(r[1], r[2], r[3]))
+
+    def two(r):
+        return r[0] != "ps" and SCRATCH[r[0]][2] in (BF, F16, U16)
+
+    def add(eng, kind, args, rd, wr, cost, tile=None):
+        ops.append(dict(eng=eng, kind=kind, args=args, rd=[r for r in rd if isinstance(r, tuple) and r[0] != "ps"],
+                        wr=wr, cost=cost, tile=tile))
+        return len(ops) - 1
+
+    def base(r):
+        return [r[1], r[2]] if r[0] == "ind" else [r]
+
+    def vcost(out, ins):
+        if out[0] == "ind":
+            return 50 + width(ins[0]) * SC * CYC
+        n = width(out)
+        if ins[0][0] == "ind":
+            return 50 + n * GA * CYC
+        k = 0.5 if all(two(r) for r in [out] + ins) else 1.0
+        if len(ins) == 2 and all(r[0] != "ps" for r in ins):
+            k *= 2
+        return max(64, n * k) * CYC + 30
+
+    def vop(kind, out, ins, extra, cols=()):
+        rd = [x for r in ins for x in base(r)] + list(cols)
+        wr = [out]
+        if out[0] == "ind":
+            wr = [out[1]]
+            rd = rd + [out[2]]
+        tile = [r[4] for r in ins if r[0] == "ps"]
+        return add("V", kind, (out, ins, extra), rd, wr, vcost(out, ins), tile[0] if tile else None)
+
+    def ts(out, a, s1, op0, s2=None, op1=None):
+        return vop("ts", out, [a], (s1, s2, op0, op1), [s for s in (s1, s2) if isinstance(s, tuple)])
+
+    def tt(out, a, b, op):
+        return vop("tt", out, [a, b], op)
+
+    def cp(out, a):
+        return vop("cp", out, [a], None)
+
+    def ms(out, v):
+        return add("V", "ms", (out, v), [], [out], max(64, width(out) / 2) * CYC + 30)
+
+    def act(out, a, f, bias=0.0, scale=1.0):
+        n = width(out)
+        c = 65 + n * GA * CYC if a[0] == "ind" else 60 + max(64, n) * CYC
+        return add("S", "act", (out, a, f, bias, scale), base(a) + [bias, scale], [out], c, a[4] if a[0] == "ps" else None)
+
+    def lin(out, a, scale, bias=0.0):
+        return act(out, a, ACT.Identity, bias, scale)
+
+    def mm(n, terms):
+        c = 40.0
+        rd = []
+        for t in terms:
+            c += max(64, width(t[1])) * PECYC + 5
+            rd += [t[0], t[1]]
+        i = add("PE", "mm", (n, terms), rd, [], c)
+        return ("ps", 0, n, 1, i)
+
+    def dma(q, out, src, rd, wr, nbytes):
+        return add(q, "dma", (out, src), rd, wr, 2000 + nbytes / DMA)
+
+    def send(k, out, src):
+        i = add("G", "send", (k, out, src), [src], [], width(src) * 256 / RDMA)
+        j = add("X", "recv", (k,), [], [out], 0.0)
+        ops[j]["after"] = i
+
+    def ind(win, offs):
+        return ("ind", win, offs)
+
+    def M(n):
+        return R("m_" + n, 0, 128)
+
+    def W(n, k):
+        return R("w_" + n, k * WR, (k + 1) * WR)
+
+    def col(i):
+        return R("col", i, i + 1)
+
+    def iota(out, pat, b, cm):
+        add("G", "iota", (out, pat, b, cm), [], [out], 130 + 2 * width(out) * CYC)
+
+    def pick(out, a, sign, op, fill):
+        add("G", "pick", (out, a, sign, op, fill), [a], [out], 170 + 2 * width(out) * CYC)
+
+    def wrap(mat, plane, a, b, more=()):
+        return mm((b - a) // 16, [(R(mat, 15 - i, 143 - i), R(plane, a + i, b, 16)) for i in range(16)] + list(more))
+
+    def Z(k, a, b):
+        return R("nz", k * ZB + a, k * ZB + b)
+
+    def OF(k, a, b):
+        return R("off", k * 72 + a // 16, k * 72 + b // 16)
+
+    def offsets(k, a, b):
+        cp(OF(k, a, b), wrap("dgb", "nz", k * ZB + a, k * ZB + b))
+
+    dma("Y", R("tv", 0, NT), ("trav", 0, NT), [], [R("tv", 0, NT)], 128 * NT * 2)
+    dma("S", R("wt", 0, 1), ("wts", 0, 1), [], [R("wt", 0, 4)], 512)
+    dma("S", R("tht", 0, 1), ("th", 0, 1), [], [R("tht", 0, 4)], 512)
+    for a, b in LD:
+        dma("Y", R("xi", a, b), ("peers", a, b), [], [R("xi", a, b)], 512 * b + 128 * NT * 2)
+    PC, GC, LC, C0, WC, B1, BT, BSW, BSL, BSL64, N15, HI, HI2 = range(13)
+    iota(R("pi", 0, 1), [[0, 1]], 0, 1)
+    iota(R("c144", 0, 144), [[1, 144]], 0, 0)
+    iota(R("cg", 0, 240), [[16, 15], [0, 16]], -96, 0)
+    iota(R("dum", 0, 128), [[2, 128]], P, 0)
+    iota(R("cs", 0, NT), [[16, 8], [0, 128]], 0, 0)
+    iota(R("cv", 0, 512), [[0, 8], [-1, 64]], 1, 1)
+    c128 = R("c144", 0, 128)
+    cg = R("cg", 96, 224)
+    cp(col(PC), R("pi", 0, 1))
+    ts(R("pi", 1, 2), R("pi", 0, 1), 112, ALU.bitwise_and)
+    cp(col(GC), R("pi", 1, 2))
+    act(col(LC), col(GC), ACT.Identity, col(PC), -1.0)
+    act(col(BT), col(LC), ACT.Relu, -14.0 * 4096, 4096.0)
+    lin(col(N15), col(BT), -1.0 / 4096, 1.0)
+    act(col(C0), col(LC), ACT.Relu, 1.0, -1.0)
+    lin(col(BSW), col(LC), -0.5, 6.5)
+    lin(col(BSL), col(LC), -1.5, 18.5)
+    lin(col(BSL64), col(LC), -96.0, 1184.0)
+    ts(M("i1"), c128, col(PC), ALU.is_equal)
+    ts(M("bo"), cg, col(GC), ALU.is_equal)
+    for n, v in (("n4", -4.0), ("n1", -1.0), ("n2", -2.0), ("i2", 2.0), ("n3", -3.0), ("i4", 4.0), ("i64", 64.0),
+                 ("i64r", 1.0 / 64), ("n16r", -1.0 / 16)):
+        if n in OPT["cs"]:
+            lin(M(n), M("i1"), v)
+        else:
+            ts(M(n), c128, col(PC), ALU.is_equal, v, ALU.mult)
+    for n, v in (("nbo4", -4.0), ("bo4", 4.0), ("bo32", 32.0), ("nbo", -1.0)):
+        if n in OPT["cs"]:
+            lin(M(n), M("bo"), v)
+        else:
+            ts(M(n), cg, col(GC), ALU.is_equal, v, ALU.mult)
+    lin(R("dum", 0, 128), R("dum", 0, 128), col(C0))
+    pick(M("n4t"), M("nbo4"), 1, ALU.is_gt, 0.0)
+    pick(M("g2"), M("n4t"), 1, ALU.not_equal, 1.0)
+    pick(M("mf"), M("n4t"), 1, ALU.not_equal, 4.0)
+    lin(M("mt"), M("g2"), col(N15))
+    pick(M("g3"), M("n4t"), 1, ALU.not_equal, -1.0)
+    lin(M("ml"), M("g3"), -1.0)
+    pick(M("g4"), M("bo"), -1, ALU.is_gt, 0.0)
+    lin(M("tu"), M("g4"), 0.5)
+    lin(M("tu3"), M("g4"), 1.5)
+    ts(R("dgb", 0, 144), R("c144", 0, 144), col(GC), ALU.subtract, 15.0, ALU.is_equal)
+    ts(R("sel", 0, NT), R("cs", 0, NT), col(GC), ALU.is_equal)
+    ts(R("nsel", 0, NT), R("cs", 0, NT), col(GC), ALU.is_equal, -1.0, ALU.mult)
+    ts(R("cw", 0, 240), R("cg", 0, 240), 16.0, ALU.is_equal, 4096.0, ALU.mult)
+    ts(col(HI), col(PC), 64.0, ALU.is_ge, 16.0, ALU.mult)
+    lin(col(HI2), col(HI), -16384.0)
+    ts(R("cw2", 0, 240), R("cg", 0, 240), col(HI), ALU.is_equal, 4096.0, ALU.mult)
+    act(R("cmp", 0, 512), R("cv", 0, 512), ACT.Relu, -64.0 * 4096, 4096.0)
+    act(R("cmp", 512, 768), R("cv", 0, 256), ACT.Relu, col(HI2), 4096.0)
+    ms(R("n192", 0, 128), -192.0)
+    cp(col(WC), R("wt", 0, 1))
+    lin(R("dgw", 0, 144), R("dgb", 0, 144), col(WC))
+    lin(M("wm"), M("bo"), col(WC))
+    ts(col(B1), R("tht", 0, 1), -1.0 / 64, ALU.mult, -12.0 + 1.0 / 128, ALU.add)
+    if OPT["dps"]:
+        lin(R("da", 0, NT), R("tv", 0, NT), 0.25, 191.75)
+    else:
+        ts(R("da", 0, NT), R("tv", 0, NT), 0.25, ALU.mult, 191.75, ALU.add)
+    send(0, R("dbb", WR, NT), R("da", WR, NT))
+    for a, b in [(0, WR)] + CH:
+        t = mm(b - a, [(M("i1"), R("tv", a, b)), (M("n4"), R("da", a, b))])
+        act(R("nq", a, b), t, ACT.Abs, 1533.5, 2.0)
+        if OPT["hs"]:
+            lin(R("sb", WR + a, WR + b), R("nq", a, b), 1.0, -1.5)
+        else:
+            ts(R("sb", WR + a, WR + b), R("nq", a, b), -1.5, ALU.add)
+    for q, (a, b) in enumerate(LD):
+        ts(R("bt", a, b), R("xi", a, b), 3, ALU.bitwise_and)
+        if q < OPT["sxq"]:
+            lin(R("xq", a, b), R("xi", a, b), 1.0 / 64, -31.0 / 64)
+        else:
+            ts(R("xq", a, b), R("xi", a, b), -31.0, ALU.add, 1.0 / 64, ALU.mult)
+        if q >= len(LD) - OPT["rv"]:
+            ts(R("rt", a, b), R("xq", a, b), BIGC, ALU.add, -BIGC, ALU.add)
+        else:
+            lin(R("rt", a, b), R("xq", a, b), 1.0, BIGC)
+            lin(R("rt", a, b), R("rt", a, b), 1.0, -BIGC)
+    gB, gR, gX = R("bt", 0, P), R("rt", 0, P), R("xq", 0, P)
+
+    for k in range(6):
+        v, t = divmod(k, 3)
+        hb, dn = ("sb", "da") if v == 0 else ("lb", "dbb")
+        last = k == 5
+        ow = OF(k, 0, WR)
+        so = OF(k + 1, NT, ZB)
+        h = R(hb, WR, 2 * WR) if t == 0 else W("hw", k - 1)
+        dp = (R("da", 0, WR) if v == 0 else R("lb", 0, WR)) if t == 0 else W("dw", k - 1)
+        hn = W("hw", k) if k != 2 else R("sb", WR, 2 * WR)
+        dpn = W("dw", k) if k != 2 else R("sb", 0, WR)
+        zw = Z(k, 0, WR)
+        if t == 0:
+            for src, a, b in ([(R("da", 0, NT), 0, NT)] if v == 0 else [(R(dn, WR, NT), WR, NT), (dp, 0, WR)]):
+                n, c0 = (b - a) // 16, v * 64 + a // 16
+                p = wrap("dgw", src[0], src[1], src[2], [(M("wm"), R("n192", 0, n))])
+                cp(R("ci", c0, c0 + n), p)
+                ts(R("cj", c0, c0 + n), R("ci", c0, c0 + n), P - 1, ALU.bitwise_and)
+                cp(OF(k, a, b), R("cj", c0, c0 + n))
+            c0 = v * 128
+            p = mm(WR, [(M("wm"), R("n192", 0, 128)), (M("wm"), dp)])
+            cp(R("wi", c0, c0 + WR), p)
+            ts(R("wj", c0, c0 + WR), R("wi", c0, c0 + WR), P - 1, ALU.bitwise_and)
+            ts(zw, R("wj", c0, c0 + WR), col(C0), ALU.mult)
+        for hf in range(2):
+            if hf == 0:
+                e0, n = 0, 512
+                terms = [(zw, R("nsel", 0, NT, 2))]
+                terms += [(R("sel", q * 128, q * 128 + 128), Z(k, 64, 128), q * 64) for q in range(8)]
+            else:
+                e0, n = 512, 256
+                terms = [(R("sel", q * 256 + 64, q * 256 + 192), Z(k, 0, 64), q * 64) for q in range(4)]
+                terms[1:1] = [(Z(k, 0, 64), R("nsel", q * 128, q * 128 + 64), q // 2 * 64, q % 2 * 64) for q in range(8)]
+            e, cm = R("eq", e0, e0 + n), R("cmp", e0, e0 + n)
+            if OPT["eqv"][hf]:
+                tt(e, mm(n, terms), cm, ALU.is_equal)
+            else:
+                ea = R("ea", e0, e0 + n)
+                act(ea, mm(n, [(M("i1"), cm)] + terms), ACT.Abs)
+                act(e, ea, ACT.Relu, 1.0, -1.0)
+        terms = [(R("cw2", 96 - 32 * q, 224 - 32 * q), R("eq", 512 + q * 64, 576 + q * 64), 0) for q in range(4)]
+        terms += [(R("cw", 112 - 16 * q, 240 - 16 * q), R("eq", q * 64, q * 64 + 64), 64) for q in range(8)]
+        ofw = Z(k + 1, NT, ZB)
+        tt(ofw, mm(WR, [(M("bo"), zw)] + terms), R("dum", 0, 128), ALU.min)
+        if t == 2:
+            offsets(k + 1, NT, ZB)
+        twin = [(M("nbo4"), ofw), (M("bo4"), zw)]
+        s, mis, rg, lo, df, ad, c1, x, db = [W(n, k) for n in ("s", "mis", "rg", "lo", "df", "ad", "c1", "x", "db")]
+        tt(s, ind(gB, ow), h, ALU.subtract)
+        act(rg, ind(gR, ow), ACT.Identity)
+        act(mis, s, ACT.Abs, -2.0)
+        tt(lo, ind(gX, ow), rg, ALU.subtract)
+        if t < 2:
+            act(W("tt", k), mm(WR, [(M("mt"), mis)]), ACT.Relu, col(BT), 4096.0)
+            tt(Z(k + 1, 0, WR), ind(gR, ow), W("tt", k), ALU.min)
+        if t > 0:
+            tt(W("u", k), ind(gR, ow), W("gv", k - 1), ALU.subtract)
+        bb = [W("bg", k)] if OPT["bg"] else [h, s]
+        if OPT["bg"]:
+            act(bb[0], ind(gB, ow), ACT.Identity)
+        p = mm(WR, [(M("n4"), dp)] + [(M("n1"), r) for r in bb] + [(M("i64"), lo)])
+        act(ad, p, ACT.Abs, 799.0 / 256, 1.0 / 256)
+        act(df, p, ACT.Identity, 799.0)
+        act(c1, mm(WR, [(M("mf"), mis)] + twin + [(M("bo"), ad)]), ACT.Sign, col(B1))
+        act(x, mm(WR, [(M("i1"), df), (M("bo32"), c1)]), ACT.Relu, 112.0, 0.25)
+        act(db, mm(WR, [(M("n3"), h), (M("n2"), s), (M("n4t"), mis)]), ACT.Relu, 1.0)
+        tt(hn, mm(WR, [(M("ml"), mis), (M("n3"), h), (M("n1"), c1)]), h, ALU.min)
+        if OPT["dpv"]:
+            tt(dpn, dp, x, ALU.add)
+        else:
+            act(dpn, mm(WR, [(M("i1"), dp), (M("i1"), x)]), ACT.Identity)
+        if k == 2:
+            send(1, R("lb", 0, 2 * WR), R("sb", 0, 2 * WR))
+        if not last:
+            act(W("bn", k), mm(WR, [(M("i1"), r) for r in bb + [db, c1]]), ACT.Identity, 1.0)
+        xg, xn = W("xg", k), W("xn", k)
+        if last:
+            act(xg, ind(gX, ow), ACT.Identity, 32.0, 64.0)
+        else:
+            act(xg, ind(gX, ow), ACT.Identity, 1.0 / 64)
+        xt = [(M("i1" if last else "i64r"), db), (M("i1" if last else "i64r"), c1), (M("n4" if last else "n16r"), x)]
+        if t == 0:
+            act(xn, mm(WR, xt), ACT.Identity)
+        if t < 2:
+            if OPT["chgv"]:
+                tt(W("chg", k), hn, h, ALU.is_lt)
+            else:
+                act(W("chg", k), mm(WR, [(M("i1"), h), (M("n1"), hn)]), ACT.Sign)
+        if t == 0:
+            act(W("gv", k), mm(WR, [(M("bo"), zw)]), ACT.Identity)
+        else:
+            nd, c4, sw, sl, u, dl = [W(n, k) for n in ("nd", "c4", "sw", "sl", "u", "dl")]
+            held = [W("chg", k - i) for i in range(1, t + 1)]
+            act(nd, mm(WR, [(M("i1"), s), (M("i2"), h)]), ACT.Abs, -1.0)
+            act(c4, mm(WR, [(M("i1"), s), (M("n4t"), mis), (M("n4"), nd)] + (twin if t == 1 else [])), ACT.Sign)
+            p = mm(WR, [(M("i4"), c) for c in held] + [(M("n1"), s), (M("tu3"), c4), (M("i1"), db)])
+            if last:
+                act(sl, p, ACT.Relu, col(BSL64), 64.0)
+            else:
+                act(sl, p, ACT.Relu, col(BSL))
+            tt(dl, sl if OPT["dlv"] else mm(WR, [(M("i1"), sl)]), u, ALU.mult)
+            tt(xn, mm(WR, xt), dl, ALU.subtract)
+            if t == 1:
+                z0 = Z(k - 1, 0, WR)
+                act(sw, mm(WR, [(M("i1"), c) for c in held] + [(M("tu"), c4)]), ACT.Relu, col(BSW))
+                tt(W("y", k), sw if OPT["dlv"] else mm(WR, [(M("i1"), sw)]), u, ALU.mult)
+                tt(W("z", k), mm(WR, [(M("bo"), zw), (M("nbo"), z0)]), W("chg", k), ALU.mult)
+                act(W("gv", k), mm(WR, [(M("bo"), z0), (M("i1"), W("y", k)), (M("i1"), W("z", k))]), ACT.Identity)
+        for ci, (a, b) in enumerate(CH):
+            on = OF(k, a, b)
+            hh = R(hb, WR + a, WR + b)
+            sn, mn = R("ns", a, b), R("nm", a, b)
+            if ci < OPT["sint"][k]:
+                act(sn, ind(gB, on), ACT.Identity)
+                act(mn, mm(b - a, [(M("n1"), hh), (M("i1"), sn)]), ACT.Abs, -2.0)
+            else:
+                tt(sn, ind(gB, on), hh, ALU.subtract)
+                act(mn, sn, ACT.Abs, -2.0)
+            if t < 2:
+                act(R("nt", a, b), mm(b - a, [(M("mt"), mn)]), ACT.Relu, col(BT), 4096.0)
+                tt(Z(k + 1, a, b), ind(gR, on), R("nt", a, b), ALU.min)
+                if not OPT["one"]:
+                    offsets(k + 1, 0 if ci == 0 else a, b if ci == 0 else ZB)
+                elif ci == 1:
+                    offsets(k + 1, 0, ZB)
+            tt(hh, mm(b - a, [(M("n2"), hh), (M("ml"), mn)]), hh, ALU.min)
+            if k == 2:
+                send(2 + ci, R("lb", WR + a, WR + b), hh)
+        if last:
+            act(R("yo", 0, HO), R("xq", 0, HO), ACT.Identity, 31.0, 64.0)
+            tt(ind(R("yo", 0, TW), so), xg, xn, ALU.add)
+            dma("Y", ("yp", 0, HO), R("yo", 0, HO), [R("yo", 0, HO)], [], 128 * HO * 4)
+            for a, b in [(0, WR)] + CH:
+                hh = hn if a == 0 else R(hb, WR + a, WR + b)
+                dd = dpn if a == 0 else R(dn, a, b)
+                act(R("nq", a, b), hh, ACT.Abs, 0.5, 2.0)
+                act(R("ot", a, b), mm(b - a, [(M("i4"), dd), (M("n1"), R("nq", a, b))]), ACT.Identity, -765.5)
+                dma("Y", ("yt", a, b), R("ot", a, b), [R("ot", a, b)], [], 128 * (b - a) * 2)
+        else:
+            cp(ind(R("bt", 0, TW), so), W("bn", k))
+            if t > 0:
+                tt(ind(R("rt", 0, TW), so), rg, W("dl", k), ALU.subtract)
+            tt(ind(R("xq", 0, TW), so), xg, xn, ALU.add)
+    return ops
+
+
+def depend(ops):
+    hist = {}
+    deps = [set() for _ in ops]
+    reader = {}
+    for i, op in enumerate(ops):
+        for isw, regs in ((False, op["rd"]), (True, op["wr"])):
+            for r in regs:
+                for (j, w, a, b) in hist.get(r[0], []):
+                    if j != i and (w or isw) and a < r[2] and r[1] < b:
+                        deps[i].add(j)
+        for isw, regs in ((False, op["rd"]), (True, op["wr"])):
+            for r in regs:
+                hl = hist.setdefault(r[0], [])
+                if isw:
+                    hl[:] = [e for e in hl if not (r[1] <= e[2] and e[3] <= r[2])]
+                hl.append((i, isw, r[1], r[2]))
+        if op["tile"] is not None:
+            deps[i].add(op["tile"])
+            if op["tile"] in reader:
+                deps[i].add(reader[op["tile"]][1])
+            reader[op["tile"]] = (reader.get(op["tile"], (i, i))[0], i)
+        if "after" in op:
+            deps[i].add(op["after"])
+    return deps, reader
+
+
+ISSUE = {"dma": 60.0, "send": 300.0, "recv": 0.0}
+QUEUES = ("V", "S", "PE", "G", "Y", "X", "link")
+
+
+def finish(kind, st, cost, free):
+    if kind == "send":
+        free["link"] = max(free["link"], st + 1500.0) + cost
+        return free["link"] + 1000.0
+    return st + cost
+
+
+def replay(ops, cost, lat, order, deps):
+    free = {e: 0.0 for e in QUEUES}
+    fin = [0.0] * len(ops)
+    for i in order:
+        op = ops[i]
+        st = free[op["eng"]]
+        for j in deps[i]:
+            if fin[j] + lat > st:
+                st = fin[j] + lat
+        fin[i] = finish(op["kind"], st, cost[i], free)
+        free[op["eng"]] = st + ISSUE.get(op["kind"], cost[i])
+    return max(fin)
+
+
+def schedule(ops, deps0, reader, succ, weight, win):
+    n = len(ops)
+    LAT = COSTS[0][4]
+    deps = [set(d) for d in deps0]
+    prio = [0.0] * n
+    for i in range(n - 1, -1, -1):
+        prio[i] = weight[i] + max([prio[j] + LAT for j in succ[i]] + [0.0])
+    free = {e: 0.0 for e in QUEUES}
+    fin = [None] * n
+    start = [None] * n
+    banks = {}
+    bank_tile = [None] * 8
+    left = [len(d) for d in deps]
+    ready = [i for i in range(n) if left[i] == 0]
+    rt = [0.0] * n
+    order = []
+    while ready:
+        cand = []
+        opts = []
+        for b in range(8):
+            pt = bank_tile[b]
+            if pt is None:
+                opts.append((0.0, b))
+            elif fin[reader[pt][1]] is not None:
+                opts.append((fin[reader[pt][1]] + LAT, b))
+        best = min(opts) if opts else None
+        for i in ready:
+            op = ops[i]
+            st = max(free[op["eng"]], rt[i])
+            bk = None
+            if op["kind"] == "mm":
+                if best is None or left[reader[i][0]] > 1:
+                    continue
+                bk = best[1]
+                st = max(st, best[0])
+            cand.append((st, i, bk))
+        first = min(cand)
+        eng = ops[first[1]]["eng"]
+        st, i, bk = max([c for c in cand if ops[c[1]]["eng"] == eng and c[0] <= first[0] + win],
+                        key=lambda c: 1e9 - c[1] if eng == "Y" and not deps0[c[1]] else prio[c[1]])
+        op = ops[i]
+        if bk is not None:
+            if bank_tile[bk] is not None:
+                deps[i].add(reader[bank_tile[bk]][1])
+            bank_tile[bk] = i
+            banks[i] = bk
+        start[i] = st
+        fin[i] = finish(op["kind"], st, op["cost"], free)
+        free[op["eng"]] = st + ISSUE.get(op["kind"], op["cost"])
+        order.append(i)
+        ready.remove(i)
+        for j in succ[i]:
+            left[j] -= 1
+            rt[j] = max(rt[j], fin[i] + LAT)
+            if left[j] == 0:
+                ready.append(j)
+    assert len(order) == n
+    return order, deps, start, fin, banks
+
+
+PLAN = {}
+
+
+def plan():
+    if not PLAN:
+        ops = build(COSTS[0])
+        other = [([o["cost"] for o in build(c)], c[4]) for c in COSTS[1:]]
+        deps, reader = depend(ops)
+        succ = [[] for _ in ops]
+        for i, d in enumerate(deps):
+            for j in d:
+                succ[j].append(i)
+        state = [12345]
+
+        def rnd():
+            state[0] = (state[0] * 1103515245 + 12345) % 2147483648
+            return state[0] / 2147483648.0
+
+        best = cur = None
+        for it in range(OPT["tries"] + OPT["steps"]):
+            if it < OPT["tries"]:
+                jit = rnd() * 0.8
+                weight = [o["cost"] * (1 + jit * (rnd() - 0.5)) for o in ops]
+                win = rnd() * 400.0
+            else:
+                weight, win = list(cur[1]), cur[2]
+                for _ in range(1 + int(rnd() * 4)):
+                    weight[int(rnd() * len(ops))] += (rnd() - 0.5) * rnd() * 8000.0
+                if rnd() < 0.05:
+                    win = rnd() * 400.0
+            r = schedule(ops, deps, reader, succ, weight, win)
+            score = [max(r[3])] + [replay(ops, cs, lat, r[0], r[1]) for cs, lat in other]
+            c = (0.5 * score[0] + 0.25 * score[1] + 0.25 * score[2], weight, win, r, score)
+            if best is None or c[0] < best[0]:
+                best = c
+            if it < OPT["tries"]:
+                cur = best
+            elif c[0] <= cur[0] + 150.0 * (1 - (it - OPT["tries"]) / OPT["steps"]):
+                cur = c
+        PLAN["ops"] = ops
+        PLAN["sched"] = best[3]
+        PLAN["score"] = best[4]
+    return PLAN["ops"], PLAN["sched"]
+
+
+def rank_program(g, core, T, topo):
+    rank = T.rank_of(core)
+    if rank is None:
+        return
+    n = len(T.cores)
+    nxt, prv = T.cores[(rank + 1) % n], T.cores[(rank - 1) % n]
+    rid, pid = topo.addr(nxt, core)
+    ops, (order, deps, start, fin, banks) = plan()
+    Q = {"V": g.vector, "S": g.scalar, "PE": g.tensor, "G": g, "Y": g.sync}
+
+    def ap(r):
+        if not isinstance(r, tuple):
+            return r
+        if r[0] == "ind":
+            return ap(r[1]).indirect(ap(r[2]))
+        if r[0] == "ps":
+            return T["ps%d" % banks[r[4]]][:, r[1]:r[2]]
+        if len(r) == 3:
+            return T[r[0]][:] if T[r[0]].shape[1] == r[2] - r[1] else T[r[0]][:, r[1]:r[2]]
+        if r[3] == 1:
+            return T[r[0]][:, r[1]:r[2]]
+        return T[r[0]][:, r[1]:r[2]:r[3]]
+
+    needed = set(j for d in deps for j in d)
+    token = {}
+    count = {"V": 0, "S": 0, "PE": 0, "G": 0}
+    seen = {e: {} for e in Q}
+    nd = [0]
+    sent = [0]
+    final = {}
+    for i in order:
+        op = ops[i]
+        kind, args, e = op["kind"], op["args"], op["eng"]
+        if kind == "recv":
+            token[i] = ("r%d" % args[0], len(topo.engines(prv, core)))
+            final[token[i][0]] = token[i][1]
+            continue
+        q = Q[e]
+        want = {}
+        for j in deps[i]:
+            s, c = token[j]
+            want[s] = max(want.get(s, 0), c)
+        for s in sorted(want):
+            if seen[e].get(s, 0) < want[s]:
+                q.wait_ge(T.sem[s], want[s])
+                seen[e][s] = want[s]
+        if kind == "send":
+            g.remote_dma(ap(args[1]), ap(args[2]), T.sem["r%d" % args[0]], T.sem.sent, pid, rid, topo.mask(core, nxt))
+            sent[0] += len(topo.engines(core, nxt))
+            token[i] = ("sent", sent[0])
+            final["sent"] = sent[0]
+            continue
+        if kind == "dma":
+            s = "d%d" % nd[0]
+            nd[0] += 1
+            q.dma_start(ap(args[0]), ap(args[1])).then_inc(T.sem[s], 16)
+            token[i] = (s, 16)
+            final[s] = 16
+            continue
+        if kind == "ts":
+            s1, s2, op0, op1 = args[2]
+            if op1 is None:
+                ins = q.tensor_scalar(ap(args[0]), ap(args[1][0]), ap(s1), None, op0)
+            else:
+                ins = q.tensor_scalar(ap(args[0]), ap(args[1][0]), ap(s1), ap(s2), op0, op1)
+        elif kind == "tt":
+            ins = q.tensor_tensor(ap(args[0]), ap(args[1][0]), ap(args[1][1]), args[2])
+        elif kind == "cp":
+            ins = q.tensor_copy(ap(args[0]), ap(args[1][0]))
+        elif kind == "ms":
+            ins = q.memset(ap(args[0]), args[1])
+        elif kind == "act":
+            ins = q.activation(ap(args[0]), ap(args[1]), args[2], bias=ap(args[3]), scale=ap(args[4]))
+        elif kind == "iota":
+            ins = g.iota(ap(args[0]), args[1], args[2], args[3],
+                         allow_small_or_imprecise_dtypes=SCRATCH[args[0][0]][2] != I32)
+        elif kind == "pick":
+            ins = g.affine_select(ap(args[0]), ap(args[1]), [[args[2], 128]], args[3], args[4], 0, -args[2])
+        else:
+            bank = T["ps%d" % banks[i]]
+            for ti, t in enumerate(args[1]):
+                c0 = t[2] if len(t) > 2 else 0
+                p0 = t[3] if len(t) > 3 else 0
+                w = len(range(t[1][1], t[1][2], t[1][3]))
+                ins = q.matmul(bank[p0:p0 + t[0][2] - t[0][1], c0:c0 + w], ap(t[0]), ap(t[1]), ti == 0, ti == len(args[1]) - 1)
+        if i in needed:
+            count[e] += 1
+            ins.then_inc(T.sem[e], 1)
+            token[i] = (e, count[e])
+    final.update(count)
+    for s in sorted(final):
+        if final[s] and seen["Y"].get(s, 0) < final[s]:
+            g.sync.wait_ge(T.sem[s], final[s])

@@ -4,37 +4,42 @@ ALU = AluOpType
 ACT = ActivationFunctionType
 P, NT, WR, HO = 2048, 1024, 128, 768
 TW = P + 2 * WR
-CH = [(128, 576), (576, 1024)]
 LD = [(0, 512), (512, 1024), (1024, 1536), (1536, 1792), (1792, 2048)]
 ZB = NT + WR
-BIGC = 12582912.0
-OPT = dict(eqv=(1, 1), sint=(1, 1, 1, 1, 1, 1), sxq=5, rv=5, dps=0, hs=0, dpv=0, chgv=0, dlv=1, bg=1, one=1,
-           cs=("i2", "i4", "i64r", "n16r", "bo32", "nbo"), tries=30, steps=5000)
+BIG = 8388608.0
+C3 = [0, 128, 576, 1024]
+C2 = [0, 512, 1024]
+OPT = dict(cb=[C3] * 6, cm=[C3] * 6, cr=[C3] * 6, cz=[C3] * 6, cx=[C3] * 6, cw=[[0, 1024]] * 6,
+           scan=(1, 1, 1, 1, 1, 1), sig=1, gep=0, gyo=0, split=1, c14=(0,) * 6, bne=1, dfirst=0,
+           tries=40, steps=40000, heat=200.0)
 
 BF, F32, F16, I32, U16 = "bfloat16", "float32", "float16", "int32", "uint16"
-WB = ["mis", "s", "tt", "lo", "df", "ad", "c1", "x", "db", "hw", "dw", "chg", "nd", "c4", "sw", "sl", "bg"]
-WF = ["rg", "bn", "xn", "u", "dl", "gv", "xg"]
-WH = ["y", "z"]
-MB = ["i1", "n1", "i2", "n2", "n3", "i4", "n4", "i64", "i64r", "n16r", "bo", "bo32", "bo4", "nbo", "nbo4",
-      "mt", "ml", "mf", "n4t", "tu", "tu3", "g2", "g3", "g4", "wm"]
+WB = ["un", "ep", "ad", "dw", "bn"]
+WF = ["xn", "rn", "rb"]
+WH = ["dl", "y", "zz", "sc", "sf"]
+MB = ["i1", "n1", "n2", "i2", "i3", "i64", "n64", "bo", "nbo", "bo64", "nbo64", "bos", "bo2", "l2", "mx", "nmx", "m4",
+      "g2", "mz", "bo3", "u3", "wm"]
 SCRATCH = {
-    "xi": ("sbuf", [128, P], I32), "bt": ("sbuf", [128, TW], I32), "rt": ("sbuf", [128, TW], F32),
-    "xq": ("sbuf", [128, TW], F32), "yo": ("sbuf", [128, TW], F32),
+    "xi": ("sbuf", [128, TW], I32), "bt": ("sbuf", [128, TW], I32), "rt": ("sbuf", [128, TW], F32),
+    "yo": ("sbuf", [128, TW], F32),
     "tv": ("sbuf", [128, NT], BF), "da": ("sbuf", [128, NT], BF), "dbb": ("sbuf", [128, NT], BF),
     "sb": ("sbuf", [128, NT + WR], BF), "lb": ("sbuf", [128, NT + WR], BF),
-    "ns": ("sbuf", [128, NT], BF), "nm": ("sbuf", [128, NT], BF), "nt": ("sbuf", [128, NT], BF),
+    "nb": ("sbuf", [128, 2 * NT], BF), "nm": ("sbuf", [128, 2 * NT], BF), "nr": ("sbuf", [128, 2 * NT], F16),
     "nz": ("sbuf", [128, 7 * ZB], F16), "nq": ("sbuf", [128, NT], BF), "ot": ("sbuf", [128, NT], BF),
-    "ea": ("sbuf", [128, 768], BF), "eq": ("sbuf", [128, 768], BF),
-    "off": ("sbuf", [128, 7 * 72], U16),
+    "eq": ("sbuf", [128, 2 * 768], BF), "off": ("sbuf", [128, 7 * 72], U16),
     "ci": ("sbuf", [128, 128], I32), "cj": ("sbuf", [128, 128], I32),
     "wi": ("sbuf", [128, 256], I32), "wj": ("sbuf", [128, 256], I32),
+    "w_e4": ("sbuf", [128, 6 * WR], I32),
+    "w_c": ("sbuf", [128, 12 * WR], BF), "w_s": ("sbuf", [128, 12 * WR], BF),
     "wt": ("sbuf", [128, 4], I32), "tht": ("sbuf", [128, 4], I32), "pi": ("sbuf", [128, 8], I32),
     "col": ("sbuf", [128, 24], F32),
     "c144": ("sbuf", [128, 144], BF), "cg": ("sbuf", [128, 240], BF), "cs": ("sbuf", [128, NT], BF),
-    "sel": ("sbuf", [128, NT], BF), "nsel": ("sbuf", [128, NT], BF), "cmp": ("sbuf", [128, 768], BF),
-    "cv": ("sbuf", [128, 512], BF),
+    "sel": ("sbuf", [128, NT], BF), "nsel": ("sbuf", [128, 512], BF), "cmp": ("sbuf", [128, 768], BF),
+    "cv": ("sbuf", [128, 512], BF), "seg": ("sbuf", [128, 128], BF), "diag": ("sbuf", [128, 128], BF),
+    "j16": ("sbuf", [128, 128], BF),
     "dgb": ("sbuf", [128, 144], BF), "dgw": ("sbuf", [128, 144], BF),
-    "cw": ("sbuf", [128, 240], BF), "cw2": ("sbuf", [128, 240], BF), "n192": ("sbuf", [128, 128], BF),
+    "cw": ("sbuf", [128, 240], BF), "cw2": ("sbuf", [128, 240], BF),
+    "n768": ("sbuf", [128, 128], BF), "two": ("sbuf", [128, 128], BF), "four": ("sbuf", [128, 128], BF),
     "dum": ("sbuf", [128, 128], F32),
 }
 for _n in WB:
@@ -48,10 +53,10 @@ for _n in MB:
 for _n in range(8):
     SCRATCH["ps%d" % _n] = ("psum", [128, 512], F32)
 NDMA = 16
-SEMAPHORES = ["V", "S", "PE", "G", "sent"] + ["d%d" % i for i in range(NDMA)] + ["r%d" % i for i in range(4)]
+SEMAPHORES = ["V", "S", "PE", "G", "sent"] + ["d%d" % i for i in range(NDMA)] + ["r%d" % i for i in range(5)]
 
-COSTS = [(1.04, 0.52, 1.56, 3.8, 90.0, 180.0, 50.0), (0.9, 0.45, 1.1, 1.8, 60.0, 150.0, 30.0),
-         (1.2, 0.6, 2.0, 5.5, 180.0, 250.0, 80.0)]
+COSTS = [(0.9, 0.45, 1.56, 3.8, 80.0, 200.0, 50.0), (0.85, 0.43, 1.1, 1.8, 60.0, 150.0, 30.0),
+         (1.2, 0.6, 2.0, 5.5, 160.0, 250.0, 80.0)]
 
 
 def R(name, a, b, step=1):
@@ -68,13 +73,15 @@ def build(costs):
     def two(r):
         return r[0] != "ps" and SCRATCH[r[0]][2] in (BF, F16, U16)
 
-    def add(eng, kind, args, rd, wr, cost, tile=None):
-        ops.append(dict(eng=eng, kind=kind, args=args, rd=[r for r in rd if isinstance(r, tuple) and r[0] != "ps"],
-                        wr=wr, cost=cost, tile=tile))
-        return len(ops) - 1
-
     def base(r):
         return [r[1], r[2]] if r[0] == "ind" else [r]
+
+    def add(*forms):
+        rd = []
+        for f in forms:
+            rd += [r for r in f[3] if isinstance(r, tuple) and r[0] != "ps" and r not in rd]
+        ops.append(dict(alt=[(f[0], f[1], f[2], f[5]) for f in forms], rd=rd, wr=forms[0][4], tile=forms[0][6]))
+        return len(ops) - 1
 
     def vcost(out, ins):
         if out[0] == "ind":
@@ -94,43 +101,64 @@ def build(costs):
             wr = [out[1]]
             rd = rd + [out[2]]
         tile = [r[4] for r in ins if r[0] == "ps"]
-        return add("V", kind, (out, ins, extra), rd, wr, vcost(out, ins), tile[0] if tile else None)
+        return ("V", kind, (out, ins, extra), rd, wr, vcost(out, ins), tile[0] if tile else None)
 
-    def ts(out, a, s1, op0, s2=None, op1=None):
+    def fts(out, a, s1, op0, s2=None, op1=None):
         return vop("ts", out, [a], (s1, s2, op0, op1), [s for s in (s1, s2) if isinstance(s, tuple)])
 
-    def tt(out, a, b, op):
-        return vop("tt", out, [a, b], op)
-
-    def cp(out, a):
-        return vop("cp", out, [a], None)
-
-    def ms(out, v):
-        return add("V", "ms", (out, v), [], [out], max(64, width(out) / 2) * CYC + 30)
-
-    def act(out, a, f, bias=0.0, scale=1.0):
+    def fact(out, a, f, bias=0.0, scale=1.0):
         n = width(out)
         c = 65 + n * GA * CYC if a[0] == "ind" else 60 + max(64, n) * CYC
-        return add("S", "act", (out, a, f, bias, scale), base(a) + [bias, scale], [out], c, a[4] if a[0] == "ps" else None)
+        return ("S", "act", (out, a, f, bias, scale), base(a) + [bias, scale], [out], c, a[4] if a[0] == "ps" else None)
+
+    def ts(*a):
+        return add(fts(*a))
+
+    def tt(out, a, b, op):
+        return add(vop("tt", out, [a, b], op))
+
+    def cp(out, a):
+        return add(vop("cp", out, [a], None))
+
+    def ms(out, v):
+        return add(("V", "ms", (out, v), [], [out], max(64, width(out) / 2) * CYC + 30, None))
+
+    def act(*a):
+        return add(fact(*a))
 
     def lin(out, a, scale, bias=0.0):
-        return act(out, a, ACT.Identity, bias, scale)
+        return add(fact(out, a, ACT.Identity, bias, scale), fts(out, a, scale, ALU.mult, bias, ALU.add))
 
-    def mm(n, terms):
-        c = 40.0
-        rd = []
-        for t in terms:
-            c += max(64, width(t[1])) * PECYC + 5
-            rd += [t[0], t[1]]
-        i = add("PE", "mm", (n, terms), rd, [], c)
-        return ("ps", 0, n, 1, i)
+    def relu(out, a, bias):
+        return add(fact(out, a, ACT.Relu, bias), fts(out, a, bias, ALU.add, 0.0, ALU.max))
+
+    def step(out, a, level, bias, scale):
+        f = [fts(out, a, level, ALU.is_ge)]
+        if OPT["sig"]:
+            f.insert(0, fact(out, a, ACT.Sigmoid, bias, scale))
+        return add(*f)
+
+    def mm(n, *groups):
+        if not OPT["split"]:
+            groups = [[t for gr in groups for t in gr]]
+        groups = [gr for gr in groups if gr]
+        first = None
+        for q, terms in enumerate(groups):
+            c = 30.0
+            rd = []
+            for t in terms:
+                c += max(64, width(t[1])) * PECYC + 5
+                rd += [t[0], t[1]]
+            i = add(("PE", "mm", (n, terms, first, q == len(groups) - 1), rd, [], c, first))
+            first = i if first is None else first
+        return ("ps", 0, n, 1, first)
 
     def dma(q, out, src, rd, wr, nbytes):
-        return add(q, "dma", (out, src), rd, wr, 2000 + nbytes / DMA)
+        return add((q, "dma", (out, src), rd, wr, 2000 + nbytes / DMA, None))
 
     def send(k, out, src):
-        i = add("G", "send", (k, out, src), [src], [], width(src) * 256 / RDMA)
-        j = add("X", "recv", (k,), [], [out], 0.0)
+        i = add(("G", "send", (k, out, src), [src], [], width(src) * 256 / RDMA, None))
+        j = add(("X", "recv", (k,), [], [out], 0.0, None))
         ops[j]["after"] = i
 
     def ind(win, offs):
@@ -146,10 +174,10 @@ def build(costs):
         return R("col", i, i + 1)
 
     def iota(out, pat, b, cm):
-        add("G", "iota", (out, pat, b, cm), [], [out], 130 + 2 * width(out) * CYC)
+        add(("G", "iota", (out, pat, b, cm), [], [out], 130 + 2 * width(out) * CYC, None))
 
     def pick(out, a, sign, op, fill):
-        add("G", "pick", (out, a, sign, op, fill), [a], [out], 170 + 2 * width(out) * CYC)
+        add(("G", "pick", (out, a, sign, op, fill), [a], [out], 170 + 2 * width(out) * CYC, None))
 
     def wrap(mat, plane, a, b, more=()):
         return mm((b - a) // 16, [(R(mat, 15 - i, 143 - i), R(plane, a + i, b, 16)) for i in range(16)] + list(more))
@@ -163,234 +191,236 @@ def build(costs):
     def offsets(k, a, b):
         cp(OF(k, a, b), wrap("dgb", "nz", k * ZB + a, k * ZB + b))
 
+    def fold(out, plane, tmp):
+        add(("V", "scan", (tmp, [R("seg", 0, 128), plane], (0.0, ALU.mult, ALU.add)), [R("seg", 0, 128), plane], [tmp],
+             64 * CYC + 30, None))
+        cp(out, R(tmp[0], tmp[1] + 15, tmp[2], 16))
+
+    def gcopy(out, a):
+        return ("G", "gcp", (out, a), [a], [out], 170 + 2 * width(out) * CYC, None)
+
+    def parts(c):
+        return list(zip(c[:-1], c[1:]))
+
     dma("Y", R("tv", 0, NT), ("trav", 0, NT), [], [R("tv", 0, NT)], 128 * NT * 2)
     dma("S", R("wt", 0, 1), ("wts", 0, 1), [], [R("wt", 0, 4)], 512)
     dma("S", R("tht", 0, 1), ("th", 0, 1), [], [R("tht", 0, 4)], 512)
     for a, b in LD:
         dma("Y", R("xi", a, b), ("peers", a, b), [], [R("xi", a, b)], 512 * b + 128 * NT * 2)
-    PC, GC, LC, C0, WC, B1, BT, BSW, BSL, BSL64, N15, HI, HI2 = range(13)
+    PC, GC, LC, C0, WC, TH, TB, L15, BZ, N15, HI, HI2 = range(12)
     iota(R("pi", 0, 1), [[0, 1]], 0, 1)
     iota(R("c144", 0, 144), [[1, 144]], 0, 0)
     iota(R("cg", 0, 240), [[16, 15], [0, 16]], -96, 0)
     iota(R("dum", 0, 128), [[2, 128]], P, 0)
     iota(R("cs", 0, NT), [[16, 8], [0, 128]], 0, 0)
-    iota(R("cv", 0, 512), [[0, 8], [-1, 64]], 1, 1)
+    iota(R("j16", 0, 128), [[0, 8], [1, 16]], 0, 0)
     c128 = R("c144", 0, 128)
     cg = R("cg", 96, 224)
     cp(col(PC), R("pi", 0, 1))
     ts(R("pi", 1, 2), R("pi", 0, 1), 112, ALU.bitwise_and)
     cp(col(GC), R("pi", 1, 2))
     act(col(LC), col(GC), ACT.Identity, col(PC), -1.0)
-    act(col(BT), col(LC), ACT.Relu, -14.0 * 4096, 4096.0)
-    lin(col(N15), col(BT), -1.0 / 4096, 1.0)
-    act(col(C0), col(LC), ACT.Relu, 1.0, -1.0)
-    lin(col(BSW), col(LC), -0.5, 6.5)
-    lin(col(BSL), col(LC), -1.5, 18.5)
-    lin(col(BSL64), col(LC), -96.0, 1184.0)
+    act(col(L15), col(LC), ACT.Relu, -14.0, 1.0)
+    lin(col(BZ), col(L15), 4096.0, -4096.0)
+    lin(col(N15), col(L15), -2048.0, 2048.0)
     ts(M("i1"), c128, col(PC), ALU.is_equal)
     ts(M("bo"), cg, col(GC), ALU.is_equal)
-    for n, v in (("n4", -4.0), ("n1", -1.0), ("n2", -2.0), ("i2", 2.0), ("n3", -3.0), ("i4", 4.0), ("i64", 64.0),
-                 ("i64r", 1.0 / 64), ("n16r", -1.0 / 16)):
-        if n in OPT["cs"]:
-            lin(M(n), M("i1"), v)
-        else:
-            ts(M(n), c128, col(PC), ALU.is_equal, v, ALU.mult)
-    for n, v in (("nbo4", -4.0), ("bo4", 4.0), ("bo32", 32.0), ("nbo", -1.0)):
-        if n in OPT["cs"]:
-            lin(M(n), M("bo"), v)
-        else:
-            ts(M(n), cg, col(GC), ALU.is_equal, v, ALU.mult)
-    lin(R("dum", 0, 128), R("dum", 0, 128), col(C0))
-    pick(M("n4t"), M("nbo4"), 1, ALU.is_gt, 0.0)
-    pick(M("g2"), M("n4t"), 1, ALU.not_equal, 1.0)
-    pick(M("mf"), M("n4t"), 1, ALU.not_equal, 4.0)
-    lin(M("mt"), M("g2"), col(N15))
-    pick(M("g3"), M("n4t"), 1, ALU.not_equal, -1.0)
-    lin(M("ml"), M("g3"), -1.0)
-    pick(M("g4"), M("bo"), -1, ALU.is_gt, 0.0)
-    lin(M("tu"), M("g4"), 0.5)
-    lin(M("tu3"), M("g4"), 1.5)
+    for n, v in (("n1", -1.0), ("n2", -2.0), ("i2", 2.0), ("i3", 3.0), ("i64", 64.0), ("n64", -64.0)):
+        lin(M(n), M("i1"), v)
+    for n, v in (("bo2", 2.0), ("nbo", -1.0), ("bo64", 64.0), ("nbo64", -64.0), ("bos", 1.0 / 8192), ("bo3", 3.0)):
+        lin(M(n), M("bo"), v)
+    ts(R("diag", 0, 128), R("j16", 0, 128), col(LC), ALU.is_equal)
+    ts(R("seg", 0, 128), R("j16", 0, 128), 0.5, ALU.is_ge)
+    tt(R("dum", 0, 128), R("dum", 0, 128), R("diag", 0, 128), ALU.mult)
+    pick(M("l2"), M("bo2"), 1, ALU.is_gt, 0.0)
+    pick(M("mx"), M("l2"), 1, ALU.not_equal, -1.0)
+    lin(M("nmx"), M("mx"), -1.0)
+    pick(M("g2"), M("nmx"), 1, ALU.not_equal, 2.0)
+    lin(M("mz"), M("g2"), col(N15))
+    pick(M("m4"), M("nmx"), 1, ALU.not_equal, 3.5)
+    pick(M("u3"), M("bo3"), -1, ALU.is_gt, 0.0)
     ts(R("dgb", 0, 144), R("c144", 0, 144), col(GC), ALU.subtract, 15.0, ALU.is_equal)
     ts(R("sel", 0, NT), R("cs", 0, NT), col(GC), ALU.is_equal)
-    ts(R("nsel", 0, NT), R("cs", 0, NT), col(GC), ALU.is_equal, -1.0, ALU.mult)
+    ts(R("nsel", 0, 512), R("cs", 0, NT, 2), col(GC), ALU.is_equal, -1.0, ALU.mult)
     ts(R("cw", 0, 240), R("cg", 0, 240), 16.0, ALU.is_equal, 4096.0, ALU.mult)
     ts(col(HI), col(PC), 64.0, ALU.is_ge, 16.0, ALU.mult)
-    lin(col(HI2), col(HI), -16384.0)
     ts(R("cw2", 0, 240), R("cg", 0, 240), col(HI), ALU.is_equal, 4096.0, ALU.mult)
-    act(R("cmp", 0, 512), R("cv", 0, 512), ACT.Relu, -64.0 * 4096, 4096.0)
-    act(R("cmp", 512, 768), R("cv", 0, 256), ACT.Relu, col(HI2), 4096.0)
-    ms(R("n192", 0, 128), -192.0)
-    cp(col(WC), R("wt", 0, 1))
+    ms(R("cv", 0, 512), 4096.0)
+    for a, b, p0, p1, c0 in ((0, 512, 0, 128, -64), (512, 768, 0, 128, -64), (512, 768, 0, 64, 0)):
+        add(("G", "tri", (R("cmp", a, b), R("cv", 0, b - a), p0, p1, c0), [R("cv", 0, 512)], [R("cmp", a, b)],
+             170 + 2 * (b - a) * CYC, None))
+    ms(R("n768", 0, 128), -768.0)
+    ms(R("two", 0, 128), 2.0)
+    ms(R("four", 0, 128), 4.0)
+    lin(col(WC), R("wt", 0, 1), 0.25)
     lin(R("dgw", 0, 144), R("dgb", 0, 144), col(WC))
     lin(M("wm"), M("bo"), col(WC))
-    ts(col(B1), R("tht", 0, 1), -1.0 / 64, ALU.mult, -12.0 + 1.0 / 128, ALU.add)
-    if OPT["dps"]:
-        lin(R("da", 0, NT), R("tv", 0, NT), 0.25, 191.75)
-    else:
-        ts(R("da", 0, NT), R("tv", 0, NT), 0.25, ALU.mult, 191.75, ALU.add)
+    lin(col(TH), R("tht", 0, 1), 1.0 / 2048, 4.0 - 1.0 / 4096)
+    lin(col(TB), col(TH), -524288.0)
+    lin(R("da", 0, NT), R("tv", 0, NT), 1.0, 767.0)
     send(0, R("dbb", WR, NT), R("da", WR, NT))
-    for a, b in [(0, WR)] + CH:
-        t = mm(b - a, [(M("i1"), R("tv", a, b)), (M("n4"), R("da", a, b))])
+    for a, b in parts(C3):
+        t = mm(b - a, [(M("i1"), R("tv", a, b)), (M("n1"), R("da", a, b))])
         act(R("nq", a, b), t, ACT.Abs, 1533.5, 2.0)
-        if OPT["hs"]:
-            lin(R("sb", WR + a, WR + b), R("nq", a, b), 1.0, -1.5)
-        else:
-            ts(R("sb", WR + a, WR + b), R("nq", a, b), -1.5, ALU.add)
-    for q, (a, b) in enumerate(LD):
+        lin(R("sb", WR + a, WR + b), R("nq", a, b), 1.0, -1.5 if a else 0.5)
+    for a, b in LD:
         ts(R("bt", a, b), R("xi", a, b), 3, ALU.bitwise_and)
-        if q < OPT["sxq"]:
-            lin(R("xq", a, b), R("xi", a, b), 1.0 / 64, -31.0 / 64)
-        else:
-            ts(R("xq", a, b), R("xi", a, b), -31.0, ALU.add, 1.0 / 64, ALU.mult)
-        if q >= len(LD) - OPT["rv"]:
-            ts(R("rt", a, b), R("xq", a, b), BIGC, ALU.add, -BIGC, ALU.add)
-        else:
-            lin(R("rt", a, b), R("xq", a, b), 1.0, BIGC)
-            lin(R("rt", a, b), R("rt", a, b), 1.0, -BIGC)
-    gB, gR, gX = R("bt", 0, P), R("rt", 0, P), R("xq", 0, P)
+        lin(R("rt", a, b), R("xi", a, b), (1.0 + 2.0 ** -18) / 64, BIG - 0.5)
+    gB, gR, gX = R("bt", 0, P), R("rt", 0, P), R("xi", 0, P)
 
     for k in range(6):
         v, t = divmod(k, 3)
         hb, dn = ("sb", "da") if v == 0 else ("lb", "dbb")
         last = k == 5
+        pl = (k % 2) * NT
+
+        def H(a, b):
+            return R(hb, WR + a, WR + b)
+
+        def B(a, b):
+            return R("nb", pl + a, pl + b)
+
+        def MS(a, b):
+            return R("nm", pl + a, pl + b)
+
+        def RG(a, b):
+            return R("nr", pl + a, pl + b)
+
         ow = OF(k, 0, WR)
         so = OF(k + 1, NT, ZB)
-        h = R(hb, WR, 2 * WR) if t == 0 else W("hw", k - 1)
-        dp = (R("da", 0, WR) if v == 0 else R("lb", 0, WR)) if t == 0 else W("dw", k - 1)
-        hn = W("hw", k) if k != 2 else R("sb", WR, 2 * WR)
-        dpn = W("dw", k) if k != 2 else R("sb", 0, WR)
+        dq = (R("da", 0, WR) if v == 0 else R("lb", 0, WR)) if t == 0 else W("dw", k - 1)
+        dqn = W("dw", k) if k != 2 else R("sb", 0, WR)
         zw = Z(k, 0, WR)
         if t == 0:
-            for src, a, b in ([(R("da", 0, NT), 0, NT)] if v == 0 else [(R(dn, WR, NT), WR, NT), (dp, 0, WR)]):
+            for src, a, b in ([(R("da", 0, NT), 0, NT)] if v == 0 else [(R(dn, WR, NT), WR, NT)]):
                 n, c0 = (b - a) // 16, v * 64 + a // 16
-                p = wrap("dgw", src[0], src[1], src[2], [(M("wm"), R("n192", 0, n))])
+                p = wrap("dgw", src[0], src[1], src[2], [(M("wm"), R("n768", 0, n))])
                 cp(R("ci", c0, c0 + n), p)
                 ts(R("cj", c0, c0 + n), R("ci", c0, c0 + n), P - 1, ALU.bitwise_and)
                 cp(OF(k, a, b), R("cj", c0, c0 + n))
             c0 = v * 128
-            p = mm(WR, [(M("wm"), R("n192", 0, 128)), (M("wm"), dp)])
+            p = mm(WR, [(M("wm"), R("n768", 0, 128)), (M("wm"), dq)])
             cp(R("wi", c0, c0 + WR), p)
             ts(R("wj", c0, c0 + WR), R("wi", c0, c0 + WR), P - 1, ALU.bitwise_and)
-            ts(zw, R("wj", c0, c0 + WR), col(C0), ALU.mult)
+            tt(zw, R("wj", c0, c0 + WR), R("diag", 0, 128), ALU.mult)
+            if v:
+                fold(ow, zw, W("sf", k))
+        eb = (k % 2) * 768
         for hf in range(2):
             if hf == 0:
                 e0, n = 0, 512
-                terms = [(zw, R("nsel", 0, NT, 2))]
+                terms = [(zw, R("nsel", 0, 512))]
                 terms += [(R("sel", q * 128, q * 128 + 128), Z(k, 64, 128), q * 64) for q in range(8)]
             else:
                 e0, n = 512, 256
                 terms = [(R("sel", q * 256 + 64, q * 256 + 192), Z(k, 0, 64), q * 64) for q in range(4)]
-                terms[1:1] = [(Z(k, 0, 64), R("nsel", q * 128, q * 128 + 64), q // 2 * 64, q % 2 * 64) for q in range(8)]
-            e, cm = R("eq", e0, e0 + n), R("cmp", e0, e0 + n)
-            if OPT["eqv"][hf]:
-                tt(e, mm(n, terms), cm, ALU.is_equal)
-            else:
-                ea = R("ea", e0, e0 + n)
-                act(ea, mm(n, [(M("i1"), cm)] + terms), ACT.Abs)
-                act(e, ea, ACT.Relu, 1.0, -1.0)
-        terms = [(R("cw2", 96 - 32 * q, 224 - 32 * q), R("eq", 512 + q * 64, 576 + q * 64), 0) for q in range(4)]
-        terms += [(R("cw", 112 - 16 * q, 240 - 16 * q), R("eq", q * 64, q * 64 + 64), 64) for q in range(8)]
+                terms[1:1] = [(Z(k, 0, 64), R("nsel", q * 64, q * 64 + 64), q // 2 * 64, q % 2 * 64) for q in range(8)]
+            tt(R("eq", eb + e0, eb + e0 + n), mm(n, terms), R("cmp", e0, e0 + n), ALU.is_equal)
+        terms = [(R("cw2", 96 - 32 * q, 224 - 32 * q), R("eq", eb + 512 + q * 64, eb + 576 + q * 64), 0) for q in range(4)]
+        terms += [(R("cw", 112 - 16 * q, 240 - 16 * q), R("eq", eb + q * 64, eb + q * 64 + 64), 64) for q in range(8)]
         ofw = Z(k + 1, NT, ZB)
         tt(ofw, mm(WR, [(M("bo"), zw)] + terms), R("dum", 0, 128), ALU.min)
-        if t == 2:
+        if OPT["scan"][k]:
+            fold(so, ofw, W("sc", k))
+        elif t == 2:
             offsets(k + 1, NT, ZB)
-        twin = [(M("nbo4"), ofw), (M("bo4"), zw)]
-        s, mis, rg, lo, df, ad, c1, x, db = [W(n, k) for n in ("s", "mis", "rg", "lo", "df", "ad", "c1", "x", "db")]
-        tt(s, ind(gB, ow), h, ALU.subtract)
-        act(rg, ind(gR, ow), ACT.Identity)
-        act(mis, s, ACT.Abs, -2.0)
-        tt(lo, ind(gX, ow), rg, ALU.subtract)
+        for a, b in parts(OPT["cb"][k]):
+            lin(B(a, b), ind(gB, OF(k, a, b)), 1.0, -2.0 if a else 0.0)
+        for a, b in parts(OPT["cm"][k]):
+            tt(MS(a, b), B(a, b), H(a, b), ALU.not_equal)
+        rw = RG(0, WR)
         if t < 2:
-            act(W("tt", k), mm(WR, [(M("mt"), mis)]), ACT.Relu, col(BT), 4096.0)
-            tt(Z(k + 1, 0, WR), ind(gR, ow), W("tt", k), ALU.min)
-        if t > 0:
-            tt(W("u", k), ind(gR, ow), W("gv", k - 1), ALU.subtract)
-        bb = [W("bg", k)] if OPT["bg"] else [h, s]
-        if OPT["bg"]:
-            act(bb[0], ind(gB, ow), ACT.Identity)
-        p = mm(WR, [(M("n4"), dp)] + [(M("n1"), r) for r in bb] + [(M("i64"), lo)])
-        act(ad, p, ACT.Abs, 799.0 / 256, 1.0 / 256)
-        act(df, p, ACT.Identity, 799.0)
-        act(c1, mm(WR, [(M("mf"), mis)] + twin + [(M("bo"), ad)]), ACT.Sign, col(B1))
-        act(x, mm(WR, [(M("i1"), df), (M("bo32"), c1)]), ACT.Relu, 112.0, 0.25)
-        act(db, mm(WR, [(M("n3"), h), (M("n2"), s), (M("n4t"), mis)]), ACT.Relu, 1.0)
-        tt(hn, mm(WR, [(M("ml"), mis), (M("n3"), h), (M("n1"), c1)]), h, ALU.min)
-        if OPT["dpv"]:
-            tt(dpn, dp, x, ALU.add)
+            for a, b in parts(OPT["cr"][k]):
+                relu(RG(a, b), ind(gR, OF(k, a, b)), -BIG)
+            for a, b in parts(OPT["cz"][k]):
+                relu(Z(k + 1, a, b), mm(b - a, [(M("i1"), RG(a, b)), (M("mz"), MS(a, b))]), col(BZ))
+            for a, b in parts(OPT["cw"][k]):
+                offsets(k + 1, a, ZB if b == NT and not OPT["scan"][k] else b)
+        elif not last:
+            relu(rw, ind(gR, ow), -BIG)
         else:
-            act(dpn, mm(WR, [(M("i1"), dp), (M("i1"), x)]), ACT.Identity)
-        if k == 2:
-            send(1, R("lb", 0, 2 * WR), R("sb", 0, 2 * WR))
-        if not last:
-            act(W("bn", k), mm(WR, [(M("i1"), r) for r in bb + [db, c1]]), ACT.Identity, 1.0)
-        xg, xn = W("xg", k), W("xn", k)
-        if last:
-            act(xg, ind(gX, ow), ACT.Identity, 32.0, 64.0)
-        else:
-            act(xg, ind(gX, ow), ACT.Identity, 1.0 / 64)
-        xt = [(M("i1" if last else "i64r"), db), (M("i1" if last else "i64r"), c1), (M("n4" if last else "n16r"), x)]
-        if t == 0:
-            act(xn, mm(WR, xt), ACT.Identity)
-        if t < 2:
-            if OPT["chgv"]:
-                tt(W("chg", k), hn, h, ALU.is_lt)
-            else:
-                act(W("chg", k), mm(WR, [(M("i1"), h), (M("n1"), hn)]), ACT.Sign)
-        if t == 0:
-            act(W("gv", k), mm(WR, [(M("bo"), zw)]), ACT.Identity)
-        else:
-            nd, c4, sw, sl, u, dl = [W(n, k) for n in ("nd", "c4", "sw", "sl", "u", "dl")]
-            held = [W("chg", k - i) for i in range(1, t + 1)]
-            act(nd, mm(WR, [(M("i1"), s), (M("i2"), h)]), ACT.Abs, -1.0)
-            act(c4, mm(WR, [(M("i1"), s), (M("n4t"), mis), (M("n4"), nd)] + (twin if t == 1 else [])), ACT.Sign)
-            p = mm(WR, [(M("i4"), c) for c in held] + [(M("n1"), s), (M("tu3"), c4), (M("i1"), db)])
-            if last:
-                act(sl, p, ACT.Relu, col(BSL64), 64.0)
-            else:
-                act(sl, p, ACT.Relu, col(BSL))
-            tt(dl, sl if OPT["dlv"] else mm(WR, [(M("i1"), sl)]), u, ALU.mult)
-            tt(xn, mm(WR, xt), dl, ALU.subtract)
-            if t == 1:
-                z0 = Z(k - 1, 0, WR)
-                act(sw, mm(WR, [(M("i1"), c) for c in held] + [(M("tu"), c4)]), ACT.Relu, col(BSW))
-                tt(W("y", k), sw if OPT["dlv"] else mm(WR, [(M("i1"), sw)]), u, ALU.mult)
-                tt(W("z", k), mm(WR, [(M("bo"), zw), (M("nbo"), z0)]), W("chg", k), ALU.mult)
-                act(W("gv", k), mm(WR, [(M("bo"), z0), (M("i1"), W("y", k)), (M("i1"), W("z", k))]), ACT.Identity)
-        for ci, (a, b) in enumerate(CH):
-            on = OF(k, a, b)
-            hh = R(hb, WR + a, WR + b)
-            sn, mn = R("ns", a, b), R("nm", a, b)
-            if ci < OPT["sint"][k]:
-                act(sn, ind(gB, on), ACT.Identity)
-                act(mn, mm(b - a, [(M("n1"), hh), (M("i1"), sn)]), ACT.Abs, -2.0)
-            else:
-                tt(sn, ind(gB, on), hh, ALU.subtract)
-                act(mn, sn, ACT.Abs, -2.0)
-            if t < 2:
-                act(R("nt", a, b), mm(b - a, [(M("mt"), mn)]), ACT.Relu, col(BT), 4096.0)
-                tt(Z(k + 1, a, b), ind(gR, on), R("nt", a, b), ALU.min)
-                if not OPT["one"]:
-                    offsets(k + 1, 0 if ci == 0 else a, b if ci == 0 else ZB)
-                elif ci == 1:
-                    offsets(k + 1, 0, ZB)
-            tt(hh, mm(b - a, [(M("n2"), hh), (M("ml"), mn)]), hh, ALU.min)
+            lin(W("rb", k), ind(gX, ow), (1.0 + 2.0 ** -18) / 64, BIG - 0.5)
+            relu(rw, W("rb", k), -BIG)
+        A, bw, mis, un, ep, ad, bn = H(0, WR), B(0, WR), MS(0, WR), W("un", k), W("ep", k), W("ad", k), W("bn", k)
+        c1, c4 = R("w_c", 2 * k * WR, (2 * k + 1) * WR), R("w_c", (2 * k + 1) * WR, (2 * k + 2) * WR)
+        ts(W("e4", k), ind(gX, ow), 60, ALU.bitwise_and)
+        lin(ep, W("e4", k), 1.0, 704.0)
+        act(ad, mm(WR, [(M("i1"), ep), (M("n1"), dq)]), ACT.Abs, 64.0)
+        ts(un, A, 2.5, ALU.is_ge)
+        early = [(M("nbo64"), ofw), (M("bo64"), zw), (M("i1"), A)]
+        terms = [(M("n1"), bw), (M("nmx"), mis)]
+        both = t > 0 and OPT["c14"][k]
+        e4 = ([(M("nbo64"), ofw), (M("bo64"), zw)] if t == 1 else []) + [(M("n2"), un)]
+        t4 = [(M("i1"), bw), (M("m4"), mis)]
+        if both:
+            early += [x + (WR,) for x in e4]
+            terms += [x + (WR,) for x in t4]
+        elif t > 0:
+            step(c4, mm(WR, e4, t4), 4.0, -1024.0, 256.0)
+        n = 2 * WR if both else WR
+        step(R("w_c", c1[1], c1[1] + n), mm(n, early, terms, [(M("bos"), ad)]), col(TH), col(TB), 524288.0)
+        tt(dqn, mm(WR, [(M("i1"), ep)], [(M("bo64"), c1)]), dq, ALU.max)
+        if OPT["bne"]:
+            tt(bn, mm(WR, [(M("i1"), R("two", 0, WR)), (M("nmx"), mis), (M("n1"), A)], [(M("i2"), c1)]), bw, ALU.max)
+        for a, b in parts(OPT["cx"][k]):
+            terms = [(M("n1"), B(a, b)), (M("mx"), MS(a, b))]
+            late = []
+            if a == 0:
+                terms.append((M("i1"), R("four", 0, WR)))
+                late = [(M("n2"), c1)]
+            tt(H(a, b), mm(b - a, terms, late), H(a, b), ALU.min)
             if k == 2:
-                send(2 + ci, R("lb", WR + a, WR + b), hh)
+                q = OPT["cx"][k].index(a)
+                if a == 0 and OPT["dfirst"]:
+                    send(4, R("lb", 0, WR), R("sb", 0, WR))
+                c = WR + a if a or OPT["dfirst"] else 0
+                send(1 + q, R("lb", c, WR + b), R("sb", c, WR + b))
+        if not OPT["bne"]:
+            tt(bn, mm(WR, [(M("i1"), R("two", 0, WR)), (M("nmx"), mis)], [(M("n1"), A)]), bw, ALU.max)
+        xe = [(M("i64"), rw), (M("i1"), ep), (M("i1"), dq)]
+        xt = [(M("n1"), dqn), (M("i1"), bn)]
+        if t > 0:
+            sl, sw, dl = R("w_s", 2 * k * WR, (2 * k + 1) * WR), R("w_s", (2 * k + 1) * WR, (2 * k + 2) * WR), W("dl", k)
+            un0, z0 = W("un", k - t), Z(k - t, 0, WR)
+            terms = [(M("nmx"), mis), (M("n1"), un), (M("n1"), bw), (M("i3"), un0)]
+            late = [(M("u3"), c4)]
+            if t == 1:
+                terms.append((M("i3"), un0, WR))
+                late.append((M("u3"), c4, WR))
+            n = 2 * WR if t == 1 else WR
+            step(R("w_s", sl[1], sl[1] + n), mm(n, terms, late), 3.5, -896.0, 256.0)
+            u = mm(WR, [(M("i1"), rw), (M("nbo"), z0)] +
+                   ([] if t == 1 else [(M("n1"), W("y", k - 1)), (M("n1"), W("zz", k - 1))]))
+            tt(dl, u, sl, ALU.mult)
+            if t == 1:
+                tt(W("y", k), u, sw, ALU.mult)
+                tt(W("zz", k), mm(WR, [(M("bo"), zw), (M("nbo"), z0)]), un, ALU.mult)
+            xt.append((M("n64"), dl))
+        xn = W("xn", k)
+        lin(xn, mm(WR, xe, xt), 1.0, -704.0)
         if last:
-            act(R("yo", 0, HO), R("xq", 0, HO), ACT.Identity, 31.0, 64.0)
-            tt(ind(R("yo", 0, TW), so), xg, xn, ALU.add)
+            if OPT["gyo"]:
+                add(gcopy(R("yo", 0, HO), R("xi", 0, HO)))
+            else:
+                lin(R("yo", 0, HO), R("xi", 0, HO), 1.0)
+            cp(ind(R("yo", 0, TW), so), xn)
             dma("Y", ("yp", 0, HO), R("yo", 0, HO), [R("yo", 0, HO)], [], 128 * HO * 4)
-            for a, b in [(0, WR)] + CH:
-                hh = hn if a == 0 else R(hb, WR + a, WR + b)
-                dd = dpn if a == 0 else R(dn, a, b)
-                act(R("nq", a, b), hh, ACT.Abs, 0.5, 2.0)
-                act(R("ot", a, b), mm(b - a, [(M("i4"), dd), (M("n1"), R("nq", a, b))]), ACT.Identity, -765.5)
+            for a, b in parts(OPT["cx"][k]):
+                for c, d in parts([a, WR, b] if a < WR < b else [a, b]):
+                    act(R("nq", c, d), H(c, d), ACT.Abs, 0.5 if c else -3.5, 2.0)
+                terms = [(M("n1"), R("nq", a, b))]
+                if a == 0:
+                    terms.append((M("i1"), dqn))
+                if b > WR:
+                    terms.append((M("i1"), R(dn, max(a, WR), b), max(a, WR) - a))
+                lin(R("ot", a, b), mm(b - a, terms), 1.0, -765.5)
                 dma("Y", ("yt", a, b), R("ot", a, b), [R("ot", a, b)], [], 128 * (b - a) * 2)
         else:
-            cp(ind(R("bt", 0, TW), so), W("bn", k))
-            if t > 0:
-                tt(ind(R("rt", 0, TW), so), rg, W("dl", k), ALU.subtract)
-            tt(ind(R("xq", 0, TW), so), xg, xn, ALU.add)
+            cp(ind(R("bt", 0, TW), so), bn)
+            if k in (1, 2):
+                lin(W("rn", k), mm(WR, [(M("i1"), rw), (M("n1"), W("dl", k))]), 1.0, BIG)
+                cp(ind(R("rt", 0, TW), so), W("rn", k))
+            cp(ind(R("xi", 0, TW), so), xn)
     return ops
 
 
@@ -411,10 +441,9 @@ def depend(ops):
                     hl[:] = [e for e in hl if not (r[1] <= e[2] and e[3] <= r[2])]
                 hl.append((i, isw, r[1], r[2]))
         if op["tile"] is not None:
-            deps[i].add(op["tile"])
-            if op["tile"] in reader:
-                deps[i].add(reader[op["tile"]][1])
-            reader[op["tile"]] = (reader.get(op["tile"], (i, i))[0], i)
+            deps[i].add(reader[op["tile"]][1] if op["tile"] in reader else op["tile"])
+            first = reader.get(op["tile"], (None, i))[0]
+            reader[op["tile"]] = (i if first is None and op["alt"][0][1] != "mm" else first, i)
         if "after" in op:
             deps[i].add(op["after"])
     return deps, reader
@@ -431,31 +460,60 @@ def finish(kind, st, cost, free):
     return st + cost
 
 
-def replay(ops, cost, lat, order, deps):
+def replay(eng, kind, cost, lat, order, deps, opens=None, last=None):
     free = {e: 0.0 for e in QUEUES}
-    fin = [0.0] * len(ops)
+    prev = {e: -1 for e in QUEUES}
+    fin = [0.0] * len(eng)
+    pred = [-1] * len(eng)
+    idle = [(0.0, b, -1) for b in range(8)]
+    wait, banks = {}, {}
     for i in order:
-        op = ops[i]
-        st = free[op["eng"]]
+        e = eng[i]
+        st = free[e]
+        p = prev[e]
         for j in deps[i]:
-            if fin[j] + lat > st:
-                st = fin[j] + lat
-        fin[i] = finish(op["kind"], st, cost[i], free)
-        free[op["eng"]] = st + ISSUE.get(op["kind"], cost[i])
-    return max(fin)
+            x = fin[j] + lat
+            if x > st:
+                st = x
+                p = j
+        if opens:
+            if opens[i]:
+                if not idle:
+                    return None
+                o = min(idle)
+                idle.remove(o)
+                banks[i] = o[1]
+                if o[2] >= 0:
+                    wait[i] = o[2]
+                    if o[0] > st:
+                        st = o[0]
+                        p = o[2]
+        k = kind[i]
+        if k in ISSUE:
+            fin[i] = finish(k, st, cost[i], free)
+            free[e] = st + ISSUE[k]
+        else:
+            fin[i] = free[e] = st + cost[i]
+        if opens and i in last:
+            idle.append((fin[i] + lat, banks[last[i]], i))
+        prev[e] = i
+        pred[i] = p
+    return max(fin), fin, wait, banks, pred
 
 
-def schedule(ops, deps0, reader, succ, weight, win):
-    n = len(ops)
+def schedule(eng, kind, opens, cost, deps0, reader, succ, weight, win):
+    n = len(eng)
     LAT = COSTS[0][4]
-    deps = [set(d) for d in deps0]
+    deps = list(deps0)
     prio = [0.0] * n
     for i in range(n - 1, -1, -1):
-        prio[i] = weight[i] + max([prio[j] + LAT for j in succ[i]] + [0.0])
+        m = 0.0
+        for j in succ[i]:
+            if prio[j] + LAT > m:
+                m = prio[j] + LAT
+        prio[i] = weight[i] + m
     free = {e: 0.0 for e in QUEUES}
     fin = [None] * n
-    start = [None] * n
-    banks = {}
     bank_tile = [None] * 8
     left = [len(d) for d in deps]
     ready = [i for i in range(n) if left[i] == 0]
@@ -463,37 +521,32 @@ def schedule(ops, deps0, reader, succ, weight, win):
     order = []
     while ready:
         cand = []
-        opts = []
+        best = None
         for b in range(8):
             pt = bank_tile[b]
             if pt is None:
-                opts.append((0.0, b))
+                o = (0.0, b)
             elif fin[reader[pt][1]] is not None:
-                opts.append((fin[reader[pt][1]] + LAT, b))
-        best = min(opts) if opts else None
+                o = (fin[reader[pt][1]] + LAT, b)
+            else:
+                continue
+            if best is None or o < best:
+                best = o
         for i in ready:
-            op = ops[i]
-            st = max(free[op["eng"]], rt[i])
-            bk = None
-            if op["kind"] == "mm":
-                if best is None or left[reader[i][0]] > 1:
+            st = max(free[eng[i]], rt[i])
+            if opens[i]:
+                if best is None or left[reader[i][0]] > 1 or any(left[j] > 1 for j in succ[i] if kind[j] == "mm"):
                     continue
-                bk = best[1]
                 st = max(st, best[0])
-            cand.append((st, i, bk))
+            cand.append((st, i))
         first = min(cand)
-        eng = ops[first[1]]["eng"]
-        st, i, bk = max([c for c in cand if ops[c[1]]["eng"] == eng and c[0] <= first[0] + win],
-                        key=lambda c: 1e9 - c[1] if eng == "Y" and not deps0[c[1]] else prio[c[1]])
-        op = ops[i]
-        if bk is not None:
-            if bank_tile[bk] is not None:
-                deps[i].add(reader[bank_tile[bk]][1])
-            bank_tile[bk] = i
-            banks[i] = bk
-        start[i] = st
-        fin[i] = finish(op["kind"], st, op["cost"], free)
-        free[op["eng"]] = st + ISSUE.get(op["kind"], op["cost"])
+        e = eng[first[1]]
+        st, i = max([c for c in cand if eng[c[1]] == e and c[0] <= first[0] + win],
+                    key=lambda c: 1e9 - c[1] if e == "Y" and not deps0[c[1]] else prio[c[1]])
+        if opens[i]:
+            bank_tile[best[1]] = i
+        fin[i] = finish(kind[i], st, cost[i], free)
+        free[e] = st + ISSUE.get(kind[i], cost[i])
         order.append(i)
         ready.remove(i)
         for j in succ[i]:
@@ -502,16 +555,17 @@ def schedule(ops, deps0, reader, succ, weight, win):
             if left[j] == 0:
                 ready.append(j)
     assert len(order) == n
-    return order, deps, start, fin, banks
+    return order, max(fin)
 
 
 PLAN = {}
+SHARE = (0.5, 0.25, 0.25)
 
 
 def plan():
     if not PLAN:
-        ops = build(COSTS[0])
-        other = [([o["cost"] for o in build(c)], c[4]) for c in COSTS[1:]]
+        sets = [build(c) for c in COSTS]
+        ops = sets[0]
         deps, reader = depend(ops)
         succ = [[] for _ in ops]
         for i, d in enumerate(deps):
@@ -523,31 +577,90 @@ def plan():
             state[0] = (state[0] * 1103515245 + 12345) % 2147483648
             return state[0] / 2147483648.0
 
-        best = cur = None
-        for it in range(OPT["tries"] + OPT["steps"]):
-            if it < OPT["tries"]:
-                jit = rnd() * 0.8
-                weight = [o["cost"] * (1 + jit * (rnd() - 0.5)) for o in ops]
-                win = rnd() * 400.0
+        n = len(ops)
+        form = [0] * n
+        eng = [o["alt"][0][0] for o in ops]
+        kind = [o["alt"][0][1] for o in ops]
+        cost = [[o["alt"][0][3] for o in s] for s in sets]
+        opens = [kind[i] == "mm" and ops[i]["tile"] is None for i in range(n)]
+        best = None
+        for it in range(OPT["tries"]):
+            jit = rnd() * 0.8
+            r = schedule(eng, kind, opens, cost[0], deps, reader, succ, [c * (1 + jit * (rnd() - 0.5)) for c in cost[0]],
+                         rnd() * 400.0)
+            if best is None or r[1] < best[1]:
+                best = r
+        order = best[0]
+        dl = [sorted(d) for d in deps]
+        hard = [[j for j in dl[i] if not (kind[i] == kind[j] == "mm")] for i in range(n)]
+        last = {reader[i][1]: i for i in reader}
+
+        def judge(seq):
+            r = replay(eng, kind, cost[0], COSTS[0][4], seq, hard, opens, last)
+            if r is None:
+                return None
+            dd = [hard[i] + [r[2][i]] if i in r[2] else hard[i] for i in range(n)]
+            score = [r[0]] + [replay(eng, kind, cost[q], COSTS[q][4], seq, dd)[0] for q in range(1, len(COSTS))]
+            return (sum(w * s for w, s in zip(SHARE, score)) + 0.02 * sum(r[1]) / n, score, r, dd)
+
+        def move(seq, i, j):
+            a, b = seq.index(j), seq.index(i)
+            take = {i}
+            for x in range(b, a - 1, -1):
+                if seq[x] in take:
+                    take.update(dl[seq[x]])
+            if j in take:
+                return None
+            mid = seq[a:b + 1]
+            return seq[:a] + [x for x in mid if x in take] + [x for x in mid if x not in take] + seq[b + 1:]
+
+        def setform(i, f):
+            form[i] = f
+            eng[i], kind[i] = ops[i]["alt"][f][0], ops[i]["alt"][f][1]
+            for q in range(len(COSTS)):
+                cost[q][i] = sets[q][i]["alt"][f][3]
+
+        cur = judge(order)
+        best = (cur, order, list(form))
+        path = None
+        for it in range(OPT["steps"]):
+            if path is None:
+                path = []
+                i = max(range(n), key=lambda x: cur[2][1][x])
+                while i >= 0:
+                    path.append(i)
+                    i = cur[2][4][i]
+            i = path[int(rnd() * len(path))] if rnd() < 0.6 else int(rnd() * n)
+            old = form[i]
+            seq = order
+            if len(ops[i]["alt"]) > 1 and rnd() < 0.25:
+                setform(i, (old + 1) % len(ops[i]["alt"]))
+            elif eng[i] == "X" or (eng[i] == "Y" and not dl[i]):
+                continue
             else:
-                weight, win = list(cur[1]), cur[2]
-                for _ in range(1 + int(rnd() * 4)):
-                    weight[int(rnd() * len(ops))] += (rnd() - 0.5) * rnd() * 8000.0
-                if rnd() < 0.05:
-                    win = rnd() * 400.0
-            r = schedule(ops, deps, reader, succ, weight, win)
-            score = [max(r[3])] + [replay(ops, cs, lat, r[0], r[1]) for cs, lat in other]
-            c = (0.5 * score[0] + 0.25 * score[1] + 0.25 * score[2], weight, win, r, score)
-            if best is None or c[0] < best[0]:
-                best = c
-            if it < OPT["tries"]:
-                cur = best
-            elif c[0] <= cur[0] + 150.0 * (1 - (it - OPT["tries"]) / OPT["steps"]):
-                cur = c
+                line = [x for x in order if eng[x] == eng[i]]
+                p = line.index(i)
+                d = 1 + int(rnd() * rnd() * 6)
+                if rnd() < 0.5:
+                    seq = move(order, i, line[p - d]) if p >= d else None
+                else:
+                    seq = move(order, line[p + d], i) if p + d < len(line) else None
+                if seq is None or (eng[i] == "Y" and not dl[line[max(p - d, 0)]]):
+                    continue
+            c = judge(seq)
+            if c is not None and c[0] <= cur[0] + OPT["heat"] * (1 - it / OPT["steps"]) * rnd():
+                cur, order, path = c, seq, None
+                if c[0] < best[0][0]:
+                    best = (c, seq, list(form))
+            elif form[i] != old:
+                setform(i, old)
+        c, order, form = best
         PLAN["ops"] = ops
-        PLAN["sched"] = best[3]
-        PLAN["score"] = best[4]
-    return PLAN["ops"], PLAN["sched"]
+        PLAN["sched"] = (order, c[3], [f - sets[0][i]["alt"][form[i]][3] for i, f in enumerate(c[2][1])], c[2][1], c[2][3])
+        PLAN["score"] = c[1]
+        PLAN["form"] = form
+        PLAN["pred"] = c[2][4]
+    return PLAN["ops"], PLAN["sched"], PLAN["form"]
 
 
 def rank_program(g, core, T, topo):
@@ -557,7 +670,7 @@ def rank_program(g, core, T, topo):
     n = len(T.cores)
     nxt, prv = T.cores[(rank + 1) % n], T.cores[(rank - 1) % n]
     rid, pid = topo.addr(nxt, core)
-    ops, (order, deps, start, fin, banks) = plan()
+    ops, (order, deps, start, fin, banks), form = plan()
     Q = {"V": g.vector, "S": g.scalar, "PE": g.tensor, "G": g, "Y": g.sync}
 
     def ap(r):
@@ -581,8 +694,7 @@ def rank_program(g, core, T, topo):
     sent = [0]
     final = {}
     for i in order:
-        op = ops[i]
-        kind, args, e = op["kind"], op["args"], op["eng"]
+        e, kind, args, _ = ops[i]["alt"][form[i]]
         if kind == "recv":
             token[i] = ("r%d" % args[0], len(topo.engines(prv, core)))
             final[token[i][0]] = token[i][1]
@@ -626,15 +738,24 @@ def rank_program(g, core, T, topo):
         elif kind == "iota":
             ins = g.iota(ap(args[0]), args[1], args[2], args[3],
                          allow_small_or_imprecise_dtypes=SCRATCH[args[0][0]][2] != I32)
+        elif kind == "scan":
+            ins = q.tensor_tensor_scan(ap(args[0]), ap(args[1][0]), ap(args[1][1]), *args[2])
+        elif kind == "tri":
+            w = args[0][2] - args[0][1]
+            ins = g.affine_select(T[args[0][0]][args[2]:args[3], args[0][1]:args[0][2]], T[args[1][0]][args[2]:args[3], 0:w],
+                                  [[0, w // 64], [-1, 64]], ALU.is_ge, 0.0, args[4], 1)
+        elif kind == "gcp":
+            ins = g.affine_select(ap(args[0]), ap(args[1]), [[0, args[0][2] - args[0][1]]], ALU.is_ge, 0.0, 0, 0)
         elif kind == "pick":
             ins = g.affine_select(ap(args[0]), ap(args[1]), [[args[2], 128]], args[3], args[4], 0, -args[2])
         else:
-            bank = T["ps%d" % banks[i]]
+            bank = T["ps%d" % banks[i if args[2] is None else args[2]]]
             for ti, t in enumerate(args[1]):
                 c0 = t[2] if len(t) > 2 else 0
                 p0 = t[3] if len(t) > 3 else 0
                 w = len(range(t[1][1], t[1][2], t[1][3]))
-                ins = q.matmul(bank[p0:p0 + t[0][2] - t[0][1], c0:c0 + w], ap(t[0]), ap(t[1]), ti == 0, ti == len(args[1]) - 1)
+                ins = q.matmul(bank[p0:p0 + t[0][2] - t[0][1], c0:c0 + w], ap(t[0]), ap(t[1]),
+                               ti == 0 and args[2] is None, args[3] and ti == len(args[1]) - 1)
         if i in needed:
             count[e] += 1
             ins.then_inc(T.sem[e], 1)

@@ -9,15 +9,15 @@ ZB = NT + WR
 BIG = 8388608.0
 C3 = [0, 128, 576, 1024]
 C2 = [0, 512, 1024]
-OPT = dict(cb=[C3] * 6, cm=[C3] * 6, cr=[C3] * 6, cz=[C3] * 6, cx=[C3] * 6, cw=[[0, 1024]] * 6,
-           scan=(1, 1, 1, 1, 1, 1), sig=1, gep=0, gyo=0, split=1, c14=(0,) * 6, bne=1, dfirst=0,
-           tries=40, steps=40000, heat=200.0)
+OPT = dict(cb=[C3] * 6, cm=[C3] * 6, cr=[C3] * 6, cz=[C3] * 6, cx=[C3] * 6, cw=[[0, 128, 1024]] * 6,
+           zm=(1,) * 6, zv=[(0, 1, 1)] * 6, rv=(0, 0, 0, 1, 1), gcp=1, split=1, bne=1, dfirst=1, late="ad",
+           tries=40, steps=100000, heat=300.0, crit=0.7, flip=0.05, mean=0.5, load=0.2, part=0.7)
 
 BF, F32, F16, I32, U16 = "bfloat16", "float32", "float16", "int32", "uint16"
-WB = ["un", "ep", "ad", "dw", "bn"]
-WF = ["xn", "rn", "rb"]
-WH = ["dl", "y", "zz", "sc", "sf"]
-MB = ["i1", "n1", "n2", "i2", "i3", "i64", "n64", "bo", "nbo", "bo64", "nbo64", "bos", "bo2", "l2", "mx", "nmx", "m4",
+WB = ["un", "ep", "ad", "dw", "bn", "bg", "tw"]
+WF = ["xn", "rb"]
+WH = ["rn", "dl", "y", "zz", "sc", "sf", "ofw", "zm"]
+MB = ["i1", "n1", "n2", "i2", "i3", "i64", "n64", "bo", "nbo", "bo64", "bos", "bo2", "l2", "l8", "mx5", "mx", "nmx", "m4",
       "g2", "mz", "bo3", "u3", "wm"]
 SCRATCH = {
     "xi": ("sbuf", [128, TW], I32), "bt": ("sbuf", [128, TW], I32), "rt": ("sbuf", [128, TW], F32),
@@ -33,13 +33,12 @@ SCRATCH = {
     "w_c": ("sbuf", [128, 12 * WR], BF), "w_s": ("sbuf", [128, 12 * WR], BF),
     "wt": ("sbuf", [128, 4], I32), "tht": ("sbuf", [128, 4], I32), "pi": ("sbuf", [128, 8], I32),
     "col": ("sbuf", [128, 24], F32),
-    "c144": ("sbuf", [128, 144], BF), "cg": ("sbuf", [128, 240], BF), "cs": ("sbuf", [128, NT], BF),
+    "c144": ("sbuf", [128, 144], BF), "cg": ("sbuf", [128, 240], BF), "cs": ("sbuf", [128, 512], BF),
     "sel": ("sbuf", [128, NT], BF), "nsel": ("sbuf", [128, 512], BF), "cmp": ("sbuf", [128, 768], BF),
     "cv": ("sbuf", [128, 512], BF), "seg": ("sbuf", [128, 128], BF), "diag": ("sbuf", [128, 128], BF),
     "j16": ("sbuf", [128, 128], BF),
     "dgb": ("sbuf", [128, 144], BF), "dgw": ("sbuf", [128, 144], BF),
-    "cw": ("sbuf", [128, 240], BF), "cw2": ("sbuf", [128, 240], BF),
-    "n768": ("sbuf", [128, 128], BF), "two": ("sbuf", [128, 128], BF), "four": ("sbuf", [128, 128], BF),
+    "k2": ("sbuf", [128, 32], BF), "npair": ("sbuf", [128, 256], BF), "n768": ("sbuf", [128, 128], BF),
     "dum": ("sbuf", [128, 128], F32),
 }
 for _n in WB:
@@ -55,8 +54,8 @@ for _n in range(8):
 NDMA = 16
 SEMAPHORES = ["V", "S", "PE", "G", "sent"] + ["d%d" % i for i in range(NDMA)] + ["r%d" % i for i in range(5)]
 
-COSTS = [(0.9, 0.45, 1.56, 3.8, 80.0, 200.0, 50.0), (0.85, 0.43, 1.1, 1.8, 60.0, 150.0, 30.0),
-         (1.2, 0.6, 2.0, 5.5, 160.0, 250.0, 80.0)]
+COSTS = [(0.9, 0.45, 1.56, 3.8, 90.0, 250.0, 80.0, 1600.0), (0.85, 0.43, 1.1, 1.8, 60.0, 160.0, 40.0, 2200.0),
+         (1.2, 0.6, 2.0, 5.5, 160.0, 350.0, 120.0, 1200.0)]
 
 
 def R(name, a, b, step=1):
@@ -65,7 +64,7 @@ def R(name, a, b, step=1):
 
 def build(costs):
     ops = []
-    CYC, PECYC, GA, SC, _, DMA, RDMA = costs
+    CYC, PECYC, GA, SC, _, DMA, RDMA, FIX = costs
 
     def width(r):
         return len(range(r[1], r[2], r[3]))
@@ -132,11 +131,10 @@ def build(costs):
     def relu(out, a, bias):
         return add(fact(out, a, ACT.Relu, bias), fts(out, a, bias, ALU.add, 0.0, ALU.max))
 
-    def step(out, a, level, bias, scale):
-        f = [fts(out, a, level, ALU.is_ge)]
-        if OPT["sig"]:
-            f.insert(0, fact(out, a, ACT.Sigmoid, bias, scale))
-        return add(*f)
+    def step(out, a, level, bias, scale, vector=False):
+        f = [fact(out, a, ACT.Sigmoid, bias, scale), fts(out, a, level, ALU.is_ge)]
+        f[0][3].append(R("seg", 0, 128))
+        return add(*(f[::-1] if vector else f))
 
     def mm(n, *groups):
         if not OPT["split"]:
@@ -154,7 +152,7 @@ def build(costs):
         return ("ps", 0, n, 1, first)
 
     def dma(q, out, src, rd, wr, nbytes):
-        return add((q, "dma", (out, src), rd, wr, 2000 + nbytes / DMA, None))
+        return add((q, "dma", (out, src), rd, wr, FIX + nbytes / DMA, None))
 
     def send(k, out, src):
         i = add(("G", "send", (k, out, src), [src], [], width(src) * 256 / RDMA, None))
@@ -196,8 +194,11 @@ def build(costs):
              64 * CYC + 30, None))
         cp(out, R(tmp[0], tmp[1] + 15, tmp[2], 16))
 
-    def gcopy(out, a):
-        return ("G", "gcp", (out, a), [a], [out], 170 + 2 * width(out) * CYC, None)
+    def copy(out, a):
+        f = [fact(out, a, ACT.Identity), vop("cp", out, [a], None)]
+        if OPT["gcp"]:
+            f.insert(0, ("G", "gcp", (out, a), [a], [out], 170 + 2 * width(out) * CYC, None))
+        return add(*f)
 
     def parts(c):
         return list(zip(c[:-1], c[1:]))
@@ -207,15 +208,15 @@ def build(costs):
     dma("S", R("tht", 0, 1), ("th", 0, 1), [], [R("tht", 0, 4)], 512)
     for a, b in LD:
         dma("Y", R("xi", a, b), ("peers", a, b), [], [R("xi", a, b)], 512 * b + 128 * NT * 2)
-    PC, GC, LC, C0, WC, TH, TB, L15, BZ, N15, HI, HI2 = range(12)
+    PC, GC, LC, PR, WC, TH, TB, L15, BZ, N15, HI, BT, EV = range(13)
     iota(R("pi", 0, 1), [[0, 1]], 0, 1)
     iota(R("c144", 0, 144), [[1, 144]], 0, 0)
-    iota(R("cg", 0, 240), [[16, 15], [0, 16]], -96, 0)
-    iota(R("dum", 0, 128), [[2, 128]], P, 0)
-    iota(R("cs", 0, NT), [[16, 8], [0, 128]], 0, 0)
+    iota(R("cg", 0, 128), [[16, 8], [0, 16]], 0, 0)
+    iota(R("dum", 0, 128), [[0, 128]], P, 2)
+    iota(R("cs", 0, 512), [[16, 8], [0, 64]], 0, 0)
     iota(R("j16", 0, 128), [[0, 8], [1, 16]], 0, 0)
     c128 = R("c144", 0, 128)
-    cg = R("cg", 96, 224)
+    cg = R("cg", 0, 128)
     cp(col(PC), R("pi", 0, 1))
     ts(R("pi", 1, 2), R("pi", 0, 1), 112, ALU.bitwise_and)
     cp(col(GC), R("pi", 1, 2))
@@ -225,12 +226,13 @@ def build(costs):
     lin(col(N15), col(L15), -2048.0, 2048.0)
     ts(M("i1"), c128, col(PC), ALU.is_equal)
     ts(M("bo"), cg, col(GC), ALU.is_equal)
-    for n, v in (("n1", -1.0), ("n2", -2.0), ("i2", 2.0), ("i3", 3.0), ("i64", 64.0), ("n64", -64.0)):
+    for n, v in (("n1", -1.0), ("n2", -2.0), ("i2", 2.0), ("i64", 64.0), ("n64", -64.0)):
         lin(M(n), M("i1"), v)
-    for n, v in (("bo2", 2.0), ("nbo", -1.0), ("bo64", 64.0), ("nbo64", -64.0), ("bos", 1.0 / 8192), ("bo3", 3.0)):
+    for n, v in (("bo2", 2.0), ("nbo", -1.0), ("bo64", 768.0), ("bos", 1.0 / 8192), ("bo3", 64.0)):
         lin(M(n), M("bo"), v)
     ts(R("diag", 0, 128), R("j16", 0, 128), col(LC), ALU.is_equal)
-    ts(R("seg", 0, 128), R("j16", 0, 128), 0.5, ALU.is_ge)
+    f = fact(R("seg", 0, 128), R("j16", 0, 128), ACT.Sigmoid, -128.0, 256.0)
+    add(f[:5] + (f[5] + 1300.0,) + f[6:])
     tt(R("dum", 0, 128), R("dum", 0, 128), R("diag", 0, 128), ALU.mult)
     pick(M("l2"), M("bo2"), 1, ALU.is_gt, 0.0)
     pick(M("mx"), M("l2"), 1, ALU.not_equal, -1.0)
@@ -240,18 +242,23 @@ def build(costs):
     pick(M("m4"), M("nmx"), 1, ALU.not_equal, 3.5)
     pick(M("u3"), M("bo3"), -1, ALU.is_gt, 0.0)
     ts(R("dgb", 0, 144), R("c144", 0, 144), col(GC), ALU.subtract, 15.0, ALU.is_equal)
-    ts(R("sel", 0, NT), R("cs", 0, NT), col(GC), ALU.is_equal)
-    ts(R("nsel", 0, 512), R("cs", 0, NT, 2), col(GC), ALU.is_equal, -1.0, ALU.mult)
-    ts(R("cw", 0, 240), R("cg", 0, 240), 16.0, ALU.is_equal, 4096.0, ALU.mult)
+    ts(R("nsel", 0, 512), R("cs", 0, 512), col(GC), ALU.is_equal, -1.0, ALU.mult)
     ts(col(HI), col(PC), 64.0, ALU.is_ge, 16.0, ALU.mult)
-    ts(R("cw2", 0, 240), R("cg", 0, 240), col(HI), ALU.is_equal, 4096.0, ALU.mult)
+    ts(R("k2", 0, 32), R("cg", 0, 32), col(HI), ALU.is_equal, 4096.0, ALU.mult)
+    for h in range(2):
+        ts(R("sel", h, NT, 2), R("cs", 0, 512), col(GC), ALU.is_equal)
+    if any(OPT["zm"]):
+        ts(R("pi", 2, 3), R("pi", 0, 1), 16, ALU.bitwise_and)
+        lin(col(EV + 1), R("pi", 2, 3), 1.0 / 16)
+        lin(col(EV), col(EV + 1), -1.0, 1.0)
+        ts(R("pi", 3, 4), R("pi", 0, 1), 5, ALU.logical_shift_right)
+        lin(col(PR), R("pi", 3, 4), 16.0)
+        ts(R("npair", 0, 256), R("cs", 0, 256), col(PR), ALU.is_equal, -1.0, ALU.mult)
     ms(R("cv", 0, 512), 4096.0)
     for a, b, p0, p1, c0 in ((0, 512, 0, 128, -64), (512, 768, 0, 128, -64), (512, 768, 0, 64, 0)):
         add(("G", "tri", (R("cmp", a, b), R("cv", 0, b - a), p0, p1, c0), [R("cv", 0, 512)], [R("cmp", a, b)],
              170 + 2 * (b - a) * CYC, None))
     ms(R("n768", 0, 128), -768.0)
-    ms(R("two", 0, 128), 2.0)
-    ms(R("four", 0, 128), 4.0)
     lin(col(WC), R("wt", 0, 1), 0.25)
     lin(R("dgw", 0, 144), R("dgb", 0, 144), col(WC))
     lin(M("wm"), M("bo"), col(WC))
@@ -262,8 +269,8 @@ def build(costs):
     for a, b in parts(C3):
         t = mm(b - a, [(M("i1"), R("tv", a, b)), (M("n1"), R("da", a, b))])
         act(R("nq", a, b), t, ACT.Abs, 1533.5, 2.0)
-        lin(R("sb", WR + a, WR + b), R("nq", a, b), 1.0, -1.5 if a else 0.5)
-    for a, b in LD:
+        lin(R("sb", WR + a, WR + b), R("nq", a, b), 1.0, -1.5)
+    for q, (a, b) in enumerate(LD):
         ts(R("bt", a, b), R("xi", a, b), 3, ALU.bitwise_and)
         lin(R("rt", a, b), R("xi", a, b), (1.0 + 2.0 ** -18) / 64, BIG - 0.5)
     gB, gR, gX = R("bt", 0, P), R("rt", 0, P), R("xi", 0, P)
@@ -295,6 +302,8 @@ def build(costs):
             for src, a, b in ([(R("da", 0, NT), 0, NT)] if v == 0 else [(R(dn, WR, NT), WR, NT)]):
                 n, c0 = (b - a) // 16, v * 64 + a // 16
                 p = wrap("dgw", src[0], src[1], src[2], [(M("wm"), R("n768", 0, n))])
+                if v and OPT["late"]:
+                    ops[p[4]]["rd"].append(W(OPT["late"], 2))
                 cp(R("ci", c0, c0 + n), p)
                 ts(R("cj", c0, c0 + n), R("ci", c0, c0 + n), P - 1, ALU.bitwise_and)
                 cp(OF(k, a, b), R("cj", c0, c0 + n))
@@ -314,18 +323,22 @@ def build(costs):
             else:
                 e0, n = 512, 256
                 terms = [(R("sel", q * 256 + 64, q * 256 + 192), Z(k, 0, 64), q * 64) for q in range(4)]
-                terms[1:1] = [(Z(k, 0, 64), R("nsel", q * 64, q * 64 + 64), q // 2 * 64, q % 2 * 64) for q in range(8)]
+                if OPT["zm"][k]:
+                    for h in range(2):
+                        lin(R("w_zm", k * WR + 64 * h, k * WR + 64 * h + 64), Z(k, 0, 64), col(EV + h))
+                    terms.insert(0, (W("zm", k), R("npair", 0, 256)))
+                else:
+                    terms[1:1] = [(Z(k, 0, 64), R("nsel", q * 64, q * 64 + 64), q // 2 * 64, q % 2 * 64) for q in range(8)]
             tt(R("eq", eb + e0, eb + e0 + n), mm(n, terms), R("cmp", e0, e0 + n), ALU.is_equal)
-        terms = [(R("cw2", 96 - 32 * q, 224 - 32 * q), R("eq", eb + 512 + q * 64, eb + 576 + q * 64), 0) for q in range(4)]
-        terms += [(R("cw", 112 - 16 * q, 240 - 16 * q), R("eq", eb + q * 64, eb + q * 64 + 64), 64) for q in range(8)]
-        ofw = Z(k + 1, NT, ZB)
-        tt(ofw, mm(WR, [(M("bo"), zw)] + terms), R("dum", 0, 128), ALU.min)
-        if OPT["scan"][k]:
-            fold(so, ofw, W("sc", k))
-        elif t == 2:
-            offsets(k + 1, NT, ZB)
+        lo = [(R("eq", eb + 512 + q * 64, eb + 576 + q * 64), R("k2", 0, 32), 32 * q, 0) for q in range(4)]
+        hi = [(R("eq", eb + q * 64, eb + q * 64 + 64), R("cv", 0, 16), 16 * q, 64) for q in range(8)]
+        ofw, tw = W("ofw", k), W("tw", k)
+        p = mm(WR, [(zw, R("m_bo", 0, 64))] + lo + hi + [(zw, R("m_bo", 64, 128), 64)])
+        step(tw, p, 3000.0, -3000.0, 1.0)
+        tt(ofw, p, R("dum", 0, 128), ALU.min)
+        cp(so, mm(8, [(ofw, R("m_bo", 0, 128, 16))]))
         for a, b in parts(OPT["cb"][k]):
-            lin(B(a, b), ind(gB, OF(k, a, b)), 1.0, -2.0 if a else 0.0)
+            lin(B(a, b), ind(gB, OF(k, a, b)), 1.0, -2.0)
         for a, b in parts(OPT["cm"][k]):
             tt(MS(a, b), B(a, b), H(a, b), ALU.not_equal)
         rw = RG(0, WR)
@@ -335,7 +348,11 @@ def build(costs):
             for a, b in parts(OPT["cz"][k]):
                 relu(Z(k + 1, a, b), mm(b - a, [(M("i1"), RG(a, b)), (M("mz"), MS(a, b))]), col(BZ))
             for a, b in parts(OPT["cw"][k]):
-                offsets(k + 1, a, ZB if b == NT and not OPT["scan"][k] else b)
+                if b == WR:
+                    tt(W("sc", k), mm(WR, [(Z(k + 1, 0, WR), M("bo"))]), R("diag", 0, 128), ALU.mult)
+                    cp(OF(k + 1, 0, WR), mm(8, [(W("sc", k), R("m_bo", 0, 128, 16))]))
+                else:
+                    offsets(k + 1, a, b)
         elif not last:
             relu(rw, ind(gR, ow), -BIG)
         else:
@@ -344,31 +361,21 @@ def build(costs):
         A, bw, mis, un, ep, ad, bn = H(0, WR), B(0, WR), MS(0, WR), W("un", k), W("ep", k), W("ad", k), W("bn", k)
         c1, c4 = R("w_c", 2 * k * WR, (2 * k + 1) * WR), R("w_c", (2 * k + 1) * WR, (2 * k + 2) * WR)
         ts(W("e4", k), ind(gX, ow), 60, ALU.bitwise_and)
-        lin(ep, W("e4", k), 1.0, 704.0)
-        act(ad, mm(WR, [(M("i1"), ep), (M("n1"), dq)]), ACT.Abs, 64.0)
-        ts(un, A, 2.5, ALU.is_ge)
-        early = [(M("nbo64"), ofw), (M("bo64"), zw), (M("i1"), A)]
-        terms = [(M("n1"), bw), (M("nmx"), mis)]
-        both = t > 0 and OPT["c14"][k]
-        e4 = ([(M("nbo64"), ofw), (M("bo64"), zw)] if t == 1 else []) + [(M("n2"), un)]
-        t4 = [(M("i1"), bw), (M("m4"), mis)]
-        if both:
-            early += [x + (WR,) for x in e4]
-            terms += [x + (WR,) for x in t4]
-        elif t > 0:
-            step(c4, mm(WR, e4, t4), 4.0, -1024.0, 256.0)
-        n = 2 * WR if both else WR
-        step(R("w_c", c1[1], c1[1] + n), mm(n, early, terms, [(M("bos"), ad)]), col(TH), col(TB), 524288.0)
+        copy(ep, W("e4", k))
+        act(ad, mm(WR, [(M("n1"), dq), (M("i1"), ep)]), ACT.Abs, 768.0)
+        step(un, A, 0.5, -128.0, 256.0, True)
+        lin(W("bg", k), bw, 1.0, 2.0)
+        if t > 0:
+            step(c4, mm(WR, [(M("n2"), un), (M("i1"), bw), (M("m4"), mis)], [(tw, M("n2"))] if t == 1 else []),
+                 2.0, -512.0, 256.0)
+        step(c1, mm(WR, [(M("i1"), A), (M("n1"), bw), (M("nmx"), mis)], [(tw, M("n2")), (M("bos"), ad)]),
+             col(TH), col(TB), 524288.0)
         tt(dqn, mm(WR, [(M("i1"), ep)], [(M("bo64"), c1)]), dq, ALU.max)
         if OPT["bne"]:
-            tt(bn, mm(WR, [(M("i1"), R("two", 0, WR)), (M("nmx"), mis), (M("n1"), A)], [(M("i2"), c1)]), bw, ALU.max)
+            tt(bn, mm(WR, [(M("nmx"), mis), (M("n1"), A)], [(M("i2"), c1)]), W("bg", k), ALU.max)
         for a, b in parts(OPT["cx"][k]):
             terms = [(M("n1"), B(a, b)), (M("mx"), MS(a, b))]
-            late = []
-            if a == 0:
-                terms.append((M("i1"), R("four", 0, WR)))
-                late = [(M("n2"), c1)]
-            tt(H(a, b), mm(b - a, terms, late), H(a, b), ALU.min)
+            tt(H(a, b), mm(b - a, terms, [] if a else [(M("n2"), c1)]), H(a, b), ALU.min)
             if k == 2:
                 q = OPT["cx"][k].index(a)
                 if a == 0 and OPT["dfirst"]:
@@ -376,38 +383,38 @@ def build(costs):
                 c = WR + a if a or OPT["dfirst"] else 0
                 send(1 + q, R("lb", c, WR + b), R("sb", c, WR + b))
         if not OPT["bne"]:
-            tt(bn, mm(WR, [(M("i1"), R("two", 0, WR)), (M("nmx"), mis)], [(M("n1"), A)]), bw, ALU.max)
+            tt(bn, mm(WR, [(M("nmx"), mis)], [(M("n1"), A)]), W("bg", k), ALU.max)
         xe = [(M("i64"), rw), (M("i1"), ep), (M("i1"), dq)]
         xt = [(M("n1"), dqn), (M("i1"), bn)]
         if t > 0:
             sl, sw, dl = R("w_s", 2 * k * WR, (2 * k + 1) * WR), R("w_s", (2 * k + 1) * WR, (2 * k + 2) * WR), W("dl", k)
             un0, z0 = W("un", k - t), Z(k - t, 0, WR)
-            terms = [(M("nmx"), mis), (M("n1"), un), (M("n1"), bw), (M("i3"), un0)]
+            terms = [(M("nmx"), mis), (M("n1"), un), (M("n1"), W("bg", k)), (M("i64"), un0)]
             late = [(M("u3"), c4)]
             if t == 1:
-                terms.append((M("i3"), un0, WR))
+                terms.append((M("i64"), un0, WR))
                 late.append((M("u3"), c4, WR))
             n = 2 * WR if t == 1 else WR
-            step(R("w_s", sl[1], sl[1] + n), mm(n, terms, late), 3.5, -896.0, 256.0)
+            step(R("w_s", sl[1], sl[1] + n), mm(n, terms, late), 64.5, -16512.0, 256.0)
             u = mm(WR, [(M("i1"), rw), (M("nbo"), z0)] +
                    ([] if t == 1 else [(M("n1"), W("y", k - 1)), (M("n1"), W("zz", k - 1))]))
             tt(dl, u, sl, ALU.mult)
             if t == 1:
                 tt(W("y", k), u, sw, ALU.mult)
                 tt(W("zz", k), mm(WR, [(M("bo"), zw), (M("nbo"), z0)]), un, ALU.mult)
-            xt.append((M("n64"), dl))
-        xn = W("xn", k)
-        lin(xn, mm(WR, xe, xt), 1.0, -704.0)
-        if last:
-            if OPT["gyo"]:
-                add(gcopy(R("yo", 0, HO), R("xi", 0, HO)))
+            if k in (1, 2):
+                tt(W("rn", k), rw, dl, ALU.subtract)
+                xe, xt = xe[1:], xt + [(M("i64"), W("rn", k))]
             else:
-                lin(R("yo", 0, HO), R("xi", 0, HO), 1.0)
+                xt.append((M("n64"), dl))
+        xn = W("xn", k)
+        lin(xn, mm(WR, xe, xt), 1.0)
+        if last:
+            copy(R("yo", 0, HO), R("xi", 0, HO))
             cp(ind(R("yo", 0, TW), so), xn)
             dma("Y", ("yp", 0, HO), R("yo", 0, HO), [R("yo", 0, HO)], [], 128 * HO * 4)
             for a, b in parts(OPT["cx"][k]):
-                for c, d in parts([a, WR, b] if a < WR < b else [a, b]):
-                    act(R("nq", c, d), H(c, d), ACT.Abs, 0.5 if c else -3.5, 2.0)
+                act(R("nq", a, b), H(a, b), ACT.Abs, 0.5, 2.0)
                 terms = [(M("n1"), R("nq", a, b))]
                 if a == 0:
                     terms.append((M("i1"), dqn))
@@ -418,8 +425,8 @@ def build(costs):
         else:
             cp(ind(R("bt", 0, TW), so), bn)
             if k in (1, 2):
-                lin(W("rn", k), mm(WR, [(M("i1"), rw), (M("n1"), W("dl", k))]), 1.0, BIG)
-                cp(ind(R("rt", 0, TW), so), W("rn", k))
+                lin(W("rb", k), W("rn", k), 1.0, BIG)
+                cp(ind(R("rt", 0, TW), so), W("rb", k))
             cp(ind(R("xi", 0, TW), so), xn)
     return ops
 
@@ -455,8 +462,8 @@ QUEUES = ("V", "S", "PE", "G", "Y", "X", "link")
 
 def finish(kind, st, cost, free):
     if kind == "send":
-        free["link"] = max(free["link"], st + 1500.0) + cost
-        return free["link"] + 1000.0
+        free["link"] = max(free["link"], st + 1200.0) + cost
+        return free["link"] + 800.0
     return st + cost
 
 
@@ -599,9 +606,15 @@ def plan():
             r = replay(eng, kind, cost[0], COSTS[0][4], seq, hard, opens, last)
             if r is None:
                 return None
-            dd = [hard[i] + [r[2][i]] if i in r[2] else hard[i] for i in range(n)]
-            score = [r[0]] + [replay(eng, kind, cost[q], COSTS[q][4], seq, dd)[0] for q in range(1, len(COSTS))]
-            return (sum(w * s for w, s in zip(SHARE, score)) + 0.02 * sum(r[1]) / n, score, r, dd)
+            dd, score, total = None, [r[0]], r[0]
+            if whole[0]:
+                dd = list(hard)
+                for i in r[2]:
+                    dd[i] = hard[i] + [r[2][i]]
+                score += [replay(eng, kind, cost[q], COSTS[q][4], seq, dd)[0] for q in range(1, len(COSTS))]
+                total = sum(w * s for w, s in zip(SHARE, score))
+            return (total + OPT["mean"] * sum(r[1]) / n +
+                    OPT["load"] * sum(cost[0][i] for i in range(n) if eng[i] == "V"), score, r, dd)
 
         def move(seq, i, j):
             a, b = seq.index(j), seq.index(i)
@@ -614,27 +627,52 @@ def plan():
             mid = seq[a:b + 1]
             return seq[:a] + [x for x in mid if x in take] + [x for x in mid if x not in take] + seq[b + 1:]
 
+        def later(seq, j, i):
+            a, b = seq.index(j), seq.index(i)
+            take = {j}
+            for x in range(a, b + 1):
+                if seq[x] in take:
+                    take.update(succ[seq[x]])
+            if i in take:
+                return None
+            mid = seq[a:b + 1]
+            return seq[:a] + [x for x in mid if x not in take] + [x for x in mid if x in take] + seq[b + 1:]
+
         def setform(i, f):
             form[i] = f
             eng[i], kind[i] = ops[i]["alt"][f][0], ops[i]["alt"][f][1]
             for q in range(len(COSTS)):
                 cost[q][i] = sets[q][i]["alt"][f][3]
 
+        whole = [False]
         cur = judge(order)
         best = (cur, order, list(form))
         path = None
-        for it in range(OPT["steps"]):
+        for it in range(OPT["steps"] + 1):
+            if it == int(OPT["steps"] * OPT["part"]):
+                whole[0] = True
+                cur = judge(order)
+                best = (cur, order, list(form))
             if path is None:
                 path = []
                 i = max(range(n), key=lambda x: cur[2][1][x])
                 while i >= 0:
                     path.append(i)
                     i = cur[2][4][i]
-            i = path[int(rnd() * len(path))] if rnd() < 0.6 else int(rnd() * n)
+            x = int(rnd() * len(path))
+            crit = rnd() < OPT["crit"]
+            i = path[x] if crit else int(rnd() * n)
             old = form[i]
             seq = order
-            if len(ops[i]["alt"]) > 1 and rnd() < 0.25:
+            if len(ops[i]["alt"]) > 1 and rnd() < OPT["flip"]:
                 setform(i, (old + 1) % len(ops[i]["alt"]))
+            elif crit and x + 1 < len(path) and eng[path[x + 1]] == eng[i] and path[x + 1] not in dl[i] and eng[i] != "Y":
+                y = x + 1
+                while y + 1 < len(path) and eng[path[y + 1]] == eng[i] and rnd() < 0.5:
+                    y += 1
+                seq = move(order, i, path[y]) if rnd() < 0.5 else later(order, path[y], i)
+                if seq is None:
+                    continue
             elif eng[i] == "X" or (eng[i] == "Y" and not dl[i]):
                 continue
             else:
@@ -644,7 +682,7 @@ def plan():
                 if rnd() < 0.5:
                     seq = move(order, i, line[p - d]) if p >= d else None
                 else:
-                    seq = move(order, line[p + d], i) if p + d < len(line) else None
+                    seq = later(order, i, line[p + d]) if p + d < len(line) else None
                 if seq is None or (eng[i] == "Y" and not dl[line[max(p - d, 0)]]):
                     continue
             c = judge(seq)

@@ -10,17 +10,22 @@ BIG = 8388608.0
 C3 = [0, 128, 576, 1024]
 C2 = [0, 512, 1024]
 OPT = dict(cb=[C3] * 6, cm=[C3] * 6, cr=[C3] * 6, cz=[C3] * 6, cx=[C3] * 6, cw=[[0, 128, 1024]] * 6,
-           zm=(1,) * 6, zv=[(0, 1, 1)] * 6, rv=(0, 0, 0, 1, 1), gcp=1, split=1, bne=1, dfirst=1, late="ad",
-           tries=40, steps=100000, heat=300.0, crit=0.7, flip=0.05, mean=0.5, load=0.2, part=0.7)
+           zm=(1,) * 6, zv=[(0, 0, 0)] * 6, gcp=1, split=(1, 1, 1, 0, 0, 1), bne=1, dfirst=1, late="dl",
+           boost=(0.0, 0.0), hold=0, scan=0, otv=(0, 0, 1), dfv=(0, 0, 1, 2, 2, 2), sou=1, sig=0,
+           ld=[0, 1024, 1792, 2048], flat=1, sends=[0, 128, 256, 704, 1152], yd=[0, 576, 1024],
+           bx=(0,) * 6, rx=0, pe=(25.0, 5.0), de=(0,) * 6, join=(1,) * 6,
+           tries=40, steps=480000, heat=300.0, crit=0.7, flip=0.05, mean=0.5, load=0.2, part=0.93, sort=200, seed=2,
+           runs=0, short=0, warm=300.0)
 
 BF, F32, F16, I32, U16 = "bfloat16", "float32", "float16", "int32", "uint16"
-WB = ["un", "ep", "ad", "dw", "bn", "bg", "tw"]
+WB = ["df", "x", "un", "ep", "ad", "dw", "bn", "bg", "tw"]
 WF = ["xn", "rb"]
 WH = ["rn", "dl", "y", "zz", "sc", "sf", "ofw", "zm"]
-MB = ["i1", "n1", "n2", "i2", "i3", "i64", "n64", "bo", "nbo", "bo64", "bos", "bo2", "l2", "l8", "mx5", "mx", "nmx", "m4",
+MB = ["i1", "n1", "n2", "i2", "i3", "i64", "n64", "bo", "nbo", "bo64", "bos", "bo2", "l2", "mxw", "nmxw", "l8", "mx5", "mx", "nmx", "m4",
       "g2", "mz", "bo3", "u3", "wm"]
 SCRATCH = {
     "xi": ("sbuf", [128, TW], I32), "bt": ("sbuf", [128, TW], I32), "rt": ("sbuf", [128, TW], F32),
+    "ri": ("sbuf", [128, TW], I32), "nt": ("sbuf", [128, 2 * NT], BF),
     "yo": ("sbuf", [128, TW], F32),
     "tv": ("sbuf", [128, NT], BF), "da": ("sbuf", [128, NT], BF), "dbb": ("sbuf", [128, NT], BF),
     "sb": ("sbuf", [128, NT + WR], BF), "lb": ("sbuf", [128, NT + WR], BF),
@@ -29,17 +34,17 @@ SCRATCH = {
     "eq": ("sbuf", [128, 2 * 768], BF), "off": ("sbuf", [128, 7 * 72], U16),
     "ci": ("sbuf", [128, 128], I32), "cj": ("sbuf", [128, 128], I32),
     "wi": ("sbuf", [128, 256], I32), "wj": ("sbuf", [128, 256], I32),
-    "w_e4": ("sbuf", [128, 6 * WR], I32),
+    "w_e4": ("sbuf", [128, 6 * WR], I32), "w_b3": ("sbuf", [128, 6 * WR], I32),
     "w_c": ("sbuf", [128, 12 * WR], BF), "w_s": ("sbuf", [128, 12 * WR], BF),
     "wt": ("sbuf", [128, 4], I32), "tht": ("sbuf", [128, 4], I32), "pi": ("sbuf", [128, 8], I32),
-    "col": ("sbuf", [128, 24], F32),
+    "col": ("sbuf", [128, 24], F32), "row": ("sbuf", [128, 256], I32), "rowb": ("sbuf", [128, 256], BF),
     "c144": ("sbuf", [128, 144], BF), "cg": ("sbuf", [128, 240], BF), "cs": ("sbuf", [128, 512], BF),
     "sel": ("sbuf", [128, NT], BF), "nsel": ("sbuf", [128, 512], BF), "cmp": ("sbuf", [128, 768], BF),
     "cv": ("sbuf", [128, 512], BF), "seg": ("sbuf", [128, 128], BF), "diag": ("sbuf", [128, 128], BF),
-    "j16": ("sbuf", [128, 128], BF),
+    "j16": ("sbuf", [128, 128], BF), "six": ("sbuf", [128, 128], BF),
     "dgb": ("sbuf", [128, 144], BF), "dgw": ("sbuf", [128, 144], BF),
-    "k2": ("sbuf", [128, 32], BF), "npair": ("sbuf", [128, 256], BF), "n768": ("sbuf", [128, 128], BF),
-    "dum": ("sbuf", [128, 128], F32),
+    "k2": ("sbuf", [128, 64], BF), "npair": ("sbuf", [128, 256], BF), "n768": ("sbuf", [128, 128], BF),
+    "dum": ("sbuf", [128, 128], F16), "dn": ("sbuf", [128, NT], BF),
 }
 for _n in WB:
     SCRATCH["w_" + _n] = ("sbuf", [128, 6 * WR], BF)
@@ -54,8 +59,9 @@ for _n in range(8):
 NDMA = 16
 SEMAPHORES = ["V", "S", "PE", "G", "sent"] + ["d%d" % i for i in range(NDMA)] + ["r%d" % i for i in range(5)]
 
-COSTS = [(0.9, 0.45, 1.56, 3.8, 90.0, 250.0, 80.0, 1600.0), (0.85, 0.43, 1.1, 1.8, 60.0, 160.0, 40.0, 2200.0),
-         (1.2, 0.6, 2.0, 5.5, 160.0, 350.0, 120.0, 1200.0)]
+COSTS = [(0.84, 0.42, 1.56, 3.8, 150.0, 280.0, 90.0, 1500.0, 15.0, 25.0),
+         (0.9, 0.45, 1.1, 1.8, 80.0, 200.0, 60.0, 2000.0, 40.0, 60.0),
+         (1.2, 0.6, 2.0, 5.5, 150.0, 350.0, 120.0, 1300.0, 20.0, 20.0)]
 
 
 def R(name, a, b, step=1):
@@ -64,7 +70,8 @@ def R(name, a, b, step=1):
 
 def build(costs):
     ops = []
-    CYC, PECYC, GA, SC, _, DMA, RDMA, FIX = costs
+    now = [0]
+    CYC, PECYC, GA, SC, _, DMA, RDMA, FIX, ROW, RROW = costs
 
     def width(r):
         return len(range(r[1], r[2], r[3]))
@@ -117,6 +124,8 @@ def build(costs):
         return add(vop("tt", out, [a, b], op))
 
     def cp(out, a):
+        if OPT["sou"] and out[0] != "ind" and a[0] == "ps":
+            return add(vop("cp", out, [a], None), fact(out, a, ACT.Identity))
         return add(vop("cp", out, [a], None))
 
     def ms(out, v):
@@ -133,29 +142,29 @@ def build(costs):
 
     def step(out, a, level, bias, scale, vector=False):
         f = [fact(out, a, ACT.Sigmoid, bias, scale), fts(out, a, level, ALU.is_ge)]
-        f[0][3].append(R("seg", 0, 128))
+        f[0][3].append(col(7))
         return add(*(f[::-1] if vector else f))
 
     def mm(n, *groups):
-        if not OPT["split"]:
+        if not OPT["split"][now[0]]:
             groups = [[t for gr in groups for t in gr]]
         groups = [gr for gr in groups if gr]
         first = None
         for q, terms in enumerate(groups):
-            c = 30.0
+            c = OPT["pe"][0]
             rd = []
             for t in terms:
-                c += max(64, width(t[1])) * PECYC + 5
+                c += max(64, width(t[1])) * PECYC + OPT["pe"][1]
                 rd += [t[0], t[1]]
             i = add(("PE", "mm", (n, terms, first, q == len(groups) - 1), rd, [], c, first))
             first = i if first is None else first
         return ("ps", 0, n, 1, first)
 
-    def dma(q, out, src, rd, wr, nbytes):
-        return add((q, "dma", (out, src), rd, wr, FIX + nbytes / DMA, None))
+    def dma(q, out, src, rd, wr, nbytes, rows=8):
+        return add((q, "dma", (out, src), rd, wr, FIX + rows * ROW + nbytes / DMA, None))
 
     def send(k, out, src):
-        i = add(("G", "send", (k, out, src), [src], [], width(src) * 256 / RDMA, None))
+        i = add(("G", "send", (k, out, src), [src], [], 16 * RROW + width(src) * 256 / RDMA, None))
         j = add(("X", "recv", (k,), [], [out], 0.0, None))
         ops[j]["after"] = i
 
@@ -174,8 +183,11 @@ def build(costs):
     def iota(out, pat, b, cm):
         add(("G", "iota", (out, pat, b, cm), [], [out], 130 + 2 * width(out) * CYC, None))
 
-    def pick(out, a, sign, op, fill):
-        add(("G", "pick", (out, a, sign, op, fill), [a], [out], 170 + 2 * width(out) * CYC, None))
+    def fpick(out, a, sign, op, fill):
+        return ("G", "pick", (out, a, sign, op, fill), [a], [out], 170 + 2 * width(out) * CYC, None)
+
+    def pick(*a):
+        add(fpick(*a))
 
     def wrap(mat, plane, a, b, more=()):
         return mm((b - a) // 16, [(R(mat, 15 - i, 143 - i), R(plane, a + i, b, 16)) for i in range(16)] + list(more))
@@ -184,7 +196,7 @@ def build(costs):
         return R("nz", k * ZB + a, k * ZB + b)
 
     def OF(k, a, b):
-        return R("off", k * 72 + a // 16, k * 72 + b // 16)
+        return R("off", k * 72 + 8 + a // 16, k * 72 + 8 + b // 16)
 
     def offsets(k, a, b):
         cp(OF(k, a, b), wrap("dgb", "nz", k * ZB + a, k * ZB + b))
@@ -204,49 +216,63 @@ def build(costs):
         return list(zip(c[:-1], c[1:]))
 
     dma("Y", R("tv", 0, NT), ("trav", 0, NT), [], [R("tv", 0, NT)], 128 * NT * 2)
-    dma("S", R("wt", 0, 1), ("wts", 0, 1), [], [R("wt", 0, 4)], 512)
-    dma("S", R("tht", 0, 1), ("th", 0, 1), [], [R("tht", 0, 4)], 512)
-    for a, b in LD:
-        dma("Y", R("xi", a, b), ("peers", a, b), [], [R("xi", a, b)], 512 * b + 128 * NT * 2)
+    LD = parts(OPT["ld"])
+    flat = OPT["flat"]
+    if flat:
+        dma("S", ("row", 0, 128, 1, "one"), ("wts", 0, 1), [], [R("row", 0, 128)], 512, 1)
+        dma("S", ("row", 128, 256, 1, "one"), ("th", 0, 1), [], [R("row", 128, 256)], 512, 1)
+    else:
+        dma("S", R("wt", 0, 1), ("wts", 0, 1), [], [R("wt", 0, 4)], 512)
+        dma("S", R("tht", 0, 1), ("th", 0, 1), [], [R("tht", 0, 4)], 512)
+    for q, (a, b) in enumerate(LD):
+        dma("Y", R("xi", a, b), ("peers", a, b), [], [R("xi", a, b)], 512 * b + 128 * NT * 2, 8 * q + (16 if flat else 32))
     PC, GC, LC, PR, WC, TH, TB, L15, BZ, N15, HI, BT, EV = range(13)
     iota(R("pi", 0, 1), [[0, 1]], 0, 1)
     iota(R("c144", 0, 144), [[1, 144]], 0, 0)
     iota(R("cg", 0, 128), [[16, 8], [0, 16]], 0, 0)
-    iota(R("dum", 0, 128), [[0, 128]], P, 2)
     iota(R("cs", 0, 512), [[16, 8], [0, 64]], 0, 0)
     iota(R("j16", 0, 128), [[0, 8], [1, 16]], 0, 0)
     c128 = R("c144", 0, 128)
     cg = R("cg", 0, 128)
-    cp(col(PC), R("pi", 0, 1))
+    iota(R("col", PC, PC + 1), [[0, 1]], 0, 1)
+    iota(R("col", N15, N15 + 1), [[0, 1]], P, 2)
     ts(R("pi", 1, 2), R("pi", 0, 1), 112, ALU.bitwise_and)
     cp(col(GC), R("pi", 1, 2))
     act(col(LC), col(GC), ACT.Identity, col(PC), -1.0)
-    act(col(L15), col(LC), ACT.Relu, -14.0, 1.0)
-    lin(col(BZ), col(L15), 4096.0, -4096.0)
-    lin(col(N15), col(L15), -2048.0, 2048.0)
+    if OPT["sig"]:
+        f = fact(col(L15), col(LC), ACT.Sigmoid, -3712.0, 256.0)
+        add(f[:5] + (f[5] + 1300.0,) + f[6:])
+        lin(col(BZ), col(L15), 4096.0, -4096.0)
+    else:
+        ts(col(BZ), col(LC), 14.5, ALU.is_lt, -4096.0, ALU.mult)
+    NAT = any(any(z) for z in OPT["zv"])
+    RB = 0.0 if NAT else BIG
     ts(M("i1"), c128, col(PC), ALU.is_equal)
     ts(M("bo"), cg, col(GC), ALU.is_equal)
-    for n, v in (("n1", -1.0), ("n2", -2.0), ("i2", 2.0), ("i64", 64.0), ("n64", -64.0)):
-        lin(M(n), M("i1"), v)
-    for n, v in (("bo2", 2.0), ("nbo", -1.0), ("bo64", 768.0), ("bos", 1.0 / 8192), ("bo3", 64.0)):
+    for n, v in (("n1", -1.0), ("n2", -2.0), ("i64", 64.0)):
+        add(fpick(M(n), M("i1"), 1, ALU.not_equal, v), fact(M(n), M("i1"), ACT.Identity, 0.0, v), fts(M(n), M("i1"), v, ALU.mult))
+    for n, v in (("bo2", 2.0), ("nbo", -1.0), ("bo64", 384.0), ("bos", 1.0 / 8192), ("bo3", 64.0)):
         lin(M(n), M("bo"), v)
     ts(R("diag", 0, 128), R("j16", 0, 128), col(LC), ALU.is_equal)
-    f = fact(R("seg", 0, 128), R("j16", 0, 128), ACT.Sigmoid, -128.0, 256.0)
-    add(f[:5] + (f[5] + 1300.0,) + f[6:])
-    tt(R("dum", 0, 128), R("dum", 0, 128), R("diag", 0, 128), ALU.mult)
+    if OPT["scan"]:
+        ts(R("seg", 0, 128), R("j16", 0, 128), 0.5, ALU.is_ge)
+    lin(R("dum", 0, 128), R("diag", 0, 128), col(N15))
     pick(M("l2"), M("bo2"), 1, ALU.is_gt, 0.0)
     pick(M("mx"), M("l2"), 1, ALU.not_equal, -1.0)
     lin(M("nmx"), M("mx"), -1.0)
-    pick(M("g2"), M("nmx"), 1, ALU.not_equal, 2.0)
-    lin(M("mz"), M("g2"), col(N15))
+    lin(M("mz"), M("mx"), col(BZ))
+    if NAT:
+        lin(col(BT), col(BZ), 4.0, 16384.0)
+        lin(M("l8"), M("l2"), 4.0)
+        pick(M("mx5"), M("l8"), 1, ALU.not_equal, -5.0)
+    pick(M("mxw"), M("l2"), 1, ALU.not_equal, -2.0)
+    pick(M("nmxw"), M("nmx"), 1, ALU.not_equal, 2.0)
     pick(M("m4"), M("nmx"), 1, ALU.not_equal, 3.5)
     pick(M("u3"), M("bo3"), -1, ALU.is_gt, 0.0)
     ts(R("dgb", 0, 144), R("c144", 0, 144), col(GC), ALU.subtract, 15.0, ALU.is_equal)
     ts(R("nsel", 0, 512), R("cs", 0, 512), col(GC), ALU.is_equal, -1.0, ALU.mult)
-    ts(col(HI), col(PC), 64.0, ALU.is_ge, 16.0, ALU.mult)
-    ts(R("k2", 0, 32), R("cg", 0, 32), col(HI), ALU.is_equal, 4096.0, ALU.mult)
     for h in range(2):
-        ts(R("sel", h, NT, 2), R("cs", 0, 512), col(GC), ALU.is_equal)
+        lin(R("sel", h, NT, 2), R("nsel", 0, 512), -1.0)
     if any(OPT["zm"]):
         ts(R("pi", 2, 3), R("pi", 0, 1), 16, ALU.bitwise_and)
         lin(col(EV + 1), R("pi", 2, 3), 1.0 / 16)
@@ -254,29 +280,48 @@ def build(costs):
         ts(R("pi", 3, 4), R("pi", 0, 1), 5, ALU.logical_shift_right)
         lin(col(PR), R("pi", 3, 4), 16.0)
         ts(R("npair", 0, 256), R("cs", 0, 256), col(PR), ALU.is_equal, -1.0, ALU.mult)
-    ms(R("cv", 0, 512), 4096.0)
-    for a, b, p0, p1, c0 in ((0, 512, 0, 128, -64), (512, 768, 0, 128, -64), (512, 768, 0, 64, 0)):
-        add(("G", "tri", (R("cmp", a, b), R("cv", 0, b - a), p0, p1, c0), [R("cv", 0, 512)], [R("cmp", a, b)],
-             170 + 2 * (b - a) * CYC, None))
+    ms(R("cv", 0, 32), 4096.0)
+    iota(R("col", TH, TH + 1), [[0, 1]], -64, 1)
+    ts(R("pi", 4, 5), R("pi", 0, 1), 63, ALU.bitwise_and)
+    cp(col(HI), R("pi", 4, 5))
+    for a, b, c in ((0, 512, TH), (512, 768, HI)):
+        ts(R("cmp", a, a + 64), R("c144", 0, 64), col(c), ALU.is_le, 4096.0, ALU.mult)
+        w = 64
+        while w < b - a:
+            copy(R("cmp", a + w, a + 2 * w), R("cmp", a, a + w))
+            w *= 2
+    for out, a, sign in ((R("k2", 32, 64), R("cv", 0, 32), 1), (R("k2", 0, 32), R("k2", 32, 64), -1)):
+        add(("G", "half", (out, a, sign), [a], [out], 170 + 64 * CYC, None))
     ms(R("n768", 0, 128), -768.0)
-    lin(col(WC), R("wt", 0, 1), 0.25)
+    if min(OPT["dfv"]) < 2:
+        ms(R("six", 0, 128), 6144.0)
+    wt, tht = R("wt", 0, 1), R("tht", 0, 1)
+    if flat:
+        add(("V", "cp", (("rowb", 0, 256, 1, "one"), [("row", 0, 256, 1, "one")], None), [R("row", 0, 256)],
+             [R("rowb", 0, 256)], 256 * CYC + 30, None))
+        p = mm(2, [(("rowb", 128 * h, 128 * h + 128, 1, "one"), ("m_i1", 0, 1, 1, "one"), h) for h in range(2)])
+        wt, tht = ("ps", 0, 1, 1, p[4]), ("ps", 1, 2, 1, p[4])
+    lin(col(WC), wt, 0.25)
     lin(R("dgw", 0, 144), R("dgb", 0, 144), col(WC))
     lin(M("wm"), M("bo"), col(WC))
-    lin(col(TH), R("tht", 0, 1), 1.0 / 2048, 4.0 - 1.0 / 4096)
-    lin(col(TB), col(TH), -524288.0)
+    lin(col(TB), tht, -1.0 / 2048, 1.0 / 4096 - 4.0)
     lin(R("da", 0, NT), R("tv", 0, NT), 1.0, 767.0)
     send(0, R("dbb", WR, NT), R("da", WR, NT))
     for a, b in parts(C3):
         t = mm(b - a, [(M("i1"), R("tv", a, b)), (M("n1"), R("da", a, b))])
         act(R("nq", a, b), t, ACT.Abs, 1533.5, 2.0)
-        lin(R("sb", WR + a, WR + b), R("nq", a, b), 1.0, -1.5)
+        lin(R("sb", WR + a, WR + b), R("nq", a, b), 1.0, -3.5 if a and NAT else -1.5)
     for q, (a, b) in enumerate(LD):
         ts(R("bt", a, b), R("xi", a, b), 3, ALU.bitwise_and)
-        lin(R("rt", a, b), R("xi", a, b), (1.0 + 2.0 ** -18) / 64, BIG - 0.5)
-    gB, gR, gX = R("bt", 0, P), R("rt", 0, P), R("xi", 0, P)
+        if NAT:
+            ts(R("ri", a, b), R("xi", a, b), 6, ALU.logical_shift_right)
+        else:
+            lin(R("rt", a, b), R("xi", a, b), (1.0 + 2.0 ** -18) / 64, BIG - 0.5)
+    gB, gR, gX = R("bt", 0, P), R("ri" if NAT else "rt", 0, P), R("xi", 0, P)
 
     for k in range(6):
         v, t = divmod(k, 3)
+        now[0] = k
         hb, dn = ("sb", "da") if v == 0 else ("lb", "dbb")
         last = k == 5
         pl = (k % 2) * NT
@@ -294,7 +339,7 @@ def build(costs):
             return R("nr", pl + a, pl + b)
 
         ow = OF(k, 0, WR)
-        so = OF(k + 1, NT, ZB)
+        so = OF(k + 1, -WR, 0)
         dq = (R("da", 0, WR) if v == 0 else R("lb", 0, WR)) if t == 0 else W("dw", k - 1)
         dqn = W("dw", k) if k != 2 else R("sb", 0, WR)
         zw = Z(k, 0, WR)
@@ -311,9 +356,14 @@ def build(costs):
             p = mm(WR, [(M("wm"), R("n768", 0, 128)), (M("wm"), dq)])
             cp(R("wi", c0, c0 + WR), p)
             ts(R("wj", c0, c0 + WR), R("wi", c0, c0 + WR), P - 1, ALU.bitwise_and)
-            tt(zw, R("wj", c0, c0 + WR), R("diag", 0, 128), ALU.mult)
-            if v:
+            if v and OPT["scan"]:
+                tt(zw, R("wj", c0, c0 + WR), R("diag", 0, 128), ALU.mult)
                 fold(ow, zw, W("sf", k))
+            else:
+                lin(zw, R("wj", c0, c0 + WR), 1.0 / 16)
+                if v:
+                    tt(W("sf", k), mm(WR, [(zw, M("bo"))]), R("diag", 0, 128), ALU.mult)
+                    cp(ow, mm(8, [(W("sf", k), R("m_bo", 0, 128, 16))]))
         eb = (k % 2) * 768
         for hf in range(2):
             if hf == 0:
@@ -334,27 +384,41 @@ def build(costs):
         hi = [(R("eq", eb + q * 64, eb + q * 64 + 64), R("cv", 0, 16), 16 * q, 64) for q in range(8)]
         ofw, tw = W("ofw", k), W("tw", k)
         p = mm(WR, [(zw, R("m_bo", 0, 64))] + lo + hi + [(zw, R("m_bo", 64, 128), 64)])
-        step(tw, p, 3000.0, -3000.0, 1.0)
+        relu(tw, p, -2048.0)
         tt(ofw, p, R("dum", 0, 128), ALU.min)
-        cp(so, mm(8, [(ofw, R("m_bo", 0, 128, 16))]))
-        for a, b in parts(OPT["cb"][k]):
-            lin(B(a, b), ind(gB, OF(k, a, b)), 1.0, -2.0)
+        join = t < 2 and OPT["join"][k] and OPT["cw"][k][1] == WR
+        if not join:
+            cp(so, mm(8, [(ofw, R("m_bo", 0, 128, 16))]))
+        if OPT["bx"][k]:
+            ts(W("b3", k), ind(gX, ow), 3, ALU.bitwise_and)
+            lin(B(0, WR), W("b3", k), 1.0, -2.0)
+            copy(W("bg", k), W("b3", k))
+        for a, b in parts(OPT["cb"][k])[OPT["bx"][k]:]:
+            lin(B(a, b), ind(gB, OF(k, a, b)), 1.0, -4.0 if a and NAT else -2.0)
         for a, b in parts(OPT["cm"][k]):
             tt(MS(a, b), B(a, b), H(a, b), ALU.not_equal)
         rw = RG(0, WR)
+        shared = {}
         if t < 2:
-            for a, b in parts(OPT["cr"][k]):
-                relu(RG(a, b), ind(gR, OF(k, a, b)), -BIG)
-            for a, b in parts(OPT["cz"][k]):
-                relu(Z(k + 1, a, b), mm(b - a, [(M("i1"), RG(a, b)), (M("mz"), MS(a, b))]), col(BZ))
+            for q, (a, b) in enumerate(parts(OPT["cz"][k])):
+                if OPT["zv"][k][q]:
+                    shared[a] = mm(b - a, [(M("n1"), B(a, b)), (M("mx5"), MS(a, b))])
+                    act(R("nt", pl + a, pl + b), shared[a], ACT.Relu, col(BT), -4096.0)
+                    tt(Z(k + 1, a, b), ind(gR, OF(k, a, b)), R("nt", pl + a, pl + b), ALU.min)
+                else:
+                    relu(RG(a, b), ind(gR, OF(k, a, b)), -RB)
+                    relu(Z(k + 1, a, b), mm(b - a, [(M("i1"), RG(a, b)), (M("mz"), MS(a, b))]), col(BZ))
             for a, b in parts(OPT["cw"][k]):
                 if b == WR:
                     tt(W("sc", k), mm(WR, [(Z(k + 1, 0, WR), M("bo"))]), R("diag", 0, 128), ALU.mult)
-                    cp(OF(k + 1, 0, WR), mm(8, [(W("sc", k), R("m_bo", 0, 128, 16))]))
+                    if join:
+                        cp(OF(k + 1, -WR, WR), mm(16, [(ofw, R("m_bo", 0, 128, 16)), (W("sc", k), R("m_bo", 0, 128, 16), 8)]))
+                    else:
+                        cp(OF(k + 1, 0, WR), mm(8, [(W("sc", k), R("m_bo", 0, 128, 16))]))
                 else:
                     offsets(k + 1, a, b)
-        elif not last:
-            relu(rw, ind(gR, ow), -BIG)
+        elif not last and not OPT["rx"]:
+            relu(rw, ind(gR, ow), -RB)
         else:
             lin(W("rb", k), ind(gX, ow), (1.0 + 2.0 ** -18) / 64, BIG - 0.5)
             relu(rw, W("rb", k), -BIG)
@@ -362,30 +426,41 @@ def build(costs):
         c1, c4 = R("w_c", 2 * k * WR, (2 * k + 1) * WR), R("w_c", (2 * k + 1) * WR, (2 * k + 2) * WR)
         ts(W("e4", k), ind(gX, ow), 60, ALU.bitwise_and)
         copy(ep, W("e4", k))
-        act(ad, mm(WR, [(M("n1"), dq), (M("i1"), ep)]), ACT.Abs, 768.0)
-        step(un, A, 0.5, -128.0, 256.0, True)
-        lin(W("bg", k), bw, 1.0, 2.0)
+        if OPT["dfv"][k]:
+            tt(W("df", k), W("e4", k) if OPT["de"][k] else ep, dq, ALU.subtract)
+            act(ad, W("df", k), ACT.Abs, 768.0)
+        else:
+            act(ad, mm(WR, [(M("n1"), dq), (M("i1"), ep)]), ACT.Abs, 768.0)
+        add(fact(un, A, ACT.Relu, 0.0, 1.0 if t else 4.0), fts(un, A, 0.0, ALU.max, 1.0 if t else 4.0, ALU.mult))
+        if not OPT["bx"][k]:
+            lin(W("bg", k), bw, 1.0, 2.0)
         if t > 0:
-            step(c4, mm(WR, [(M("n2"), un), (M("i1"), bw), (M("m4"), mis)], [(tw, M("n2"))] if t == 1 else []),
-                 2.0, -512.0, 256.0)
-        step(c1, mm(WR, [(M("i1"), A), (M("n1"), bw), (M("nmx"), mis)], [(tw, M("n2")), (M("bos"), ad)]),
-             col(TH), col(TB), 524288.0)
-        tt(dqn, mm(WR, [(M("i1"), ep)], [(M("bo64"), c1)]), dq, ALU.max)
+            relu(c4, mm(WR, [(M("n2"), un), (M("i1"), bw), (M("m4"), mis)], [(tw, M("n2"))] if t == 1 else []), -2.0)
+        act(c1, mm(WR, [(M("i1"), A), (M("n1"), bw), (M("nmx"), mis)], [(tw, M("n2")), (M("bos"), ad)]),
+            ACT.Sign, col(TB))
+        if OPT["dfv"][k] == 2:
+            relu(W("x", k), mm(WR, [(M("i1"), W("df", k))], [(M("bo64"), c1)]), 6144.0)
+            i = tt(dqn, dq, W("x", k), ALU.add)
+        else:
+            i = tt(dqn, mm(WR, [(M("i1"), ep), (M("i1"), R("six", 0, WR))], [(M("bo64"), c1)]), dq, ALU.max)
+        ops[i]["boost"] = OPT["boost"][0] if k == 2 else 0.0
         if OPT["bne"]:
-            tt(bn, mm(WR, [(M("nmx"), mis), (M("n1"), A)], [(M("i2"), c1)]), W("bg", k), ALU.max)
+            tt(bn, mm(WR, [(M("nmxw"), mis), (M("n1"), A)], [(M("i1"), c1)]), W("bg", k), ALU.max)
+        held = parts(OPT["cx"][k])[-OPT["hold"]:] if last and OPT["hold"] else []
         for a, b in parts(OPT["cx"][k]):
-            terms = [(M("n1"), B(a, b)), (M("mx"), MS(a, b))]
-            tt(H(a, b), mm(b - a, terms, [] if a else [(M("n2"), c1)]), H(a, b), ALU.min)
-            if k == 2:
-                q = OPT["cx"][k].index(a)
-                if a == 0 and OPT["dfirst"]:
-                    send(4, R("lb", 0, WR), R("sb", 0, WR))
-                c = WR + a if a or OPT["dfirst"] else 0
-                send(1 + q, R("lb", c, WR + b), R("sb", c, WR + b))
+            if (a, b) in held:
+                continue
+            terms = [(M("n1"), B(a, b)), (M(("mx5" if NAT else "mx") if a else "mxw"), MS(a, b))]
+            tt(H(a, b), shared.get(a) or mm(b - a, terms, [] if a else [(M("n1"), c1)]), H(a, b), ALU.min)
+        if k == 2:
+            for q, (a, b) in enumerate(parts(OPT["sends"])):
+                send(1 + q, R("lb", a, b), R("sb", a, b))
         if not OPT["bne"]:
             tt(bn, mm(WR, [(M("nmx"), mis)], [(M("n1"), A)]), W("bg", k), ALU.max)
         xe = [(M("i64"), rw), (M("i1"), ep), (M("i1"), dq)]
         xt = [(M("n1"), dqn), (M("i1"), bn)]
+        if OPT["dfv"][k] == 2:
+            xe, xt = xe[:2], [(M("n1"), W("x", k)), (M("i1"), bn)]
         if t > 0:
             sl, sw, dl = R("w_s", 2 * k * WR, (2 * k + 1) * WR), R("w_s", (2 * k + 1) * WR, (2 * k + 2) * WR), W("dl", k)
             un0, z0 = W("un", k - t), Z(k - t, 0, WR)
@@ -395,38 +470,52 @@ def build(costs):
                 terms.append((M("i64"), un0, WR))
                 late.append((M("u3"), c4, WR))
             n = 2 * WR if t == 1 else WR
-            step(R("w_s", sl[1], sl[1] + n), mm(n, terms, late), 64.5, -16512.0, 256.0)
-            u = mm(WR, [(M("i1"), rw), (M("nbo"), z0)] +
-                   ([] if t == 1 else [(M("n1"), W("y", k - 1)), (M("n1"), W("zz", k - 1))]))
+            if OPT["sig"]:
+                step(R("w_s", sl[1], sl[1] + n), mm(n, terms, late), 256.5, -65664.0, 256.0)
+            else:
+                ts(R("w_s", sl[1], sl[1] + n), mm(n, terms, late), 256.5, ALU.is_ge)
+            u = mm(WR, [(M("n1"), rw), (M("bo"), z0)] +
+                   ([] if t == 1 else [(M("n1"), W("y", k - 1)), (M("i1"), W("zz", k - 1))]))
             tt(dl, u, sl, ALU.mult)
             if t == 1:
                 tt(W("y", k), u, sw, ALU.mult)
                 tt(W("zz", k), mm(WR, [(M("bo"), zw), (M("nbo"), z0)]), un, ALU.mult)
             if k in (1, 2):
-                tt(W("rn", k), rw, dl, ALU.subtract)
+                tt(W("rn", k), rw, dl, ALU.add)
                 xe, xt = xe[1:], xt + [(M("i64"), W("rn", k))]
             else:
-                xt.append((M("n64"), dl))
+                xt.append((M("i64"), dl))
         xn = W("xn", k)
         lin(xn, mm(WR, xe, xt), 1.0)
+        for a, b in held:
+            tt(H(a, b), mm(b - a, [(M("n1"), B(a, b)), (M("mx5" if NAT else "mx"), MS(a, b))]), H(a, b), ALU.min)
+            ops[-1]["rd"].append(xn)
         if last:
             copy(R("yo", 0, HO), R("xi", 0, HO))
-            cp(ind(R("yo", 0, TW), so), xn)
+            ops[cp(ind(R("yo", 0, TW), so), xn)]["boost"] = OPT["boost"][1]
             dma("Y", ("yp", 0, HO), R("yo", 0, HO), [R("yo", 0, HO)], [], 128 * HO * 4)
             for a, b in parts(OPT["cx"][k]):
-                act(R("nq", a, b), H(a, b), ACT.Abs, 0.5, 2.0)
+                act(R("nq", a, b), H(a, b), ACT.Abs, 4.5 if a and NAT else 0.5, 2.0)
+                if OPT["otv"][OPT["cx"][k].index(a)]:
+                    lin(R("dn", a, b), R(dn, a, b) if a else dqn, 1.0, -765.5)
+                    tt(R("ot", a, b), R("dn", a, b), R("nq", a, b), ALU.subtract)
+                    continue
                 terms = [(M("n1"), R("nq", a, b))]
                 if a == 0:
                     terms.append((M("i1"), dqn))
                 if b > WR:
                     terms.append((M("i1"), R(dn, max(a, WR), b), max(a, WR) - a))
                 lin(R("ot", a, b), mm(b - a, terms), 1.0, -765.5)
+            for a, b in parts(OPT["yd"]):
                 dma("Y", ("yt", a, b), R("ot", a, b), [R("ot", a, b)], [], 128 * (b - a) * 2)
         else:
             cp(ind(R("bt", 0, TW), so), bn)
             if k in (1, 2):
-                lin(W("rb", k), W("rn", k), 1.0, BIG)
-                cp(ind(R("rt", 0, TW), so), W("rb", k))
+                if NAT:
+                    cp(ind(R("ri", 0, TW), so), W("rn", k))
+                else:
+                    lin(W("rb", k), W("rn", k), 1.0, BIG)
+                    cp(ind(R("rt", 0, TW), so), W("rb", k))
             cp(ind(R("xi", 0, TW), so), xn)
     return ops
 
@@ -467,45 +556,58 @@ def finish(kind, st, cost, free):
     return st + cost
 
 
-def replay(eng, kind, cost, lat, order, deps, opens=None, last=None):
-    free = {e: 0.0 for e in QUEUES}
-    prev = {e: -1 for e in QUEUES}
-    fin = [0.0] * len(eng)
-    pred = [-1] * len(eng)
-    idle = [(0.0, b, -1) for b in range(8)]
-    wait, banks = {}, {}
-    for i in order:
-        e = eng[i]
-        st = free[e]
-        p = prev[e]
-        for j in deps[i]:
-            x = fin[j] + lat
-            if x > st:
-                st = x
-                p = j
-        if opens:
-            if opens[i]:
-                if not idle:
-                    return None
-                o = min(idle)
-                idle.remove(o)
-                banks[i] = o[1]
-                if o[2] >= 0:
-                    wait[i] = o[2]
-                    if o[0] > st:
-                        st = o[0]
-                        p = o[2]
-        k = kind[i]
-        if k in ISSUE:
-            fin[i] = finish(k, st, cost[i], free)
-            free[e] = st + ISSUE[k]
-        else:
-            fin[i] = free[e] = st + cost[i]
-        if opens and i in last:
-            idle.append((fin[i] + lat, banks[last[i]], i))
-        prev[e] = i
-        pred[i] = p
-    return max(fin), fin, wait, banks, pred
+MARK = 24
+
+
+def replay(eng, kind, cost, lat, order, deps, role, known=None, since=0, wait=None):
+    if known is None or since < MARK:
+        n = len(eng)
+        a, marks = 0, []
+        free, prev = {e: 0.0 for e in QUEUES}, {e: -1 for e in QUEUES}
+        idle = [(0.0, b, -1) for b in range(8)]
+        fin, pred, held, banks = [0.0] * n, [-1] * n, [-1] * n, [-1] * n
+    else:
+        a = since // MARK
+        marks = known[5][:a]
+        free, prev, idle = known[5][a]
+        free, prev, idle = dict(free), dict(prev), list(idle)
+        fin, held, banks, pred = list(known[1]), list(known[2]), list(known[3]), list(known[4])
+        a *= MARK
+    for b in range(a, len(order), MARK):
+        marks.append((dict(free), dict(prev), list(idle)))
+        for i in order[b:b + MARK]:
+            e = eng[i]
+            st = free[e] - lat
+            p = prev[e]
+            for j in deps[i]:
+                if fin[j] > st:
+                    st = fin[j]
+                    p = j
+            r = role[i]
+            if r == -2:
+                if wait is None:
+                    if not idle:
+                        return None
+                    o = min(idle)
+                    idle.remove(o)
+                    banks[i] = o[1]
+                    j = held[i] = o[2]
+                else:
+                    j = wait[i]
+                if j >= 0 and fin[j] > st:
+                    st = fin[j]
+                    p = j
+            st += lat
+            if r == -3:
+                fin[i] = finish(kind[i], st, cost[i], free)
+                free[e] = st + ISSUE[kind[i]]
+            else:
+                fin[i] = free[e] = st + cost[i]
+                if r >= 0 and wait is None:
+                    idle.append((fin[i], banks[r], i))
+            prev[e] = i
+            pred[i] = p
+    return max(fin), fin, held, banks, pred, marks
 
 
 def schedule(eng, kind, opens, cost, deps0, reader, succ, weight, win):
@@ -566,7 +668,7 @@ def schedule(eng, kind, opens, cost, deps0, reader, succ, weight, win):
 
 
 PLAN = {}
-SHARE = (0.5, 0.25, 0.25)
+SHARE = (0.5, 0.15, 0.35)
 
 
 def plan():
@@ -578,7 +680,7 @@ def plan():
         for i, d in enumerate(deps):
             for j in d:
                 succ[j].append(i)
-        state = [12345]
+        state = [OPT["seed"]]
 
         def rnd():
             state[0] = (state[0] * 1103515245 + 12345) % 2147483648
@@ -590,31 +692,36 @@ def plan():
         kind = [o["alt"][0][1] for o in ops]
         cost = [[o["alt"][0][3] for o in s] for s in sets]
         opens = [kind[i] == "mm" and ops[i]["tile"] is None for i in range(n)]
-        best = None
+        starts = []
         for it in range(OPT["tries"]):
             jit = rnd() * 0.8
-            r = schedule(eng, kind, opens, cost[0], deps, reader, succ, [c * (1 + jit * (rnd() - 0.5)) for c in cost[0]],
-                         rnd() * 400.0)
-            if best is None or r[1] < best[1]:
-                best = r
-        order = best[0]
+            weight = [c * (1 + jit * (rnd() - 0.5)) + 8000.0 * o.get("boost", 0.0) for c, o in zip(cost[0], ops)]
+            starts.append(schedule(eng, kind, opens, cost[0], deps, reader, succ, weight, rnd() * 400.0)[::-1])
+        starts.sort()
         dl = [sorted(d) for d in deps]
         hard = [[j for j in dl[i] if not (kind[i] == kind[j] == "mm")] for i in range(n)]
-        last = {reader[i][1]: i for i in reader}
+        above = [set() for _ in ops]
+        for i in range(n):
+            for j in dl[i]:
+                above[i] |= above[j] | {j}
+        lean = [[j for j in hard[i] if not any(j in above[x] for x in hard[i])] for i in range(n)]
+        role = [-2 if opens[i] else -3 if kind[i] in ISSUE else -1 for i in range(n)]
+        for i in reader:
+            role[reader[i][1]] = i
+        load = [0.0]
+        pull = [(i, o["boost"]) for i, o in enumerate(ops) if o.get("boost")]
 
-        def judge(seq):
-            r = replay(eng, kind, cost[0], COSTS[0][4], seq, hard, opens, last)
+        def judge(seq, known=None, since=0):
+            r = replay(eng, kind, cost[0], COSTS[0][4], seq, lean, role, known and known[2], since)
             if r is None:
                 return None
-            dd, score, total = None, [r[0]], r[0]
+            rest, total = [], r[0]
             if whole[0]:
-                dd = list(hard)
-                for i in r[2]:
-                    dd[i] = hard[i] + [r[2][i]]
-                score += [replay(eng, kind, cost[q], COSTS[q][4], seq, dd)[0] for q in range(1, len(COSTS))]
-                total = sum(w * s for w, s in zip(SHARE, score))
-            return (total + OPT["mean"] * sum(r[1]) / n +
-                    OPT["load"] * sum(cost[0][i] for i in range(n) if eng[i] == "V"), score, r, dd)
+                rest = [replay(eng, kind, cost[q], COSTS[q][4], seq, lean, role, known and known[3][q - 1], since, r[2])
+                        for q in range(1, len(COSTS))]
+                total = sum(w * s[0] for w, s in zip(SHARE, [r] + rest))
+            total += sum(w * r[1][i] for i, w in pull)
+            return (total + OPT["mean"] * sum(r[1]) / n + OPT["load"] * load[0], [s[0] for s in [r] + rest], r, rest)
 
         def move(seq, i, j):
             a, b = seq.index(j), seq.index(i)
@@ -639,23 +746,45 @@ def plan():
             return seq[:a] + [x for x in mid if x not in take] + [x for x in mid if x in take] + seq[b + 1:]
 
         def setform(i, f):
+            load[0] -= cost[0][i] if eng[i] == "V" else 0.0
             form[i] = f
             eng[i], kind[i] = ops[i]["alt"][f][0], ops[i]["alt"][f][1]
             for q in range(len(COSTS)):
                 cost[q][i] = sets[q][i]["alt"][f][3]
+            load[0] += cost[0][i] if eng[i] == "V" else 0.0
 
         whole = [False]
-        cur = judge(order)
-        best = (cur, order, list(form))
-        path = None
-        for it in range(OPT["steps"] + 1):
-            if it == int(OPT["steps"] * OPT["part"]):
+        runs, short, long = OPT["runs"], OPT["short"], OPT["steps"]
+        found = []
+        for it in range(runs * short + long + 1):
+            if it <= runs * short and (it % short == 0 if short else it == 0):
+                if it:
+                    found.append((best[0][0], best[1], best[2]))
+                order, shape = (starts[it // short][1], [0] * n) if it < runs * short else min(found or [(0, starts[0][1], [0] * n)])[1:]
+                for i in range(n):
+                    setform(i, shape[i])
+                cur, path = judge(order), None
+                best = (cur, order, list(form))
+            if it == runs * short + int(long * OPT["part"]):
                 whole[0] = True
+                del pull[:]
                 cur = judge(order)
                 best = (cur, order, list(form))
+            heat = OPT["heat"] * (1 - it % short / short) if it < runs * short else OPT["warm"] * (1 - (it - runs * short) / long)
+            if it % OPT["sort"] == 0:
+                lines = {e: [x for x in order if eng[x] == e][::-1] for e in QUEUES}
+                seq, done = [], set()
+                while len(seq) < n:
+                    x = min([w[-1] for w in lines.values() if w and done.issuperset(dl[w[-1]])],
+                            key=lambda y: 0.0 if kind[y] == "send" else cur[2][1][y] - cost[0][y])
+                    seq.append(lines[eng[x]].pop())
+                    done.add(x)
+                c = judge(seq)
+                if c is not None and c[0] <= cur[0] + 100.0:
+                    cur, order, path = c, seq, None
             if path is None:
                 path = []
-                i = max(range(n), key=lambda x: cur[2][1][x])
+                i = cur[2][1].index(cur[2][0])
                 while i >= 0:
                     path.append(i)
                     i = cur[2][4][i]
@@ -685,8 +814,16 @@ def plan():
                     seq = later(order, i, line[p + d]) if p + d < len(line) else None
                 if seq is None or (eng[i] == "Y" and not dl[line[max(p - d, 0)]]):
                     continue
-            c = judge(seq)
-            if c is not None and c[0] <= cur[0] + OPT["heat"] * (1 - it / OPT["steps"]) * rnd():
+            since = order.index(i)
+            if seq is not order:
+                since = 0
+                while since < n and seq[since] == order[since]:
+                    since += MARK
+                since = max(0, since - MARK)
+                if seq[:since] != order[:since]:
+                    since = 0
+            c = judge(seq, cur, since)
+            if c is not None and c[0] <= cur[0] + heat * rnd():
                 cur, order, path = c, seq, None
                 if c[0] < best[0][0]:
                     best = (c, seq, list(form))
@@ -694,7 +831,8 @@ def plan():
                 setform(i, old)
         c, order, form = best
         PLAN["ops"] = ops
-        PLAN["sched"] = (order, c[3], [f - sets[0][i]["alt"][form[i]][3] for i, f in enumerate(c[2][1])], c[2][1], c[2][3])
+        waits = [lean[i] + [c[2][2][i]] if c[2][2][i] >= 0 else lean[i] for i in range(n)]
+        PLAN["sched"] = (order, waits, [f - sets[0][i]["alt"][form[i]][3] for i, f in enumerate(c[2][1])], c[2][1], c[2][3])
         PLAN["score"] = c[1]
         PLAN["form"] = form
         PLAN["pred"] = c[2][4]
@@ -720,12 +858,15 @@ def rank_program(g, core, T, topo):
             return T["ps%d" % banks[r[4]]][:, r[1]:r[2]]
         if len(r) == 3:
             return T[r[0]][:] if T[r[0]].shape[1] == r[2] - r[1] else T[r[0]][:, r[1]:r[2]]
+        if len(r) == 5:
+            return T[r[0]][0:1, r[1]:r[2]]
         if r[3] == 1:
             return T[r[0]][:, r[1]:r[2]]
         return T[r[0]][:, r[1]:r[2]:r[3]]
 
     needed = set(j for d in deps for j in d)
     token = {}
+    knew = {}
     count = {"V": 0, "S": 0, "PE": 0, "G": 0}
     seen = {e: {} for e in Q}
     nd = [0]
@@ -743,9 +884,12 @@ def rank_program(g, core, T, topo):
             s, c = token[j]
             want[s] = max(want.get(s, 0), c)
         for s in sorted(want):
-            if seen[e].get(s, 0) < want[s]:
-                q.wait_ge(T.sem[s], want[s])
-                seen[e][s] = want[s]
+            if not any(knew.get((x, want[x]), {}).get(s, 0) >= want[s] for x in want if x != s):
+                if seen[e].get(s, 0) < want[s]:
+                    q.wait_ge(T.sem[s], want[s])
+        for s in want:
+            for x, c in list(knew.get((s, want[s]), {}).items()) + [(s, want[s])]:
+                seen[e][x] = max(seen[e].get(x, 0), c)
         if kind == "send":
             g.remote_dma(ap(args[1]), ap(args[2]), T.sem["r%d" % args[0]], T.sem.sent, pid, rid, topo.mask(core, nxt))
             sent[0] += len(topo.engines(core, nxt))
@@ -782,6 +926,9 @@ def rank_program(g, core, T, topo):
             w = args[0][2] - args[0][1]
             ins = g.affine_select(T[args[0][0]][args[2]:args[3], args[0][1]:args[0][2]], T[args[1][0]][args[2]:args[3], 0:w],
                                   [[0, w // 64], [-1, 64]], ALU.is_ge, 0.0, args[4], 1)
+        elif kind == "half":
+            ins = g.affine_select(ap(args[0]), ap(args[1]), [[-64 * args[2], 2], [0, 16]], ALU.is_ge, 0.0,
+                                  0 if args[2] > 0 else 63, args[2])
         elif kind == "gcp":
             ins = g.affine_select(ap(args[0]), ap(args[1]), [[0, args[0][2] - args[0][1]]], ALU.is_ge, 0.0, 0, 0)
         elif kind == "pick":
@@ -798,6 +945,7 @@ def rank_program(g, core, T, topo):
             count[e] += 1
             ins.then_inc(T.sem[e], 1)
             token[i] = (e, count[e])
+            knew[token[i]] = dict(seen[e])
     final.update(count)
     for s in sorted(final):
         if final[s] and seen["Y"].get(s, 0) < final[s]:

from concourse.mybir import AluOpType, ActivationFunctionType

ALU = AluOpType
ACT = ActivationFunctionType
P, NT, WR, HO = 2048, 1024, 128, 768
TW = P + 2 * WR
LD = [(0, 512), (512, 1024), (1024, 1536), (1536, 1792), (1792, 2048)]
ZB = NT + WR
BIG = 8388608.0
C3 = [0, 128, 576, 1024]
C2 = [0, 512, 1024]
OPT = dict(cb=[C3] * 6, cm=[C3] * 6, cr=[C3] * 6, cz=[C3] * 6, cx=[C3] * 6, cw=[[0, 128, 1024]] * 6,
           zm=(1,) * 6, zv=[(0, 0, 0)] * 6, gcp=1, split=(1, 1, 1, 0, 0, 1), bne=1, dfirst=1, late="dl",
           boost=(0.0, 0.0), hold=0, scan=0, otv=(0, 0, 1), dfv=(0, 0, 1, 2, 2, 2), sou=1, sig=0,
           ld=[0, 1024, 1792, 2048], flat=1, sends=[0, 128, 256, 704, 1152], yd=[0, 576, 1024],
           bx=(0,) * 6, rx=0, pe=(25.0, 5.0), de=(0,) * 6, join=(1,) * 6,
           tries=40, steps=480000, heat=300.0, crit=0.7, flip=0.05, mean=0.5, load=0.2, part=0.93, sort=200, seed=2,
           runs=0, short=0, warm=300.0)

BF, F32, F16, I32, U16 = "bfloat16", "float32", "float16", "int32", "uint16"
WB = ["df", "x", "un", "ep", "ad", "dw", "bn", "bg", "tw"]
WF = ["xn", "rb"]
WH = ["rn", "dl", "y", "zz", "sc", "sf", "ofw", "zm"]
MB = ["i1", "n1", "n2", "i2", "i3", "i64", "n64", "bo", "nbo", "bo64", "bos", "bo2", "l2", "mxw", "nmxw", "l8", "mx5", "mx", "nmx", "m4",
      "g2", "mz", "bo3", "u3", "wm"]
SCRATCH = {
    "xi": ("sbuf", [128, TW], I32), "bt": ("sbuf", [128, TW], I32), "rt": ("sbuf", [128, TW], F32),
    "ri": ("sbuf", [128, TW], I32), "nt": ("sbuf", [128, 2 * NT], BF),
    "yo": ("sbuf", [128, TW], F32),
    "tv": ("sbuf", [128, NT], BF), "da": ("sbuf", [128, NT], BF), "dbb": ("sbuf", [128, NT], BF),
    "sb": ("sbuf", [128, NT + WR], BF), "lb": ("sbuf", [128, NT + WR], BF),
    "nb": ("sbuf", [128, 2 * NT], BF), "nm": ("sbuf", [128, 2 * NT], BF), "nr": ("sbuf", [128, 2 * NT], F16),
    "nz": ("sbuf", [128, 7 * ZB], F16), "nq": ("sbuf", [128, NT], BF), "ot": ("sbuf", [128, NT], BF),
    "eq": ("sbuf", [128, 2 * 768], BF), "off": ("sbuf", [128, 7 * 72], U16),
    "ci": ("sbuf", [128, 128], I32), "cj": ("sbuf", [128, 128], I32),
    "wi": ("sbuf", [128, 256], I32), "wj": ("sbuf", [128, 256], I32),
    "w_e4": ("sbuf", [128, 6 * WR], I32), "w_b3": ("sbuf", [128, 6 * WR], I32),
    "w_c": ("sbuf", [128, 12 * WR], BF), "w_s": ("sbuf", [128, 12 * WR], BF),
    "wt": ("sbuf", [128, 4], I32), "tht": ("sbuf", [128, 4], I32), "pi": ("sbuf", [128, 8], I32),
    "col": ("sbuf", [128, 24], F32), "row": ("sbuf", [128, 256], I32), "rowb": ("sbuf", [128, 256], BF),
    "c144": ("sbuf", [128, 144], BF), "cg": ("sbuf", [128, 240], BF), "cs": ("sbuf", [128, 512], BF),
    "sel": ("sbuf", [128, NT], BF), "nsel": ("sbuf", [128, 512], BF), "cmp": ("sbuf", [128, 768], BF),
    "cv": ("sbuf", [128, 512], BF), "seg": ("sbuf", [128, 128], BF), "diag": ("sbuf", [128, 128], BF),
    "j16": ("sbuf", [128, 128], BF), "six": ("sbuf", [128, 128], BF),
    "dgb": ("sbuf", [128, 144], BF), "dgw": ("sbuf", [128, 144], BF),
    "k2": ("sbuf", [128, 64], BF), "npair": ("sbuf", [128, 256], BF), "n768": ("sbuf", [128, 128], BF),
    "dum": ("sbuf", [128, 128], F16), "dn": ("sbuf", [128, NT], BF),
}
for _n in WB:
    SCRATCH["w_" + _n] = ("sbuf", [128, 6 * WR], BF)
for _n in WF:
    SCRATCH["w_" + _n] = ("sbuf", [128, 6 * WR], F32)
for _n in WH:
    SCRATCH["w_" + _n] = ("sbuf", [128, 6 * WR], F16)
for _n in MB:
    SCRATCH["m_" + _n] = ("sbuf", [128, 128], BF)
for _n in range(8):
    SCRATCH["ps%d" % _n] = ("psum", [128, 512], F32)
NDMA = 16
SEMAPHORES = ["V", "S", "PE", "G", "sent"] + ["d%d" % i for i in range(NDMA)] + ["r%d" % i for i in range(5)]

COSTS = [(0.84, 0.42, 1.56, 3.8, 150.0, 280.0, 90.0, 1500.0, 15.0, 25.0),
         (0.9, 0.45, 1.1, 1.8, 80.0, 200.0, 60.0, 2000.0, 40.0, 60.0),
         (1.2, 0.6, 2.0, 5.5, 150.0, 350.0, 120.0, 1300.0, 20.0, 20.0)]


def R(name, a, b, step=1):
    return (name, a, b, step)


def build(costs):
    ops = []
    now = [0]
    CYC, PECYC, GA, SC, _, DMA, RDMA, FIX, ROW, RROW = costs

    def width(r):
        return len(range(r[1], r[2], r[3]))

    def two(r):
        return r[0] != "ps" and SCRATCH[r[0]][2] in (BF, F16, U16)

    def base(r):
        return [r[1], r[2]] if r[0] == "ind" else [r]

    def add(*forms):
        rd = []
        for f in forms:
            rd += [r for r in f[3] if isinstance(r, tuple) and r[0] != "ps" and r not in rd]
        ops.append(dict(alt=[(f[0], f[1], f[2], f[5]) for f in forms], rd=rd, wr=forms[0][4], tile=forms[0][6]))
        return len(ops) - 1

    def vcost(out, ins):
        if out[0] == "ind":
            return 50 + width(ins[0]) * SC * CYC
        n = width(out)
        if ins[0][0] == "ind":
            return 50 + n * GA * CYC
        k = 0.5 if all(two(r) for r in [out] + ins) else 1.0
        if len(ins) == 2 and all(r[0] != "ps" for r in ins):
            k *= 2
        return max(64, n * k) * CYC + 30

    def vop(kind, out, ins, extra, cols=()):
        rd = [x for r in ins for x in base(r)] + list(cols)
        wr = [out]
        if out[0] == "ind":
            wr = [out[1]]
            rd = rd + [out[2]]
        tile = [r[4] for r in ins if r[0] == "ps"]
        return ("V", kind, (out, ins, extra), rd, wr, vcost(out, ins), tile[0] if tile else None)

    def fts(out, a, s1, op0, s2=None, op1=None):
        return vop("ts", out, [a], (s1, s2, op0, op1), [s for s in (s1, s2) if isinstance(s, tuple)])

    def fact(out, a, f, bias=0.0, scale=1.0):
        n = width(out)
        c = 65 + n * GA * CYC if a[0] == "ind" else 60 + max(64, n) * CYC
        return ("S", "act", (out, a, f, bias, scale), base(a) + [bias, scale], [out], c, a[4] if a[0] == "ps" else None)

    def ts(*a):
        return add(fts(*a))

    def tt(out, a, b, op):
        return add(vop("tt", out, [a, b], op))

    def cp(out, a):
        if OPT["sou"] and out[0] != "ind" and a[0] == "ps":
            return add(vop("cp", out, [a], None), fact(out, a, ACT.Identity))
        return add(vop("cp", out, [a], None))

    def ms(out, v):
        return add(("V", "ms", (out, v), [], [out], max(64, width(out) / 2) * CYC + 30, None))

    def act(*a):
        return add(fact(*a))

    def lin(out, a, scale, bias=0.0):
        return add(fact(out, a, ACT.Identity, bias, scale), fts(out, a, scale, ALU.mult, bias, ALU.add))

    def relu(out, a, bias):
        return add(fact(out, a, ACT.Relu, bias), fts(out, a, bias, ALU.add, 0.0, ALU.max))

    def step(out, a, level, bias, scale, vector=False):
        f = [fact(out, a, ACT.Sigmoid, bias, scale), fts(out, a, level, ALU.is_ge)]
        f[0][3].append(col(7))
        return add(*(f[::-1] if vector else f))

    def mm(n, *groups):
        if not OPT["split"][now[0]]:
            groups = [[t for gr in groups for t in gr]]
        groups = [gr for gr in groups if gr]
        first = None
        for q, terms in enumerate(groups):
            c = OPT["pe"][0]
            rd = []
            for t in terms:
                c += max(64, width(t[1])) * PECYC + OPT["pe"][1]
                rd += [t[0], t[1]]
            i = add(("PE", "mm", (n, terms, first, q == len(groups) - 1), rd, [], c, first))
            first = i if first is None else first
        return ("ps", 0, n, 1, first)

    def dma(q, out, src, rd, wr, nbytes, rows=8):
        return add((q, "dma", (out, src), rd, wr, FIX + rows * ROW + nbytes / DMA, None))

    def send(k, out, src):
        i = add(("G", "send", (k, out, src), [src], [], 16 * RROW + width(src) * 256 / RDMA, None))
        j = add(("X", "recv", (k,), [], [out], 0.0, None))
        ops[j]["after"] = i

    def ind(win, offs):
        return ("ind", win, offs)

    def M(n):
        return R("m_" + n, 0, 128)

    def W(n, k):
        return R("w_" + n, k * WR, (k + 1) * WR)

    def col(i):
        return R("col", i, i + 1)

    def iota(out, pat, b, cm):
        add(("G", "iota", (out, pat, b, cm), [], [out], 130 + 2 * width(out) * CYC, None))

    def fpick(out, a, sign, op, fill):
        return ("G", "pick", (out, a, sign, op, fill), [a], [out], 170 + 2 * width(out) * CYC, None)

    def pick(*a):
        add(fpick(*a))

    def wrap(mat, plane, a, b, more=()):
        return mm((b - a) // 16, [(R(mat, 15 - i, 143 - i), R(plane, a + i, b, 16)) for i in range(16)] + list(more))

    def Z(k, a, b):
        return R("nz", k * ZB + a, k * ZB + b)

    def OF(k, a, b):
        return R("off", k * 72 + 8 + a // 16, k * 72 + 8 + b // 16)

    def offsets(k, a, b):
        cp(OF(k, a, b), wrap("dgb", "nz", k * ZB + a, k * ZB + b))

    def fold(out, plane, tmp):
        add(("V", "scan", (tmp, [R("seg", 0, 128), plane], (0.0, ALU.mult, ALU.add)), [R("seg", 0, 128), plane], [tmp],
             64 * CYC + 30, None))
        cp(out, R(tmp[0], tmp[1] + 15, tmp[2], 16))

    def copy(out, a):
        f = [fact(out, a, ACT.Identity), vop("cp", out, [a], None)]
        if OPT["gcp"]:
            f.insert(0, ("G", "gcp", (out, a), [a], [out], 170 + 2 * width(out) * CYC, None))
        return add(*f)

    def parts(c):
        return list(zip(c[:-1], c[1:]))

    dma("Y", R("tv", 0, NT), ("trav", 0, NT), [], [R("tv", 0, NT)], 128 * NT * 2)
    LD = parts(OPT["ld"])
    flat = OPT["flat"]
    if flat:
        dma("S", ("row", 0, 128, 1, "one"), ("wts", 0, 1), [], [R("row", 0, 128)], 512, 1)
        dma("S", ("row", 128, 256, 1, "one"), ("th", 0, 1), [], [R("row", 128, 256)], 512, 1)
    else:
        dma("S", R("wt", 0, 1), ("wts", 0, 1), [], [R("wt", 0, 4)], 512)
        dma("S", R("tht", 0, 1), ("th", 0, 1), [], [R("tht", 0, 4)], 512)
    for q, (a, b) in enumerate(LD):
        dma("Y", R("xi", a, b), ("peers", a, b), [], [R("xi", a, b)], 512 * b + 128 * NT * 2, 8 * q + (16 if flat else 32))
    PC, GC, LC, PR, WC, TH, TB, L15, BZ, N15, HI, BT, EV = range(13)
    iota(R("pi", 0, 1), [[0, 1]], 0, 1)
    iota(R("c144", 0, 144), [[1, 144]], 0, 0)
    iota(R("cg", 0, 128), [[16, 8], [0, 16]], 0, 0)
    iota(R("cs", 0, 512), [[16, 8], [0, 64]], 0, 0)
    iota(R("j16", 0, 128), [[0, 8], [1, 16]], 0, 0)
    c128 = R("c144", 0, 128)
    cg = R("cg", 0, 128)
    iota(R("col", PC, PC + 1), [[0, 1]], 0, 1)
    iota(R("col", N15, N15 + 1), [[0, 1]], P, 2)
    ts(R("pi", 1, 2), R("pi", 0, 1), 112, ALU.bitwise_and)
    cp(col(GC), R("pi", 1, 2))
    act(col(LC), col(GC), ACT.Identity, col(PC), -1.0)
    if OPT["sig"]:
        f = fact(col(L15), col(LC), ACT.Sigmoid, -3712.0, 256.0)
        add(f[:5] + (f[5] + 1300.0,) + f[6:])
        lin(col(BZ), col(L15), 4096.0, -4096.0)
    else:
        ts(col(BZ), col(LC), 14.5, ALU.is_lt, -4096.0, ALU.mult)
    NAT = any(any(z) for z in OPT["zv"])
    RB = 0.0 if NAT else BIG
    ts(M("i1"), c128, col(PC), ALU.is_equal)
    ts(M("bo"), cg, col(GC), ALU.is_equal)
    for n, v in (("n1", -1.0), ("n2", -2.0), ("i64", 64.0)):
        add(fpick(M(n), M("i1"), 1, ALU.not_equal, v), fact(M(n), M("i1"), ACT.Identity, 0.0, v), fts(M(n), M("i1"), v, ALU.mult))
    for n, v in (("bo2", 2.0), ("nbo", -1.0), ("bo64", 384.0), ("bos", 1.0 / 8192), ("bo3", 64.0)):
        lin(M(n), M("bo"), v)
    ts(R("diag", 0, 128), R("j16", 0, 128), col(LC), ALU.is_equal)
    if OPT["scan"]:
        ts(R("seg", 0, 128), R("j16", 0, 128), 0.5, ALU.is_ge)
    lin(R("dum", 0, 128), R("diag", 0, 128), col(N15))
    pick(M("l2"), M("bo2"), 1, ALU.is_gt, 0.0)
    pick(M("mx"), M("l2"), 1, ALU.not_equal, -1.0)
    lin(M("nmx"), M("mx"), -1.0)
    lin(M("mz"), M("mx"), col(BZ))
    if NAT:
        lin(col(BT), col(BZ), 4.0, 16384.0)
        lin(M("l8"), M("l2"), 4.0)
        pick(M("mx5"), M("l8"), 1, ALU.not_equal, -5.0)
    pick(M("mxw"), M("l2"), 1, ALU.not_equal, -2.0)
    pick(M("nmxw"), M("nmx"), 1, ALU.not_equal, 2.0)
    pick(M("m4"), M("nmx"), 1, ALU.not_equal, 3.5)
    pick(M("u3"), M("bo3"), -1, ALU.is_gt, 0.0)
    ts(R("dgb", 0, 144), R("c144", 0, 144), col(GC), ALU.subtract, 15.0, ALU.is_equal)
    ts(R("nsel", 0, 512), R("cs", 0, 512), col(GC), ALU.is_equal, -1.0, ALU.mult)
    for h in range(2):
        lin(R("sel", h, NT, 2), R("nsel", 0, 512), -1.0)
    if any(OPT["zm"]):
        ts(R("pi", 2, 3), R("pi", 0, 1), 16, ALU.bitwise_and)
        lin(col(EV + 1), R("pi", 2, 3), 1.0 / 16)
        lin(col(EV), col(EV + 1), -1.0, 1.0)
        ts(R("pi", 3, 4), R("pi", 0, 1), 5, ALU.logical_shift_right)
        lin(col(PR), R("pi", 3, 4), 16.0)
        ts(R("npair", 0, 256), R("cs", 0, 256), col(PR), ALU.is_equal, -1.0, ALU.mult)
    ms(R("cv", 0, 32), 4096.0)
    iota(R("col", TH, TH + 1), [[0, 1]], -64, 1)
    ts(R("pi", 4, 5), R("pi", 0, 1), 63, ALU.bitwise_and)
    cp(col(HI), R("pi", 4, 5))
    for a, b, c in ((0, 512, TH), (512, 768, HI)):
        ts(R("cmp", a, a + 64), R("c144", 0, 64), col(c), ALU.is_le, 4096.0, ALU.mult)
        w = 64
        while w < b - a:
            copy(R("cmp", a + w, a + 2 * w), R("cmp", a, a + w))
            w *= 2
    for out, a, sign in ((R("k2", 32, 64), R("cv", 0, 32), 1), (R("k2", 0, 32), R("k2", 32, 64), -1)):
        add(("G", "half", (out, a, sign), [a], [out], 170 + 64 * CYC, None))
    ms(R("n768", 0, 128), -768.0)
    if min(OPT["dfv"]) < 2:
        ms(R("six", 0, 128), 6144.0)
    wt, tht = R("wt", 0, 1), R("tht", 0, 1)
    if flat:
        add(("V", "cp", (("rowb", 0, 256, 1, "one"), [("row", 0, 256, 1, "one")], None), [R("row", 0, 256)],
             [R("rowb", 0, 256)], 256 * CYC + 30, None))
        p = mm(2, [(("rowb", 128 * h, 128 * h + 128, 1, "one"), ("m_i1", 0, 1, 1, "one"), h) for h in range(2)])
        wt, tht = ("ps", 0, 1, 1, p[4]), ("ps", 1, 2, 1, p[4])
    lin(col(WC), wt, 0.25)
    lin(R("dgw", 0, 144), R("dgb", 0, 144), col(WC))
    lin(M("wm"), M("bo"), col(WC))
    lin(col(TB), tht, -1.0 / 2048, 1.0 / 4096 - 4.0)
    lin(R("da", 0, NT), R("tv", 0, NT), 1.0, 767.0)
    send(0, R("dbb", WR, NT), R("da", WR, NT))
    for a, b in parts(C3):
        t = mm(b - a, [(M("i1"), R("tv", a, b)), (M("n1"), R("da", a, b))])
        act(R("nq", a, b), t, ACT.Abs, 1533.5, 2.0)
        lin(R("sb", WR + a, WR + b), R("nq", a, b), 1.0, -3.5 if a and NAT else -1.5)
    for q, (a, b) in enumerate(LD):
        ts(R("bt", a, b), R("xi", a, b), 3, ALU.bitwise_and)
        if NAT:
            ts(R("ri", a, b), R("xi", a, b), 6, ALU.logical_shift_right)
        else:
            lin(R("rt", a, b), R("xi", a, b), (1.0 + 2.0 ** -18) / 64, BIG - 0.5)
    gB, gR, gX = R("bt", 0, P), R("ri" if NAT else "rt", 0, P), R("xi", 0, P)

    for k in range(6):
        v, t = divmod(k, 3)
        now[0] = k
        hb, dn = ("sb", "da") if v == 0 else ("lb", "dbb")
        last = k == 5
        pl = (k % 2) * NT

        def H(a, b):
            return R(hb, WR + a, WR + b)

        def B(a, b):
            return R("nb", pl + a, pl + b)

        def MS(a, b):
            return R("nm", pl + a, pl + b)

        def RG(a, b):
            return R("nr", pl + a, pl + b)

        ow = OF(k, 0, WR)
        so = OF(k + 1, -WR, 0)
        dq = (R("da", 0, WR) if v == 0 else R("lb", 0, WR)) if t == 0 else W("dw", k - 1)
        dqn = W("dw", k) if k != 2 else R("sb", 0, WR)
        zw = Z(k, 0, WR)
        if t == 0:
            for src, a, b in ([(R("da", 0, NT), 0, NT)] if v == 0 else [(R(dn, WR, NT), WR, NT)]):
                n, c0 = (b - a) // 16, v * 64 + a // 16
                p = wrap("dgw", src[0], src[1], src[2], [(M("wm"), R("n768", 0, n))])
                if v and OPT["late"]:
                    ops[p[4]]["rd"].append(W(OPT["late"], 2))
                cp(R("ci", c0, c0 + n), p)
                ts(R("cj", c0, c0 + n), R("ci", c0, c0 + n), P - 1, ALU.bitwise_and)
                cp(OF(k, a, b), R("cj", c0, c0 + n))
            c0 = v * 128
            p = mm(WR, [(M("wm"), R("n768", 0, 128)), (M("wm"), dq)])
            cp(R("wi", c0, c0 + WR), p)
            ts(R("wj", c0, c0 + WR), R("wi", c0, c0 + WR), P - 1, ALU.bitwise_and)
            if v and OPT["scan"]:
                tt(zw, R("wj", c0, c0 + WR), R("diag", 0, 128), ALU.mult)
                fold(ow, zw, W("sf", k))
            else:
                lin(zw, R("wj", c0, c0 + WR), 1.0 / 16)
                if v:
                    tt(W("sf", k), mm(WR, [(zw, M("bo"))]), R("diag", 0, 128), ALU.mult)
                    cp(ow, mm(8, [(W("sf", k), R("m_bo", 0, 128, 16))]))
        eb = (k % 2) * 768
        for hf in range(2):
            if hf == 0:
                e0, n = 0, 512
                terms = [(zw, R("nsel", 0, 512))]
                terms += [(R("sel", q * 128, q * 128 + 128), Z(k, 64, 128), q * 64) for q in range(8)]
            else:
                e0, n = 512, 256
                terms = [(R("sel", q * 256 + 64, q * 256 + 192), Z(k, 0, 64), q * 64) for q in range(4)]
                if OPT["zm"][k]:
                    for h in range(2):
                        lin(R("w_zm", k * WR + 64 * h, k * WR + 64 * h + 64), Z(k, 0, 64), col(EV + h))
                    terms.insert(0, (W("zm", k), R("npair", 0, 256)))
                else:
                    terms[1:1] = [(Z(k, 0, 64), R("nsel", q * 64, q * 64 + 64), q // 2 * 64, q % 2 * 64) for q in range(8)]
            tt(R("eq", eb + e0, eb + e0 + n), mm(n, terms), R("cmp", e0, e0 + n), ALU.is_equal)
        lo = [(R("eq", eb + 512 + q * 64, eb + 576 + q * 64), R("k2", 0, 32), 32 * q, 0) for q in range(4)]
        hi = [(R("eq", eb + q * 64, eb + q * 64 + 64), R("cv", 0, 16), 16 * q, 64) for q in range(8)]
        ofw, tw = W("ofw", k), W("tw", k)
        p = mm(WR, [(zw, R("m_bo", 0, 64))] + lo + hi + [(zw, R("m_bo", 64, 128), 64)])
        relu(tw, p, -2048.0)
        tt(ofw, p, R("dum", 0, 128), ALU.min)
        join = t < 2 and OPT["join"][k] and OPT["cw"][k][1] == WR
        if not join:
            cp(so, mm(8, [(ofw, R("m_bo", 0, 128, 16))]))
        if OPT["bx"][k]:
            ts(W("b3", k), ind(gX, ow), 3, ALU.bitwise_and)
            lin(B(0, WR), W("b3", k), 1.0, -2.0)
            copy(W("bg", k), W("b3", k))
        for a, b in parts(OPT["cb"][k])[OPT["bx"][k]:]:
            lin(B(a, b), ind(gB, OF(k, a, b)), 1.0, -4.0 if a and NAT else -2.0)
        for a, b in parts(OPT["cm"][k]):
            tt(MS(a, b), B(a, b), H(a, b), ALU.not_equal)
        rw = RG(0, WR)
        shared = {}
        if t < 2:
            for q, (a, b) in enumerate(parts(OPT["cz"][k])):
                if OPT["zv"][k][q]:
                    shared[a] = mm(b - a, [(M("n1"), B(a, b)), (M("mx5"), MS(a, b))])
                    act(R("nt", pl + a, pl + b), shared[a], ACT.Relu, col(BT), -4096.0)
                    tt(Z(k + 1, a, b), ind(gR, OF(k, a, b)), R("nt", pl + a, pl + b), ALU.min)
                else:
                    relu(RG(a, b), ind(gR, OF(k, a, b)), -RB)
                    relu(Z(k + 1, a, b), mm(b - a, [(M("i1"), RG(a, b)), (M("mz"), MS(a, b))]), col(BZ))
            for a, b in parts(OPT["cw"][k]):
                if b == WR:
                    tt(W("sc", k), mm(WR, [(Z(k + 1, 0, WR), M("bo"))]), R("diag", 0, 128), ALU.mult)
                    if join:
                        cp(OF(k + 1, -WR, WR), mm(16, [(ofw, R("m_bo", 0, 128, 16)), (W("sc", k), R("m_bo", 0, 128, 16), 8)]))
                    else:
                        cp(OF(k + 1, 0, WR), mm(8, [(W("sc", k), R("m_bo", 0, 128, 16))]))
                else:
                    offsets(k + 1, a, b)
        elif not last and not OPT["rx"]:
            relu(rw, ind(gR, ow), -RB)
        else:
            lin(W("rb", k), ind(gX, ow), (1.0 + 2.0 ** -18) / 64, BIG - 0.5)
            relu(rw, W("rb", k), -BIG)
        A, bw, mis, un, ep, ad, bn = H(0, WR), B(0, WR), MS(0, WR), W("un", k), W("ep", k), W("ad", k), W("bn", k)
        c1, c4 = R("w_c", 2 * k * WR, (2 * k + 1) * WR), R("w_c", (2 * k + 1) * WR, (2 * k + 2) * WR)
        ts(W("e4", k), ind(gX, ow), 60, ALU.bitwise_and)
        copy(ep, W("e4", k))
        if OPT["dfv"][k]:
            tt(W("df", k), W("e4", k) if OPT["de"][k] else ep, dq, ALU.subtract)
            act(ad, W("df", k), ACT.Abs, 768.0)
        else:
            act(ad, mm(WR, [(M("n1"), dq), (M("i1"), ep)]), ACT.Abs, 768.0)
        add(fact(un, A, ACT.Relu, 0.0, 1.0 if t else 4.0), fts(un, A, 0.0, ALU.max, 1.0 if t else 4.0, ALU.mult))
        if not OPT["bx"][k]:
            lin(W("bg", k), bw, 1.0, 2.0)
        if t > 0:
            relu(c4, mm(WR, [(M("n2"), un), (M("i1"), bw), (M("m4"), mis)], [(tw, M("n2"))] if t == 1 else []), -2.0)
        act(c1, mm(WR, [(M("i1"), A), (M("n1"), bw), (M("nmx"), mis)], [(tw, M("n2")), (M("bos"), ad)]),
            ACT.Sign, col(TB))
        if OPT["dfv"][k] == 2:
            relu(W("x", k), mm(WR, [(M("i1"), W("df", k))], [(M("bo64"), c1)]), 6144.0)
            i = tt(dqn, dq, W("x", k), ALU.add)
        else:
            i = tt(dqn, mm(WR, [(M("i1"), ep), (M("i1"), R("six", 0, WR))], [(M("bo64"), c1)]), dq, ALU.max)
        ops[i]["boost"] = OPT["boost"][0] if k == 2 else 0.0
        if OPT["bne"]:
            tt(bn, mm(WR, [(M("nmxw"), mis), (M("n1"), A)], [(M("i1"), c1)]), W("bg", k), ALU.max)
        held = parts(OPT["cx"][k])[-OPT["hold"]:] if last and OPT["hold"] else []
        for a, b in parts(OPT["cx"][k]):
            if (a, b) in held:
                continue
            terms = [(M("n1"), B(a, b)), (M(("mx5" if NAT else "mx") if a else "mxw"), MS(a, b))]
            tt(H(a, b), shared.get(a) or mm(b - a, terms, [] if a else [(M("n1"), c1)]), H(a, b), ALU.min)
        if k == 2:
            for q, (a, b) in enumerate(parts(OPT["sends"])):
                send(1 + q, R("lb", a, b), R("sb", a, b))
        if not OPT["bne"]:
            tt(bn, mm(WR, [(M("nmx"), mis)], [(M("n1"), A)]), W("bg", k), ALU.max)
        xe = [(M("i64"), rw), (M("i1"), ep), (M("i1"), dq)]
        xt = [(M("n1"), dqn), (M("i1"), bn)]
        if OPT["dfv"][k] == 2:
            xe, xt = xe[:2], [(M("n1"), W("x", k)), (M("i1"), bn)]
        if t > 0:
            sl, sw, dl = R("w_s", 2 * k * WR, (2 * k + 1) * WR), R("w_s", (2 * k + 1) * WR, (2 * k + 2) * WR), W("dl", k)
            un0, z0 = W("un", k - t), Z(k - t, 0, WR)
            terms = [(M("nmx"), mis), (M("n1"), un), (M("n1"), W("bg", k)), (M("i64"), un0)]
            late = [(M("u3"), c4)]
            if t == 1:
                terms.append((M("i64"), un0, WR))
                late.append((M("u3"), c4, WR))
            n = 2 * WR if t == 1 else WR
            if OPT["sig"]:
                step(R("w_s", sl[1], sl[1] + n), mm(n, terms, late), 256.5, -65664.0, 256.0)
            else:
                ts(R("w_s", sl[1], sl[1] + n), mm(n, terms, late), 256.5, ALU.is_ge)
            u = mm(WR, [(M("n1"), rw), (M("bo"), z0)] +
                   ([] if t == 1 else [(M("n1"), W("y", k - 1)), (M("i1"), W("zz", k - 1))]))
            tt(dl, u, sl, ALU.mult)
            if t == 1:
                tt(W("y", k), u, sw, ALU.mult)
                tt(W("zz", k), mm(WR, [(M("bo"), zw), (M("nbo"), z0)]), un, ALU.mult)
            if k in (1, 2):
                tt(W("rn", k), rw, dl, ALU.add)
                xe, xt = xe[1:], xt + [(M("i64"), W("rn", k))]
            else:
                xt.append((M("i64"), dl))
        xn = W("xn", k)
        lin(xn, mm(WR, xe, xt), 1.0)
        for a, b in held:
            tt(H(a, b), mm(b - a, [(M("n1"), B(a, b)), (M("mx5" if NAT else "mx"), MS(a, b))]), H(a, b), ALU.min)
            ops[-1]["rd"].append(xn)
        if last:
            copy(R("yo", 0, HO), R("xi", 0, HO))
            ops[cp(ind(R("yo", 0, TW), so), xn)]["boost"] = OPT["boost"][1]
            dma("Y", ("yp", 0, HO), R("yo", 0, HO), [R("yo", 0, HO)], [], 128 * HO * 4)
            for a, b in parts(OPT["cx"][k]):
                act(R("nq", a, b), H(a, b), ACT.Abs, 4.5 if a and NAT else 0.5, 2.0)
                if OPT["otv"][OPT["cx"][k].index(a)]:
                    lin(R("dn", a, b), R(dn, a, b) if a else dqn, 1.0, -765.5)
                    tt(R("ot", a, b), R("dn", a, b), R("nq", a, b), ALU.subtract)
                    continue
                terms = [(M("n1"), R("nq", a, b))]
                if a == 0:
                    terms.append((M("i1"), dqn))
                if b > WR:
                    terms.append((M("i1"), R(dn, max(a, WR), b), max(a, WR) - a))
                lin(R("ot", a, b), mm(b - a, terms), 1.0, -765.5)
            for a, b in parts(OPT["yd"]):
                dma("Y", ("yt", a, b), R("ot", a, b), [R("ot", a, b)], [], 128 * (b - a) * 2)
        else:
            cp(ind(R("bt", 0, TW), so), bn)
            if k in (1, 2):
                if NAT:
                    cp(ind(R("ri", 0, TW), so), W("rn", k))
                else:
                    lin(W("rb", k), W("rn", k), 1.0, BIG)
                    cp(ind(R("rt", 0, TW), so), W("rb", k))
            cp(ind(R("xi", 0, TW), so), xn)
    return ops


def depend(ops):
    hist = {}
    deps = [set() for _ in ops]
    reader = {}
    for i, op in enumerate(ops):
        for isw, regs in ((False, op["rd"]), (True, op["wr"])):
            for r in regs:
                for (j, w, a, b) in hist.get(r[0], []):
                    if j != i and (w or isw) and a < r[2] and r[1] < b:
                        deps[i].add(j)
        for isw, regs in ((False, op["rd"]), (True, op["wr"])):
            for r in regs:
                hl = hist.setdefault(r[0], [])
                if isw:
                    hl[:] = [e for e in hl if not (r[1] <= e[2] and e[3] <= r[2])]
                hl.append((i, isw, r[1], r[2]))
        if op["tile"] is not None:
            deps[i].add(reader[op["tile"]][1] if op["tile"] in reader else op["tile"])
            first = reader.get(op["tile"], (None, i))[0]
            reader[op["tile"]] = (i if first is None and op["alt"][0][1] != "mm" else first, i)
        if "after" in op:
            deps[i].add(op["after"])
    return deps, reader


ISSUE = {"dma": 60.0, "send": 300.0, "recv": 0.0}
QUEUES = ("V", "S", "PE", "G", "Y", "X", "link")


def finish(kind, st, cost, free):
    if kind == "send":
        free["link"] = max(free["link"], st + 1200.0) + cost
        return free["link"] + 800.0
    return st + cost


MARK = 24


def replay(eng, kind, cost, lat, order, deps, role, known=None, since=0, wait=None):
    if known is None or since < MARK:
        n = len(eng)
        a, marks = 0, []
        free, prev = {e: 0.0 for e in QUEUES}, {e: -1 for e in QUEUES}
        idle = [(0.0, b, -1) for b in range(8)]
        fin, pred, held, banks = [0.0] * n, [-1] * n, [-1] * n, [-1] * n
    else:
        a = since // MARK
        marks = known[5][:a]
        free, prev, idle = known[5][a]
        free, prev, idle = dict(free), dict(prev), list(idle)
        fin, held, banks, pred = list(known[1]), list(known[2]), list(known[3]), list(known[4])
        a *= MARK
    for b in range(a, len(order), MARK):
        marks.append((dict(free), dict(prev), list(idle)))
        for i in order[b:b + MARK]:
            e = eng[i]
            st = free[e] - lat
            p = prev[e]
            for j in deps[i]:
                if fin[j] > st:
                    st = fin[j]
                    p = j
            r = role[i]
            if r == -2:
                if wait is None:
                    if not idle:
                        return None
                    o = min(idle)
                    idle.remove(o)
                    banks[i] = o[1]
                    j = held[i] = o[2]
                else:
                    j = wait[i]
                if j >= 0 and fin[j] > st:
                    st = fin[j]
                    p = j
            st += lat
            if r == -3:
                fin[i] = finish(kind[i], st, cost[i], free)
                free[e] = st + ISSUE[kind[i]]
            else:
                fin[i] = free[e] = st + cost[i]
                if r >= 0 and wait is None:
                    idle.append((fin[i], banks[r], i))
            prev[e] = i
            pred[i] = p
    return max(fin), fin, held, banks, pred, marks


def schedule(eng, kind, opens, cost, deps0, reader, succ, weight, win):
    n = len(eng)
    LAT = COSTS[0][4]
    deps = list(deps0)
    prio = [0.0] * n
    for i in range(n - 1, -1, -1):
        m = 0.0
        for j in succ[i]:
            if prio[j] + LAT > m:
                m = prio[j] + LAT
        prio[i] = weight[i] + m
    free = {e: 0.0 for e in QUEUES}
    fin = [None] * n
    bank_tile = [None] * 8
    left = [len(d) for d in deps]
    ready = [i for i in range(n) if left[i] == 0]
    rt = [0.0] * n
    order = []
    while ready:
        cand = []
        best = None
        for b in range(8):
            pt = bank_tile[b]
            if pt is None:
                o = (0.0, b)
            elif fin[reader[pt][1]] is not None:
                o = (fin[reader[pt][1]] + LAT, b)
            else:
                continue
            if best is None or o < best:
                best = o
        for i in ready:
            st = max(free[eng[i]], rt[i])
            if opens[i]:
                if best is None or left[reader[i][0]] > 1 or any(left[j] > 1 for j in succ[i] if kind[j] == "mm"):
                    continue
                st = max(st, best[0])
            cand.append((st, i))
        first = min(cand)
        e = eng[first[1]]
        st, i = max([c for c in cand if eng[c[1]] == e and c[0] <= first[0] + win],
                    key=lambda c: 1e9 - c[1] if e == "Y" and not deps0[c[1]] else prio[c[1]])
        if opens[i]:
            bank_tile[best[1]] = i
        fin[i] = finish(kind[i], st, cost[i], free)
        free[e] = st + ISSUE.get(kind[i], cost[i])
        order.append(i)
        ready.remove(i)
        for j in succ[i]:
            left[j] -= 1
            rt[j] = max(rt[j], fin[i] + LAT)
            if left[j] == 0:
                ready.append(j)
    assert len(order) == n
    return order, max(fin)


PLAN = {}
SHARE = (0.5, 0.15, 0.35)


def plan():
    if not PLAN:
        sets = [build(c) for c in COSTS]
        ops = sets[0]
        deps, reader = depend(ops)
        succ = [[] for _ in ops]
        for i, d in enumerate(deps):
            for j in d:
                succ[j].append(i)
        state = [OPT["seed"]]

        def rnd():
            state[0] = (state[0] * 1103515245 + 12345) % 2147483648
            return state[0] / 2147483648.0

        n = len(ops)
        form = [0] * n
        eng = [o["alt"][0][0] for o in ops]
        kind = [o["alt"][0][1] for o in ops]
        cost = [[o["alt"][0][3] for o in s] for s in sets]
        opens = [kind[i] == "mm" and ops[i]["tile"] is None for i in range(n)]
        starts = []
        for it in range(OPT["tries"]):
            jit = rnd() * 0.8
            weight = [c * (1 + jit * (rnd() - 0.5)) + 8000.0 * o.get("boost", 0.0) for c, o in zip(cost[0], ops)]
            starts.append(schedule(eng, kind, opens, cost[0], deps, reader, succ, weight, rnd() * 400.0)[::-1])
        starts.sort()
        dl = [sorted(d) for d in deps]
        hard = [[j for j in dl[i] if not (kind[i] == kind[j] == "mm")] for i in range(n)]
        above = [set() for _ in ops]
        for i in range(n):
            for j in dl[i]:
                above[i] |= above[j] | {j}
        lean = [[j for j in hard[i] if not any(j in above[x] for x in hard[i])] for i in range(n)]
        role = [-2 if opens[i] else -3 if kind[i] in ISSUE else -1 for i in range(n)]
        for i in reader:
            role[reader[i][1]] = i
        load = [0.0]
        pull = [(i, o["boost"]) for i, o in enumerate(ops) if o.get("boost")]

        def judge(seq, known=None, since=0):
            r = replay(eng, kind, cost[0], COSTS[0][4], seq, lean, role, known and known[2], since)
            if r is None:
                return None
            rest, total = [], r[0]
            if whole[0]:
                rest = [replay(eng, kind, cost[q], COSTS[q][4], seq, lean, role, known and known[3][q - 1], since, r[2])
                        for q in range(1, len(COSTS))]
                total = sum(w * s[0] for w, s in zip(SHARE, [r] + rest))
            total += sum(w * r[1][i] for i, w in pull)
            return (total + OPT["mean"] * sum(r[1]) / n + OPT["load"] * load[0], [s[0] for s in [r] + rest], r, rest)

        def move(seq, i, j):
            a, b = seq.index(j), seq.index(i)
            take = {i}
            for x in range(b, a - 1, -1):
                if seq[x] in take:
                    take.update(dl[seq[x]])
            if j in take:
                return None
            mid = seq[a:b + 1]
            return seq[:a] + [x for x in mid if x in take] + [x for x in mid if x not in take] + seq[b + 1:]

        def later(seq, j, i):
            a, b = seq.index(j), seq.index(i)
            take = {j}
            for x in range(a, b + 1):
                if seq[x] in take:
                    take.update(succ[seq[x]])
            if i in take:
                return None
            mid = seq[a:b + 1]
            return seq[:a] + [x for x in mid if x not in take] + [x for x in mid if x in take] + seq[b + 1:]

        def setform(i, f):
            load[0] -= cost[0][i] if eng[i] == "V" else 0.0
            form[i] = f
            eng[i], kind[i] = ops[i]["alt"][f][0], ops[i]["alt"][f][1]
            for q in range(len(COSTS)):
                cost[q][i] = sets[q][i]["alt"][f][3]
            load[0] += cost[0][i] if eng[i] == "V" else 0.0

        whole = [False]
        runs, short, long = OPT["runs"], OPT["short"], OPT["steps"]
        found = []
        for it in range(runs * short + long + 1):
            if it <= runs * short and (it % short == 0 if short else it == 0):
                if it:
                    found.append((best[0][0], best[1], best[2]))
                order, shape = (starts[it // short][1], [0] * n) if it < runs * short else min(found or [(0, starts[0][1], [0] * n)])[1:]
                for i in range(n):
                    setform(i, shape[i])
                cur, path = judge(order), None
                best = (cur, order, list(form))
            if it == runs * short + int(long * OPT["part"]):
                whole[0] = True
                del pull[:]
                cur = judge(order)
                best = (cur, order, list(form))
            heat = OPT["heat"] * (1 - it % short / short) if it < runs * short else OPT["warm"] * (1 - (it - runs * short) / long)
            if it % OPT["sort"] == 0:
                lines = {e: [x for x in order if eng[x] == e][::-1] for e in QUEUES}
                seq, done = [], set()
                while len(seq) < n:
                    x = min([w[-1] for w in lines.values() if w and done.issuperset(dl[w[-1]])],
                            key=lambda y: 0.0 if kind[y] == "send" else cur[2][1][y] - cost[0][y])
                    seq.append(lines[eng[x]].pop())
                    done.add(x)
                c = judge(seq)
                if c is not None and c[0] <= cur[0] + 100.0:
                    cur, order, path = c, seq, None
            if path is None:
                path = []
                i = cur[2][1].index(cur[2][0])
                while i >= 0:
                    path.append(i)
                    i = cur[2][4][i]
            x = int(rnd() * len(path))
            crit = rnd() < OPT["crit"]
            i = path[x] if crit else int(rnd() * n)
            old = form[i]
            seq = order
            if len(ops[i]["alt"]) > 1 and rnd() < OPT["flip"]:
                setform(i, (old + 1) % len(ops[i]["alt"]))
            elif crit and x + 1 < len(path) and eng[path[x + 1]] == eng[i] and path[x + 1] not in dl[i] and eng[i] != "Y":
                y = x + 1
                while y + 1 < len(path) and eng[path[y + 1]] == eng[i] and rnd() < 0.5:
                    y += 1
                seq = move(order, i, path[y]) if rnd() < 0.5 else later(order, path[y], i)
                if seq is None:
                    continue
            elif eng[i] == "X" or (eng[i] == "Y" and not dl[i]):
                continue
            else:
                line = [x for x in order if eng[x] == eng[i]]
                p = line.index(i)
                d = 1 + int(rnd() * rnd() * 6)
                if rnd() < 0.5:
                    seq = move(order, i, line[p - d]) if p >= d else None
                else:
                    seq = later(order, i, line[p + d]) if p + d < len(line) else None
                if seq is None or (eng[i] == "Y" and not dl[line[max(p - d, 0)]]):
                    continue
            since = order.index(i)
            if seq is not order:
                since = 0
                while since < n and seq[since] == order[since]:
                    since += MARK
                since = max(0, since - MARK)
                if seq[:since] != order[:since]:
                    since = 0
            c = judge(seq, cur, since)
            if c is not None and c[0] <= cur[0] + heat * rnd():
                cur, order, path = c, seq, None
                if c[0] < best[0][0]:
                    best = (c, seq, list(form))
            elif form[i] != old:
                setform(i, old)
        c, order, form = best
        PLAN["ops"] = ops
        waits = [lean[i] + [c[2][2][i]] if c[2][2][i] >= 0 else lean[i] for i in range(n)]
        PLAN["sched"] = (order, waits, [f - sets[0][i]["alt"][form[i]][3] for i, f in enumerate(c[2][1])], c[2][1], c[2][3])
        PLAN["score"] = c[1]
        PLAN["form"] = form
        PLAN["pred"] = c[2][4]
    return PLAN["ops"], PLAN["sched"], PLAN["form"]


def rank_program(g, core, T, topo):
    rank = T.rank_of(core)
    if rank is None:
        return
    n = len(T.cores)
    nxt, prv = T.cores[(rank + 1) % n], T.cores[(rank - 1) % n]
    rid, pid = topo.addr(nxt, core)
    ops, (order, deps, start, fin, banks), form = plan()
    Q = {"V": g.vector, "S": g.scalar, "PE": g.tensor, "G": g, "Y": g.sync}

    def ap(r):
        if not isinstance(r, tuple):
            return r
        if r[0] == "ind":
            return ap(r[1]).indirect(ap(r[2]))
        if r[0] == "ps":
            return T["ps%d" % banks[r[4]]][:, r[1]:r[2]]
        if len(r) == 3:
            return T[r[0]][:] if T[r[0]].shape[1] == r[2] - r[1] else T[r[0]][:, r[1]:r[2]]
        if len(r) == 5:
            return T[r[0]][0:1, r[1]:r[2]]
        if r[3] == 1:
            return T[r[0]][:, r[1]:r[2]]
        return T[r[0]][:, r[1]:r[2]:r[3]]

    needed = set(j for d in deps for j in d)
    token = {}
    knew = {}
    count = {"V": 0, "S": 0, "PE": 0, "G": 0}
    seen = {e: {} for e in Q}
    nd = [0]
    sent = [0]
    final = {}
    for i in order:
        e, kind, args, _ = ops[i]["alt"][form[i]]
        if kind == "recv":
            token[i] = ("r%d" % args[0], len(topo.engines(prv, core)))
            final[token[i][0]] = token[i][1]
            continue
        q = Q[e]
        want = {}
        for j in deps[i]:
            s, c = token[j]
            want[s] = max(want.get(s, 0), c)
        for s in sorted(want):
            if not any(knew.get((x, want[x]), {}).get(s, 0) >= want[s] for x in want if x != s):
                if seen[e].get(s, 0) < want[s]:
                    q.wait_ge(T.sem[s], want[s])
        for s in want:
            for x, c in list(knew.get((s, want[s]), {}).items()) + [(s, want[s])]:
                seen[e][x] = max(seen[e].get(x, 0), c)
        if kind == "send":
            g.remote_dma(ap(args[1]), ap(args[2]), T.sem["r%d" % args[0]], T.sem.sent, pid, rid, topo.mask(core, nxt))
            sent[0] += len(topo.engines(core, nxt))
            token[i] = ("sent", sent[0])
            final["sent"] = sent[0]
            continue
        if kind == "dma":
            s = "d%d" % nd[0]
            nd[0] += 1
            q.dma_start(ap(args[0]), ap(args[1])).then_inc(T.sem[s], 16)
            token[i] = (s, 16)
            final[s] = 16
            continue
        if kind == "ts":
            s1, s2, op0, op1 = args[2]
            if op1 is None:
                ins = q.tensor_scalar(ap(args[0]), ap(args[1][0]), ap(s1), None, op0)
            else:
                ins = q.tensor_scalar(ap(args[0]), ap(args[1][0]), ap(s1), ap(s2), op0, op1)
        elif kind == "tt":
            ins = q.tensor_tensor(ap(args[0]), ap(args[1][0]), ap(args[1][1]), args[2])
        elif kind == "cp":
            ins = q.tensor_copy(ap(args[0]), ap(args[1][0]))
        elif kind == "ms":
            ins = q.memset(ap(args[0]), args[1])
        elif kind == "act":
            ins = q.activation(ap(args[0]), ap(args[1]), args[2], bias=ap(args[3]), scale=ap(args[4]))
        elif kind == "iota":
            ins = g.iota(ap(args[0]), args[1], args[2], args[3],
                         allow_small_or_imprecise_dtypes=SCRATCH[args[0][0]][2] != I32)
        elif kind == "scan":
            ins = q.tensor_tensor_scan(ap(args[0]), ap(args[1][0]), ap(args[1][1]), *args[2])
        elif kind == "tri":
            w = args[0][2] - args[0][1]
            ins = g.affine_select(T[args[0][0]][args[2]:args[3], args[0][1]:args[0][2]], T[args[1][0]][args[2]:args[3], 0:w],
                                  [[0, w // 64], [-1, 64]], ALU.is_ge, 0.0, args[4], 1)
        elif kind == "half":
            ins = g.affine_select(ap(args[0]), ap(args[1]), [[-64 * args[2], 2], [0, 16]], ALU.is_ge, 0.0,
                                  0 if args[2] > 0 else 63, args[2])
        elif kind == "gcp":
            ins = g.affine_select(ap(args[0]), ap(args[1]), [[0, args[0][2] - args[0][1]]], ALU.is_ge, 0.0, 0, 0)
        elif kind == "pick":
            ins = g.affine_select(ap(args[0]), ap(args[1]), [[args[2], 128]], args[3], args[4], 0, -args[2])
        else:
            bank = T["ps%d" % banks[i if args[2] is None else args[2]]]
            for ti, t in enumerate(args[1]):
                c0 = t[2] if len(t) > 2 else 0
                p0 = t[3] if len(t) > 3 else 0
                w = len(range(t[1][1], t[1][2], t[1][3]))
                ins = q.matmul(bank[p0:p0 + t[0][2] - t[0][1], c0:c0 + w], ap(t[0]), ap(t[1]),
                               ti == 0 and args[2] is None, args[3] and ti == len(args[1]) - 1)
        if i in needed:
            count[e] += 1
            ins.then_inc(T.sem[e], 1)
            token[i] = (e, count[e])
            knew[token[i]] = dict(seen[e])
    final.update(count)
    for s in sorted(final):
        if final[s] and seen["Y"].get(s, 0) < final[s]:
            g.sync.wait_ge(T.sem[s], final[s])
